import numpy as np, ml_dtypes
CORES = [23,119,17,113]
N = 4
BF = ml_dtypes.bfloat16
def gentries(a):
    return np.ascontiguousarray(a.reshape(8, 16, -1).transpose(0, 2, 1)).reshape(8, -1)
def gtable(e):
    e = np.asarray(e); return np.ascontiguousarray(e.reshape(8, -1, 16).transpose(0, 2, 1)).reshape(128, -1).astype(np.int32)
G, C, P, RO, YC = 256, 16, 32, 2, 16
W, LG, LC, H, M = 4096, 8, 4, 128, 64
BIG = 2 ** 24
def probes(u, k):
    return (((u * u) >> 5)[..., None] + u[..., None] * k) & (W - 1)
def base(rng):
    ring = rng.integers(0, 256, (8, 8, 64, 16)); a = rng.integers(0, 8, (N, 8, G, 1)); b = rng.integers(0, 64, (N, 8, G, 1))
    X = ring[np.arange(8)[None, :, None, None], a, (b + np.arange(C)) & 63]
    X = np.clip(X + rng.integers(-4, 5, X.shape), 0, 255)
    th = np.where(rng.random((N, 8, P)) < 0.25, rng.integers(0, 300, (N, 8, P)), rng.integers(600, 1600, (N, 8, P)))
    return X, rng.integers(1, 256, (N, 8, 16)), rng.integers(0, 2048, (N, 8, RO, P)), th
def pack(X, wt, km, th):
    X = np.ascontiguousarray(X.reshape(N, 8, G, C, 16).transpose(0, 1, 4, 2, 3)).reshape(N, 128, W)
    return {"gen0": X.astype(np.float32).astype(BF), "wt": np.ascontiguousarray(wt.reshape(N, 128, 1)).astype(np.int32),
            "km": np.stack([gtable(a.reshape(8, -1)) for a in km]), "th": np.stack([gtable(a) for a in th])}
def setup_inputs(rng):
    return pack(*base(rng))
def column(rng, w, u):
    x = rng.integers(0, 256, 16); r = (int(u) - int(np.sum(w[2:] * x[2:]))) & (W - 1); x[0] = r & 15; x[1] = r >> 4
    return x
def link(rng, Y, w, k, o, alone=False):
    c = probes(np.arange(W)[None, :], k[None, None, :])[0]
    od = np.argsort(c.reshape(-1).astype(np.int16), kind="stable"); st = np.searchsorted(c.reshape(-1)[od], np.arange(W + 1))
    for i in range(G - 1):
        if alone and i == 1: continue
        j = 2 if alone and i == 0 else i + 1
        t = C * j + int(o[i]); us = od[st[t]:st[t + 1]] // P; us = us[~np.any(c[us] == C * i + C - 1, axis=1)]
        if len(us):
            x = column(rng, w, us[int(rng.integers(0, len(us)))]); Y[i, C - 1] = x; Y[j, int(o[i])] = x
def setup_inputs_deep(rng):
    X, wt, km, th = base(rng); th = rng.integers(30, 41, th.shape); B = 8 * N; b = np.arange(B)
    X = X.reshape(B, G, C, 16); w = wt.reshape(B, 1, 16).astype(np.int32); k0 = km[:, :, 0].reshape(B, 1, P).astype(np.int32); tries = min(128, max(16, 16 * G // P))
    for i in range(G - 1):
        x = rng.integers(0, 256, (B, tries, 16), dtype=np.int32); u = (np.sum(w * x, axis=2) & (W - 1)).astype(np.int32)
        c = probes(u, k0); o = c & (C - 1); to = np.where((b % 4 == 2) & (i == 0), 2, i + 1)
        hit = ((c >> LC) == to[:, None, None]) & (o != C - 1) & ~np.any(c == C * i + C - 1, axis=2)[..., None]
        like = np.where((b % 4 == 0)[:, None, None], o, np.where((b % 4 == 2)[:, None, None], C - 1 - o, 0)) + 1
        s = np.where(hit, like, 0).reshape(B, -1); a = np.argmax(s, axis=1)
        do = (s[b, a] > 0) & ((b % 2 == 0) | (rng.random(B) < 0.9)) & ((b % 4 != 2) | (i != 1))
        bb = b[do]; aa = a[do]; xs = x[bb, aa // P]
        X[bb, i, C - 1] = xs; X[bb, to[bb], o.reshape(B, -1)[bb, aa]] = xs
    X = X.reshape(N, 8, G, C, 16)
    for g in (3, 4, 7):
        wt[:, g, 0] = 1; wt[:, g, 1] = 16
    for r in range(N): link(rng, X[r, 4], wt[r, 4], km[r, 4, 0], np.full(G, C - 2))
    k = np.arange(2048)
    for g in (3, 7):
        h = int(rng.choice(np.array([3, 5, 7, 9]))); q0 = int(np.argmin((np.arange(C) * h + 1) & (C - 1))); Y = X[:, g].copy()
        for r in range(N):
            u = h - 1 + H * int(rng.integers(0, W // H)); c = (u * u // 32 + k * u) & (W - 1)
            km[r, g, 0] = rng.choice(k[(c & (C - 1)) != C - 1], P); Y[:, r * M:(r + 1) * M, q0] = column(rng, wt[r, g], u)
        for d in range(N): link(rng, Y[d], wt[d, g], km[d, g, 1], np.full(G, C - 2) if g == 3 else 2 * rng.integers(0, C // 2, G), g == 7)
        p = (C * np.arange(G)[:, None] + h * np.arange(C)) & (W - 1)
        for r in range(N):
            kid = np.zeros((G, C, 16), np.int64)
            for d in range(N): kid[(d - r) % N::N] = Y[d, r * M:(r + 1) * M]
            X[r, g, p >> LC, p & (C - 1)] = kid
    return pack(X, wt, km, th)
def setup_inputs_edges(rng):
    X, wt, km, th = base(rng)
    th[:, 0] = 0; e = X[:, 0, :1, C - 1].copy(); X[:, 0, ::2, C - 1] = e; X[:, 0, :, ::4] = e[:, :, None]
    f = rng.integers(0, 16, (N, G, C, 1)); X[:, 1] = (np.arange(16) == f) & (rng.random((N, G, C, 1)) < 0.2); X[:, 1, :, C - 1] = 255; th[:, 1] = 4080
    k = np.arange(2048)
    for q in range(N):
        u = int(255 * np.sum(wt[q, 1])) & (W - 1); c = ((u * u >> 5) + k * u) & (W - 1)
        good = k[(c & (C - 1)) != C - 1]
        km[q, 1, 0] = rng.choice(good if len(good) else k, P)
    km[:, 2] = rng.choice(np.array([0, 1, 3, 2047]), (N, RO, P))
    X[:, 3, ::2, C - 1] = 0; X[:, 3, 0, 0] = 0
    wt[:, 4] = 255; X[:, 4] = 255 - rng.integers(0, 3, (N, G, C, 16))
    X[:, 5, :, C - 1] = rng.integers(0, 256, (N, 1, 16))
    X[:, 6] = 255 * rng.integers(0, 2, (N, G, C, 16)); th[:, 6] = 255 * rng.integers(2, 9, (N, P))
    return pack(X, wt, km, th)
def setup_inputs_far(rng):
    X, wt, km, th = base(rng); k = np.arange(2048)
    for q in range(N):
        for g in (0, 1, 2, 4, 5):
            wt[q, g, 0] |= 1; wt[q, g, 8:] = wt[q, g, :8]
            b = np.concatenate([rng.integers(110, 181, (256, 8)), rng.integers(80, 101, (256, 8))], axis=1); u = np.sum(wt[q, g] * b, axis=1) & (W - 1)
            c = probes(u[None, :], k[None, None, :])[0]
            ok = (c == W - 1) if g == 4 else (c >= 3 * W // 4) & ((c & (C - 1)) != C - 1)
            if g == 5: ok = ok & np.any(c == 0, axis=1)[:, None]
            a, m = np.nonzero(ok); s = int(rng.integers(0, len(a))); x = b[a[s]]; c = c[a[s]]; K = int(m[s]); j = int(c[K]) >> LC; o = int(c[K]) & (C - 1)
            e = rng.integers(35, 71, (G, 8)); e[G // 4:G // 2] = rng.integers(0, 35, (G // 2 - G // 4, 8))
            if g > 2: e[:] = 0
            last = x + np.concatenate([e, -e], axis=1); X[q, g, :, C - 1] = last; km[q, g, 0] = K
            if g == 1:
                km[q, 1, 0] = rng.choice(k[(c & (C - 1)) != C - 1], P); th[q, 1] = rng.integers(2048, 4081, P)
                X[q, 1, :, :C - 1, :8] = rng.integers(0, 41, (G, C - 1, 8)); X[q, 1, :, :C - 1, 8:] = rng.integers(215, 256, (G, C - 1, 8))
            elif g == 4:
                d = rng.integers(1, 60, 16); X[q, 4, G - 1, C - 1] = x - d; th[q, 4] = int(np.sum(d)) + 1
            elif g == 5:
                d = rng.integers(1, 30, 16); X[q, 5, 0, 0] = x - d; X[q, 5, j, o] = x - rng.integers(30, 60, 16)
                km[q, 5, 0, ::2] = int(np.argmax(c == 0)); th[q, 5] = 4080; th[q, 5, ::2] = int(np.sum(d))
            else:
                v = np.repeat(np.array([0, 255]), 8); X[q, g, j, o] = v
                th[q, g] = 4080 if g == 0 else int(np.min(np.sum(np.abs(last - v), axis=1)))
    X[:, 3] = 255 - rng.integers(0, 64, (N, G, C, 16)); X[:, 3, :, C - 1] = rng.integers(0, 64, (N, G, 16)); th[:, 3] = rng.integers(2048, 4081, (N, P))
    return pack(X, wt, km, th)
def setup_inputs_spread(rng):
    X, wt, km, th = base(rng)
    X = np.minimum((rng.random((N, 8, G, C, 16)) * np.exp2(rng.integers(0, 9, (N, 8, G, C, 1)))).astype(np.int64), 255)
    wt = np.clip(np.exp2(8 * rng.random(wt.shape)).astype(np.int64), 1, 255); km = np.clip(np.exp2(11 * rng.random(km.shape)).astype(np.int64) - 1, 0, 2047); km[..., ::2] = rng.integers(0, 2048, km[..., ::2].shape)
    th = rng.integers(0, 4081, th.shape)
    return pack(X, wt, km, th)
def setup_inputs_ties(rng):
    X, wt, km, th = base(rng)
    pat = rng.integers(1, 254, (8, 4, 16)); a = rng.integers(0, 4, (N, 8, G, C))
    X = pat[np.arange(8)[None, :, None, None], a] + rng.integers(0, 2, (N, 8, G, C, 16)); th = rng.integers(3, 11, th.shape)
    return pack(X, wt, km, th)
def check_inputs(d):
    bad = []; v = np.asarray(d["gen0"]).astype(np.float32)
    if not np.all((v >= 0) & (v <= 255) & (v == np.floor(v))): bad.append("gen0 holds other numbers than 0 .. 255")
    for k, lo, hi in (("wt", 1, 255), ("km", 0, 2047), ("th", 0, 4080)):
        if np.min(d[k]) < lo or np.max(d[k]) > hi: bad.append("range of " + k)
    return bad
def reference(gen0, wt, km, th):
    B = 8 * N; X = gen0.astype(np.float32).astype(np.int32).reshape(B, 16, W); w = wt.astype(np.int64).reshape(B, 16, 1)
    kl = np.stack([gentries(a) for a in km]).astype(np.int64).reshape(B, RO, P); tl = np.stack([gentries(a) for a in th]).astype(np.int64).reshape(B, 1, P)
    ar = np.arange(G); q = np.arange(C); rows = np.arange(B)[:, None]
    for t in range(RO):
        x = X[:, :, C - 1::C]
        u = np.sum(w * x, axis=1) & (W - 1)
        c = probes(u, kl[:, t][:, None, :])
        pr = np.take_along_axis(X, c.reshape(B, 1, G * P), 2).reshape(B, 16, G, P)
        D = np.sum(np.abs(pr - x[..., None]), axis=1).astype(np.int64)
        best = np.min(np.where(D < tl, D * W + c, BIG), axis=2)
        j = (best & (W - 1)) >> LC; o = best & (C - 1); ok = (best < BIG) & (j > ar)
        acc = np.full((B, G), BIG, np.int64)
        np.minimum.at(acc, (rows, np.where(ok, j, 0)), np.where(ok, (best - (best & (W - 1))) + ar * C + o, BIG))
        got = acc < BIG; cut = np.where(got, 1 + ((acc & (C - 1)) >> 1), 0); ln = C - cut
        root = np.where(got, (acc & (W - 1)) >> LC, ar)
        for _ in range(LG): root = np.take_along_axis(root, root, 1)
        od = np.argsort(root * G + ar, axis=1)
        ls = np.take_along_axis(ln, od, 1); pos = np.zeros((B, G), np.int64)
        np.put_along_axis(pos, od, np.add.accumulate(ls, axis=1) - ls, 1); L = np.sum(ln, axis=1)
        place = np.where(q < cut[..., None], W, pos[..., None] + q - cut[..., None])
        src = np.zeros((B, W + 1), np.int64); np.put_along_axis(src, place.reshape(B, W), np.arange(W)[None, :], 1)
        p = ((ar * L[:, None]) >> LG)[..., None] + q * (1 + (u & (H - 1)))[..., None]
        p = np.where(p >= L[:, None, None], p - L[:, None, None], p)
        col = np.take_along_axis(src, p.reshape(B, W), 1)
        kid = np.take_along_axis(X, col[:, None, :], 2).reshape(N, 8, 16, G, C); nxt = np.empty_like(kid)
        for r in range(N):
            for d in range(N): nxt[d, :, :, r * M:(r + 1) * M] = kid[r, :, :, (d - r) % N::N]
        X = nxt.reshape(B, 16, W)
    return {"y": np.ascontiguousarray(X.reshape(N, 128, G, C)[..., :YC]).reshape(N, 128, G * YC).astype(np.float32).astype(BF)}

@@ -1,0 +1,429 @@
+import numpy as np
+from concourse.mybir import AluOpType as A, AxisListType, ActivationFunctionType as AF
+
+ROUNDS = 2
+SCRATCH = {}
+DTN = {"b": "bfloat16", "f": "float32", "i": "int32", "u": "uint16"}
+for _w in """X0 4096 b,X1 4096 b,X2 4096 b,XLD 4096 b,XR 4096 b,R8 256x8 b,DF 8192 b,AD 8192 b,wti 1 i,kmi 4 i,thi 2 i,wtf 1 f,kmf 4 f,T4 2 f,
+ipart 1 i,IC 160 f,GM 128 f,IK 256 f,IK8 256 f,PC 256 f,P16 256 f,CJ 256 f,BNbe 16 f,BNeb 16 f,PI 8 i,PF 8 f,PD 16 f,WH 128 b,Zd 144 b,
+ID 128 b,IDn 128 b,Zx0 144 b,Zx1 144 b,BS0 128 b,BS1 128 b,BS2 128 b,BSL 128 b,jn 8 i,CB 8x8 i,CTb 8x32 b,CTT 8x32 b,CL 8x128 b,CTR 16 f,iT 16 f,W256 16 f,
+U1 256 i,U 256 i,UU 256 i,UB 256 i,CA 2x256 i,CI 2x256 i,CU 2x256 u,HP 256 i,W0 256 f,pen 512 f,km0 256 f,km1 256 f,kt0 256 f,kt1 256 f,SC0 256 f,SC1 256 f,
+RSi 256 f,RS 256 f,best 16 i,Jt 16 i,nb 16 f,Jx 16 b,LJ 16 u,PX 272 b,FJ 256 b,NE 16 f,FI 16x32 i,FB 16x32 b,RT 512 b,ACC 16 f,AI 16 i,pt 16 i,zt 16 i,
+F2 16x16 b,RT2 256 b,R16 256 f,rw 16 f,NTW 16 f,SLf 16 f,SL 16 u,RL 16 u,Lc 1 f,L4 1 f,sk2 256 i,wp 256 f,pp 256 f,CC 256 u,G 256 f,Yn 256 f,Yc 256 f,
+rb 16 b,sti 256 i,TC 256 b,TC2 256 b,TS 256 i,Q 256 f,so 256 i,Qm 256 f,LU 16 u,ci 256 i,ca 256 i,LL 256 u,PW 13x256 b,YW 13x256 f,YB 4x256 f,LV 4x16 u,
+YT0 528 f,TT0 512 f,OT0 512 f,YT1 528 f,TT1 512 f,OT1 512 f,OB 6x1024 b,bk 16 i""".replace("\n", "").split(","):
+    _n, _s, _d = _w.split()
+    SCRATCH[_n] = ("sbuf", [128] + [int(z) for z in _s.split("x")], DTN[_d])
+for _b in range(8):
+    SCRATCH["ps%d" % _b] = ("psum", [128, 512], "float32")
+SEMAPHORES = (["cv", "cs", "ct", "cg", "dwt", "dkm", "dth"] + ["d%s%d" % (x, q) for x in "xy" for q in range(4)]
+              + ["%s%d_%d" % (x, t, k) for x in "al" for t in range(ROUNDS) for k in (1, 2, 3)])
+P24 = 16777216.0
+COPY, ABS = AF.Copy, AF.Abs
+SHR, AND = A.arith_shift_right, A.bitwise_and
+NUM = {n: np.arange(int(np.prod(s[1][1:]))).reshape(s[1][1:]) for n, s in SCRATCH.items()}
+
+
+def rank_program(g, core, T, topo):
+    rank = T.rank_of(core)
+    if rank is None:
+        return
+    v, s, te = g.vector, g.scalar, g.tensor
+
+    def a(n, *ix):
+        ix = tuple((slice(*z) if len(z) else slice(None)) if isinstance(z, tuple) else z for z in ix)
+        ap = T[n][(slice(None),) + ix]
+        if n not in NUM:
+            return ap, []
+        return ap, [(n, NUM[n][ix].reshape(-1) if n[:2] != "ps" else NUM[n])]
+
+    def ind(w, o):
+        return w[0].indirect(o[0]), w[1] + o[1]
+    eng = {"v": v, "s": s, "t": te, "g": g, "y": g.sync}
+    cnt, total, know, snap, ev = {}, {}, {e: {} for e in eng}, {}, []
+    wr = {n: np.full(NUM[n].size, -1) for n in NUM}
+    rd = {n: {} for n in NUM}
+
+    def need(e, reads, writes):
+        ids, own = set(), "c" + e
+        for w, lst in ((0, reads), (1, writes)):
+            for n, c in lst:
+                ids.update(np.unique(wr[n][c]).tolist())
+                if w or n[:2] == "ps":
+                    for sm, r in rd[n].items():
+                        if sm != own:
+                            ids.update(np.unique(r[c]).tolist())
+        nd, kn = {}, know[e]
+        for i in ids:
+            if i >= 0:
+                nd[ev[i][0]] = max(nd.get(ev[i][0], 0), ev[i][1])
+        for sm, val in sorted(nd.items(), key=lambda z: z[0] == own):
+            if kn.get(sm, 0) < val:
+                eng[e].wait_ge(T.sem[sm], val)
+                for s2, v2 in list(snap[(sm, val)].items()) + [(sm, val)]:
+                    kn[s2] = max(kn.get(s2, 0), v2)
+
+    def done(e, sm, val, reads, writes):
+        ev.append((sm, val))
+        snap[(sm, val)] = dict(know[e]) if e else {}
+        total[sm] = val
+        for n, c in reads:
+            rd[n].setdefault(sm, np.full(NUM[n].size, -1))[c] = len(ev) - 1
+        for n, c in writes:
+            wr[n][c] = len(ev) - 1
+            for r in rd[n].values():
+                r[c] = -1
+
+    def run(e, call, out, ins):
+        reads = [z for x in ins if isinstance(x, tuple) for z in x[1]]
+        need(e, reads, out[1])
+        sm = "c" + e
+        cnt[sm] = cnt.get(sm, 0) + 1
+        call().then_inc(T.sem[sm], 1)
+        done(e, sm, cnt[sm], reads, out[1])
+
+    def dma(e, out, in_, sm):
+        need(e, in_[1], out[1])
+        eng[e].dma_start(out[0], in_[0]).then_inc(T.sem[sm], 16)
+        done(e, sm, 16, in_[1], out[1])
+
+    def z(x):
+        return x[0] if isinstance(x, tuple) else x
+
+    def ts(out, x, s1, o0, s2=None, o1=None):
+        if o1 is None:
+            run("v", lambda: v.tensor_scalar(out[0], x[0], z(s1), None, o0), out, (x, s1))
+        else:
+            run("v", lambda: v.tensor_scalar(out[0], x[0], z(s1), z(s2), o0, o1), out, (x, s1, s2))
+
+    def tt(out, x, y, o):
+        run("v", lambda: v.tensor_tensor(out[0], x[0], y[0], o), out, (x, y))
+
+    def cp(out, x):
+        run("v", lambda: v.tensor_copy(out[0], x[0]), out, (x,))
+
+    def ac(out, x, f=COPY):
+        run("s", lambda: s.activation(out[0], x[0], f), out, (x,))
+
+    def lin(out, x, scale, bias, f=AF.Identity):
+        run("s", lambda: s.activation(out[0], x[0], f, bias=z(bias), scale=z(scale)), out, (x, bias, scale))
+
+    def tr(out, x):
+        run("v", lambda: v.transpose(out[0], x[0]), out, (x,))
+
+    def ms(out, c):
+        run("v", lambda: v.memset(out[0], c), out, ())
+
+    def red(out, x, o):
+        run("v", lambda: v.tensor_reduce(out[0], x[0], AxisListType.X, o), out, (x,))
+
+    def scan(out, x, y, o0, o1):
+        run("v", lambda: v.tensor_tensor_scan(out[0], x[0], y[0], 0.0, o0, o1), out, (x, y))
+
+    def iota(out, pat, base=0, cm=0):
+        run("g", lambda: g.iota(out[0], pat, base, cm, allow_small_or_imprecise_dtypes=True), out, ())
+
+    def mm(out, prs):
+        def call():
+            r = None
+            for n, (l, x) in enumerate(prs):
+                r = te.matmul(out[0], l[0], x[0], n == 0, n == len(prs) - 1)
+            return r
+        run("t", call, out, [x for p in prs for x in p])
+
+    def wrap(ps, f):
+        for x in range(2):
+            mm(a(ps, (x, 16, 2)), [(a("Zx%d" % x, (16 - 16 * e, 144 - 16 * e)), f(e)) for e in range(2)])
+
+    def tcol(n):
+        return lambda e: a(n, (16 * e, 256, 32))
+
+    def pf(n):
+        return a("PF", (n, n + 1))
+
+    def pd(n):
+        return a("PD", (n, n + 1))
+
+    order = [(rank + k) % 4 for k in range(4)]
+    for q in order:
+        dma("y", a("X0", (1024 * q, 1024 * q + 1024)), a("gen0", (1024 * q, 1024 * q + 1024)), "dx%d" % q)
+    dma("s", a("wti"), a("wt"), "dwt")
+    dma("s", a("kmi"), a("km"), "dkm")
+    dma("s", a("thi"), a("th"), "dth")
+    iota(a("ipart"), [[0, 1]], 0, 1)
+    iota(a("jn"), [[32, 8]], 0, 1)
+    iota(a("GM"), [[16, 8], [0, 16]])
+    iota(a("IC"), [[1, 160]])
+    for f, pt in ((5, [[0, 4], [1, 2]]), (6, [[0, 2], [1, 2], [0, 2]]), (7, [[1, 2], [0, 4]])):
+        iota(a("CB", (), f), pt)
+    for f, c in ((8, 4096), (9, 1048576), (10, 1), (20, 16)):
+        iota(a("CTb", (), f), [[0, 8]], c)
+    iota(a("CTb", (), (21, 32)), [[0, 88]])
+    iota(a("BNbe"), [[32, 8], [0, 2]])
+    iota(a("BNeb"), [[0, 2], [32, 8]])
+    iota(a("RSi"), [[0, 16], [1, 16]])
+    iota(a("FB"), [[0, 512]])
+    iota(a("P16"), [[16, 256]])
+    iota(a("F2"), [[0, 256]])
+    iota(a("PX", (256, 272)), [[0, 16]], 512)
+    iota(a("IK"), [[1, 4], [4, 64]])
+    iota(a("CJ"), [[16, 256]], 15)
+    for t in range(ROUNDS):
+        for n, w in (("YT", 528), ("TT", 512), ("OT", 512)):
+            iota(a(n + str(t)), [[0, w]])
+    ip = a("ipart")
+    for n, m in enumerate((15, 112, 31, 111)):
+        ts(a("PI", (n, n + 1)), ip, m, AND)
+    ts(a("PI", (4, 5)), ip, 4, SHR, 1, AND)
+    ts(a("PI", (5, 6)), ip, 5, SHR)
+    cp(pf(6), ip)
+    cp(a("PF", (0, 6)), a("PI", (0, 6)))
+    ts(pd(0), pf(1), 15.0, A.add)
+    cp(a("wtf"), a("wti"))
+    cp(a("kmf"), a("kmi"))
+    ts(a("T4"), a("thi"), 4096.0, A.mult)
+    ts(a("WH"), a("GM"), pf(1), A.is_equal, a("wtf"), A.mult)
+    ic = a("IC", (0, 144))
+    ts(a("Zd"), ic, pd(0), A.is_equal, 4096.0, A.mult)
+    ts(a("ID"), a("IC", (0, 128)), pf(6), A.is_equal)
+    ts(a("IDn"), a("IC", (0, 128)), pf(6), A.is_equal, -1.0, A.mult)
+    for f in range(5):
+        ts(a("CB", (), f), a("jn"), f, SHR, 1, AND)
+    for n in range(4):
+        ts(pd(8 + n), pf(5), float(n), A.is_equal)
+    ms(a("CTb", (), 11), P24)
+    ts(a("CTb", (), (0, 8)), a("CB"), -P24, A.mult, P24, A.add)
+    ts(a("CTb", (), (12, 20)), a("CB"), P24, A.mult)
+    tr(a("CTT"), a("CTb"))
+
+    def late():
+        lin(pd(3), pf(0), -1.0, 0.0)
+        lin(pd(4), pf(0), -1.0, 4095.0)
+        lin(a("RS"), a("RSi"), -2 * P24, 2 * P24, AF.Relu)
+        lin(a("iT"), a("BNeb"), 1.0, pf(2))
+        ac(a("FB", (), 20), a("iT"))
+        for n in range(4):
+            run("s", lambda: s.activation(T.CL[:, :, 32 * n:32 * n + 32], T.CTT[:], COPY, scale=pd(8 + n)[0]),
+                a("CL", (), (32 * n, 32 * n + 32)), (a("CTT"), pd(8 + n)))
+        lin(a("rw"), a("BNbe"), 1.0, pf(2))
+        lin(a("CTR"), a("rw"), 16.0, float(4080 * 4096 + 15))
+        lin(a("PC"), a("P16"), 1.0, pf(0))
+        lin(a("W256"), a("PC", (0, 16)), 1.0, 256.0)
+        lin(a("IK8"), a("IK"), 1.0 / 256, 0.0)
+        ts(pd(1), pf(3), 16.0, A.add)
+        ts(pd(2), pf(4), 0.0, A.is_equal)
+        for n in range(3):
+            ts(pd(5 + n), pf(0), float(n), A.is_equal, -1.0 if n == 2 else 1.0, A.mult)
+        ts(a("Zx0"), ic, pd(1), A.is_equal, pd(2), A.mult)
+        ts(a("Zx1"), ic, pd(1), A.is_equal, pf(4), A.mult)
+        for n in range(3):
+            ts(a("BS%d" % n), a("GM"), pf(1), A.is_equal, pd(5 + n), A.mult)
+        tt(a("BSL"), a("BS1"), a("BS2"), A.subtract)
+    lo, hi, wc = (0, 256), (256, 512), a("ps3", (0, 16))
+    own, rest = (64 * rank, 64 * rank + 64), [c for c in ((0, 64 * rank), (64 * rank + 64, 256)) if c[0] < c[1]]
+
+    for t in range(ROUNDS):
+        xn, nx = "X%d" % t, "X%d" % (t + 1)
+        win = a(xn, (0, 4096))
+
+        def last(i):
+            return a(xn, (16 * i[0] + 15, 16 * i[1], 16))
+
+        def second(i):
+            return (256 + i[0], 256 + i[1])
+        for ps, pcs in (("ps2", [own]), ("ps3", rest)):
+            for i in pcs:
+                mm(a(ps, i), [(a("WH"), last(i))])
+            for f in (lambda i: ac(a("R8", i, 0), last(i)),
+                      lambda i: ac(a("R8", i, 1), last(i)),
+                      lambda i: ac(a("R8", i, (2, 4)), a("R8", i, (0, 2))),
+                      lambda i: ac(a("R8", i, (4, 8)), a("R8", i, (0, 4))),
+                      lambda i: ac(a("XR", (16 * i[0], 16 * i[1], 2)), a("R8", i, ())),
+                      lambda i: cp(a("U1", i), a(ps, i)),
+                      lambda i: ts(a("U", i), a("U1", i), 4095, AND),
+                      lambda i: ts(a("ps6", i), a("U", i), a("kmf", (2 * t, 2 * t + 1)), A.mult),
+                      lambda i: tt(a("UU", i), a("U", i), a("U", i), A.mult),
+                      lambda i: ts(a("ps6", second(i)), a("U", i), a("kmf", (2 * t + 1, 2 * t + 2)), A.mult),
+                      lambda i: ts(a("UB", i), a("UU", i), 5, SHR),
+                      lambda i: tt(a("CA", 0, i), a("ps6", i), a("UB", i), A.add),
+                      lambda i: tt(a("CA", 1, i), a("ps6", second(i)), a("UB", i), A.add),
+                      lambda i: ts(a("CI", (), i), a("CA", (), i), 4095, AND),
+                      lambda i: cp(a("CU", (), i), a("CI", (), i)),
+                      lambda i: cp(a("XR", (16 * i[0] + 1, 16 * i[1], 2)), a("R8", i, ()))):
+                for i in pcs:
+                    f(i)
+
+        def chunk(h, g0, n, banks=()):
+            o = 256 * h + g0
+            d, x = (16 * o, 16 * (o + n)), (16 * g0, 16 * (g0 + n))
+            if not banks:
+                tt(a("DF", d), ind(win, a("CU", h, (g0, g0 + n))), a("XR", x), A.subtract)
+                ac(a("AD", d), a("DF", d), ABS)
+            else:
+                ac(a("DF", d), ind(win, a("CU", h, (g0, g0 + n))))
+                for j, b in enumerate(banks):
+                    dj, xj = (d[0] + 512 * j, d[0] + 512 * j + 512), (x[0] + 512 * j, x[0] + 512 * j + 512)
+                    mm(a(b, (0, 512)), [(a("ID"), a("DF", dj)), (a("IDn"), a("XR", xj))])
+
+            def end():
+                for j, b in enumerate(banks):
+                    ac(a("AD", (d[0] + 512 * j, d[0] + 512 * j + 512)), a(b, (0, 512)), ABS)
+                mm(a("ps%d" % h, (g0, g0 + n)), [(a("Zd", (15 - p, 143 - p)), a("AD", (d[0] + p, d[1], 16))) for p in range(16)])
+            return end
+        r0 = chunk(1, 64 * order[3], 64, ("ps6", "ps7"))
+        r1 = chunk(1, 64 * order[2] + 32, 32, ("ps4",))
+        for n, c in enumerate([(0, 64 * q, 64) for q in order] + [(1, 64 * q, 64) for q in order[:2]] + [(1, 64 * order[2], 32)]):
+            chunk(*c)()
+            if n == 2:
+                r0()
+            elif n == 4:
+                r1()
+        if t == 0:
+            late()
+        for k in range(4):
+            ts(a("HP", (64 * k, 64 * k + 64)), a("U", (k, 256, 4)), 127, AND)
+        for h, sl in enumerate((lo, hi)):
+            ts(a("pen", sl), a("ps%d" % h, lo), a("T4", (h, h + 1)), A.is_ge, P24, A.mult)
+            tt(a("ps%d" % (5 - h), lo), a("ps%d" % h, lo), a("CI", h, ()), A.add)
+            if h == 0:
+                ts(a("W0"), a("HP"), pd(3), A.mult, pd(4), A.add)
+            tt(a("km%d" % h), a("ps%d" % (5 - h), lo), a("pen", sl), A.max)
+            tr(a("kt%d" % h), a("km%d" % h))
+            scan(a("SC%d" % h), a("RS"), a("kt%d" % h), A.max, A.min)
+        for e in range(2):
+            c = (16 * e + 15, 256, 32)
+            tt(a("best", (8 * e, 8 * e + 8)), a("SC0", c), a("SC1", c), A.min)
+        be = a("best")
+        ts(a("Jt"), be, 4, SHR, 255, AND)
+        for f in range(8):
+            ts(a("FI", (), f), be, 4 + f, SHR, 1, AND)
+        ts(a("FI", (), 8), be, 12, SHR, 255, AND)
+        ts(a("FI", (), 9), be, 20, SHR, 31, AND)
+        ts(a("FI", (), 10), be, 1, SHR, 7, AND)
+        tt(a("FI", (), 11), a("Jt"), a("iT"), A.is_le)
+        ts(a("FB", (), (12, 20)), a("FI", (), (0, 8)), -1.0, A.mult, 1.0, A.add)
+        cp(a("FB", (), (0, 12)), a("FI", (), (0, 12)))
+        tr(a("RT"), a("FB"))
+        for b in range(8):
+            for e in range(2):
+                w = (256 * e, 256 * e + 32 * b + 32)
+                mm(a("ps%d" % b, w), [(a("CL", b, ()), a("RT", w))])
+        ts(a("nb"), a("FI", (), 11), 256.0, A.mult)
+        tt(a("Jx"), a("Jt"), a("nb"), A.max)
+        for b in range(8):
+            for e in range(2):
+                red(a("ACC", (2 * b + e, 2 * b + e + 1)), a("ps%d" % b, (256 * e, 256 * e + 32 * b + 32)), A.min)
+        tt(a("AI"), a("ACC"), a("CTR"), A.min)
+        ts(a("pt"), a("AI"), 4, SHR, 255, AND)
+        ts(a("zt"), a("AI"), 15, AND)
+        cp(a("F2", (), 0), a("pt"))
+        ts(a("F2", (), 2), a("AI"), float(4080 * 4096), A.is_ge, 16.0, A.mult)
+        ts(a("F2", (), 1), a("zt"), -1.0, A.mult, 15.0, A.add)
+        wrap("ps3", lambda e: a("F2", (e, 16, 2), 0))
+        tr(a("RT2"), a("F2"))
+        mm(a("ps4", lo), [(a("BS0"), a("RT2"))])
+        mm(a("ps5", lo), [(a("BS1"), a("RT2"))])
+        mm(a("ps7", lo), [(a("BSL"), a("RT2"))])
+        mm(a("ps6", lo), [(a("BS2"), a("RT2"))])
+        wrap("ps0", lambda e: a("Jx", (8 * e, 8 * e + 8)))
+        cp(a("LV", 0, ()), wc)
+        ac(a("PX", lo), a("ps4", lo))
+        cp(a("YW", 0, ()), a("ps5", lo))
+        cp(a("YB", 0, ()), a("ps5", lo))
+        n = 0
+        YT, TT, OT = ["%s%d" % (x, t) for x in ("YT", "TT", "OT")]
+        for lev in range(4):
+            L = a("LV", lev, ())
+            y0 = a("YB", lev, ())
+            if lev:
+                ac(y0, a("YW", n, ()))
+            for _ in range(3):
+                ac(a("PW", n + 1, ()), ind(a("PW", n, ()) if n else a("PX", lo), L))
+                tt(a("YW", n + 1, ()), ind(a("YW", n, ()), L), y0, A.add)
+                n += 1
+            if lev == 0:
+                cp(a("LJ"), a("ps0", (0, 16)))
+                ac(a("FJ"), ind(a("PX", (0, 272)), a("LJ")))
+                ac(a("R16"), a("ps6", lo))
+            tr(a("TC"), a("PW", n, ()))
+            wrap("ps3", tcol("TC"))
+            if lev == 0:
+                red(a("Lc"), a("ps7", lo), A.add)
+            elif lev == 1:
+                lin(a("L4"), a("Lc"), -1.0, 4095.0)
+                tr(a("TC2"), a("FJ"))
+                wrap("ps0", tcol("TC2"))
+                ts(a("sk2"), a("IK8"), a("Lc"), A.mult, 1.0 / 512 - 0.5, A.add)
+            elif lev == 2:
+                tt(a("NE"), a("ps0", (0, 16)), a("PC", (0, 16)), A.is_equal)
+                tt(a("wp"), a("W0"), a("sk2"), A.subtract)
+            else:
+                ts(a("ps6", lo), a("wp"), a("L4"), A.is_le, a("Lc"), A.mult)
+                tt(a("NTW"), a("NE"), a("W256"), A.mult)
+                tt(a("pp"), a("ps6", lo), a("wp"), A.add)
+            if lev < 3:
+                cp(a("LV", lev + 1, ()), wc)
+        yf = a("YW", 12, ())
+        lin(a("Yn"), yf, -1.0, 0.0)
+        tt(a("SLf"), wc, a("NTW"), A.max)
+        cp(a("RL"), wc)
+        cp(a("SL"), a("SLf"))
+        cp(ind(a(YT, (8, 520)), a("SL")), a("Yn"))
+        lin(a("Yc"), yf, -1.0, 4096.0)
+        scan(a("G"), a("R16"), a(YT, (7, 263)), A.add, A.add)
+        tt(a("sti"), ind(a("G", lo), a("RL")), a("Yc"), A.add)
+        tr(a("TS"), a("sti"))
+        ts(a("bk"), a("TS", (0, 256, 16)), 3, SHR)
+        ts(a("ps4", lo), a("sti"), 4097.0, A.mult)
+        ts(a("rb"), a("bk"), -256.0, A.add)
+        ts(a("so"), a("sti"), 15, AND)
+        wrap("ps3", lambda e: a("rb", (e, 16, 2)))
+        tt(a("Q"), a("ps4", lo), a("CJ"), A.add)
+        ts(a("ps5", lo), a("so"), pf(0), A.is_le)
+        ms(a("ps6", (0, 1)), 0.0)
+        ts(a("LU"), wc, 256.0, A.add)
+        tt(a("Qm"), a("ps5", lo), a("Q"), A.mult)
+        cp(ind(a(TT, (0, 512)), a("LU")), a("Q"))
+        cp(ind(a(OT, (0, 512)), a("LU")), a("Qm"))
+        scan(a("ps6", (1, 257)), a(TT, (0, 512, 2)), a(TT, (1, 512, 2)), A.max, A.max)
+        tt(a("ps7", lo), a("ps6", lo), a(OT, (0, 512, 2)), A.max)
+        tt(a("ps5", lo), a("ps7", lo), a(OT, (1, 512, 2)), A.max)
+        tt(a("ci"), a("ps5", lo), a("PC"), A.subtract)
+        ts(a("ca"), a("ci"), 4095, AND)
+        cp(a("LL"), a("ca"))
+        ac(a("XLD", (1952, 4096)), ind(win, a("LL", (122, 256))))
+        cp(a("XLD", (0, 1952)), ind(win, a("LL", (0, 122))))
+        cp(a("CC"), a("pp"))
+        mine = (1024 * rank, 1024 * rank + 1024)
+
+        def child(f, k, c0, c1):
+            out = a("OB", 3 * t + k - 1, (c0, c1)) if k else a(nx, (mine[0] + c0, mine[0] + c1))
+            f(out, ind(a("XLD", (0, 4096)), a("CC", (64 * k + c0 // 16, 64 * k + c1 // 16))))
+        for k in (1, 3):
+            child(cp, k, 0, 512)
+            child(ac, k, 512, 1024)
+        child(cp, 2, 0, 1024)
+        child(ac, 0, 0, 1024)
+
+        def engines(src, k):
+            to = T.cores[(T.rank_of(src) + k) % 4]
+            es = topo.engines(src, to)
+            if topo.chip(src) == topo.chip(to):
+                es = [x for x in es if x not in topo.engines(src, T.cores[(T.rank_of(src) + 1) % 4])]
+            return es
+        for k in (1, 3, 2):
+            rid, pid, _ = topo.addr(T.cores[(rank + k) % 4])
+            es = engines(core, k)
+            ob = a("OB", 3 * t + k - 1, ())
+            need("g", ob[1], [])
+            g.remote_dma(a(nx, mine)[0], ob[0], T.sem["a%d_%d" % (t, k)], T.sem["l%d_%d" % (t, k)], pid, rid, sum(1 << x for x in es))
+            total["l%d_%d" % (t, k)] = len(es)
+        for k in (1, 2, 3):
+            fr = (rank - k) % 4
+            done("", "a%d_%d" % (t, k), len(engines(T.cores[fr], k)), [], a(nx, (1024 * fr, 1024 * fr + 1024))[1])
+    for n, q in enumerate((rank, (rank + 2) % 4, (rank + 3) % 4, (rank + 1) % 4)):
+        c = (1024 * q, 1024 * q + 1024)
+        dma("ys"[n % 2], a("y", c), a("X2", c), "dy%d" % q)
+    for sm in sorted(total):
+        if know["g"].get(sm, 0) < total[sm]:
+            g.wait_ge(T.sem[sm], total[sm])

@@ -4,14 +4,15 @@ from concourse.mybir import AluOpType as A, AxisListType, ActivationFunctionType
 ROUNDS = 2
 SCRATCH = {}
 DTN = {"b": "bfloat16", "f": "float32", "i": "int32", "u": "uint16"}
-for _w in """X0 4096 b,X1 4096 b,X2 4096 b,XLD 4096 b,XR 4096 b,R8 256x8 b,DF 8192 b,AD 8192 b,wti 1 i,kmi 4 i,thi 2 i,wtf 1 f,kmf 4 f,T4 2 f,
-ipart 1 i,IC 160 f,GM 128 f,IK 256 f,IK8 256 f,PC 256 f,P16 256 f,CJ 256 f,BNbe 16 f,BNeb 16 f,PI 8 i,PF 8 f,PD 16 f,WH 128 b,Zd 144 b,
-ID 128 b,IDn 128 b,Zx0 144 b,Zx1 144 b,BS0 128 b,BS1 128 b,BS2 128 b,BSL 128 b,jn 8 i,CB 8x8 i,CTb 8x32 b,CTT 8x32 b,CL 8x128 b,CTR 16 f,iT 16 f,W256 16 f,
-U1 256 i,U 256 i,UU 256 i,UB 256 i,CA 2x256 i,CI 2x256 i,CU 2x256 u,HP 256 i,W0 256 f,pen 512 f,km0 256 f,km1 256 f,kt0 256 f,kt1 256 f,SC0 256 f,SC1 256 f,
-RSi 256 f,RS 256 f,best 16 i,Jt 16 i,nb 16 f,Jx 16 b,LJ 16 u,PX 272 b,FJ 256 b,NE 16 f,FI 16x32 i,FB 16x32 b,RT 512 b,ACC 16 f,AI 16 i,pt 16 i,zt 16 i,
-F2 16x16 b,RT2 256 b,R16 256 f,rw 16 f,NTW 16 f,SLf 16 f,SL 16 u,RL 16 u,Lc 1 f,L4 1 f,sk2 256 i,wp 256 f,pp 256 f,CC 256 u,G 256 f,Yn 256 f,Yc 256 f,
-rb 16 b,sti 256 i,TC 256 b,TC2 256 b,TS 256 i,Q 256 f,so 256 i,Qm 256 f,LU 16 u,ci 256 i,ca 256 i,LL 256 u,PW 13x256 b,YW 13x256 f,YB 4x256 f,LV 4x16 u,
-YT0 528 f,TT0 512 f,OT0 512 f,YT1 528 f,TT1 512 f,OT1 512 f,OB 6x1024 b,bk 16 i""".replace("\n", "").split(","):
+for _w in """X0 4096 b,X1 4096 b,X2 4096 b,XLD 4096 b,XR 4096 b,R8 256x8 b,R2 128 b,DF 8192 b,AD 8192 b,wti 1 i,kmi 4 i,thi 2 i,wtf 1 f,kmf 4 f,
+T4 2 f,BM 128 f,MQ 16 f,Zx 144 b,ipart 1 i,IC 160 f,GM 128 f,IK8 256 f,PC 256 f,CJ 256 f,BNbe 16 f,BNeb 16 f,PI 8 i,PF 8 f,PD 24 f,WH 128 b,Zd 144 b,
+ID 128 b,IDn 128 b,IDf 128 f,IDfn 128 f,Zx0 144 b,Zx1 144 b,BS0 128 b,BS1 128 b,BS2 128 b,BSL 128 b,jn 8 i,CB 8x8 i,CTb 8x32 b,CTT 8x32 b,CL 8x128 b,
+CTR 16 f,iT 16 f,iT1 16 f,iW 16 f,W256 16 f,WD 256 b,
+U1 256 i,U 256 i,UU 256 i,UB 256 i,CA 2x256 i,CI 2x256 i,CU 2x256 u,CF 2x256 f,HP 256 i,W0 256 f,pen 2x256 f,km0 256 f,km1 256 f,kt 256 f,SC 256 f,
+RSi 256 b,RS 256 f,best 16 i,Jt 16 i,Jx 16 b,LJ 16 u,PX 272 b,FJ 256 b,WJ 256 b,NE 16 f,FI 16x32 i,FB 16x32 b,RT 512 b,SH 8x256 f,SCN 16x128 f,
+AI 16 i,PZ 16x4 i,F2 16x16 b,RT2 256 b,R16 256 f,NTW 16 f,SLf 16 f,SL 16 u,RL 16 u,Lc 1 f,L4 1 f,Lh 1 f,y1 256 f,y2 256 f,
+sg 256 f,t2 256 f,CC 256 u,G 256 f,Yc 256 f,sti 256 f,WF 256 f,LI 16 i,Q 256 f,LU 16 u,ci 256 i,ca 256 i,LL 256 u,PW 9x256 b,YW 9x256 f,YB 8x256 f,WS 8x256 b,
+LV 8x16 u,YT0 528 f,TT0 512 f,YT1 528 f,TT1 512 f,OT 512 f,OB 6x1024 b""".replace("\n", "").split(","):
     _n, _s, _d = _w.split()
     SCRATCH[_n] = ("sbuf", [128] + [int(z) for z in _s.split("x")], DTN[_d])
 for _b in range(8):
@@ -19,9 +20,12 @@ for _b in range(8):
 SEMAPHORES = (["cv", "cs", "ct", "cg", "dwt", "dkm", "dth"] + ["d%s%d" % (x, q) for x in "xy" for q in range(4)]
               + ["%s%d_%d" % (x, t, k) for x in "al" for t in range(ROUNDS) for k in (1, 2, 3)])
 P24 = 16777216.0
+ROUNDER = 12582912.0
+HOLD = 8192.0
 COPY, ABS = AF.Copy, AF.Abs
 SHR, AND = A.arith_shift_right, A.bitwise_and
 NUM = {n: np.arange(int(np.prod(s[1][1:]))).reshape(s[1][1:]) for n, s in SCRATCH.items()}
+OPT = dict(split=122, first=32, last=32, hs=2)
 
 
 def rank_program(g, core, T, topo):
@@ -35,7 +39,7 @@ def rank_program(g, core, T, topo):
         ap = T[n][(slice(None),) + ix]
         if n not in NUM:
             return ap, []
-        return ap, [(n, NUM[n][ix].reshape(-1) if n[:2] != "ps" else NUM[n])]
+        return ap, [(n, NUM[n][ix].reshape(-1))]
 
     def ind(w, o):
         return w[0].indirect(o[0]), w[1] + o[1]
@@ -43,16 +47,19 @@ def rank_program(g, core, T, topo):
     cnt, total, know, snap, ev = {}, {}, {e: {} for e in eng}, {}, []
     wr = {n: np.full(NUM[n].size, -1) for n in NUM}
     rd = {n: {} for n in NUM}
+    bank = {n: {} for n in NUM if n[:2] == "ps"}
 
     def need(e, reads, writes):
         ids, own = set(), "c" + e
         for w, lst in ((0, reads), (1, writes)):
             for n, c in lst:
                 ids.update(np.unique(wr[n][c]).tolist())
-                if w or n[:2] == "ps":
+                if w:
                     for sm, r in rd[n].items():
                         if sm != own:
                             ids.update(np.unique(r[c]).tolist())
+                if n in bank:
+                    ids.update(i for sm, i in bank[n].items() if sm != own)
         nd, kn = {}, know[e]
         for i in ids:
             if i >= 0:
@@ -73,6 +80,9 @@ def rank_program(g, core, T, topo):
             wr[n][c] = len(ev) - 1
             for r in rd[n].values():
                 r[c] = -1
+        for n, c in reads + writes:
+            if n in bank:
+                bank[n][sm] = len(ev) - 1
 
     def run(e, call, out, ins):
         reads = [z for x in ins if isinstance(x, tuple) for z in x[1]]
@@ -117,8 +127,8 @@ def rank_program(g, core, T, topo):
     def red(out, x, o):
         run("v", lambda: v.tensor_reduce(out[0], x[0], AxisListType.X, o), out, (x,))
 
-    def scan(out, x, y, o0, o1):
-        run("v", lambda: v.tensor_tensor_scan(out[0], x[0], y[0], 0.0, o0, o1), out, (x, y))
+    def scan(out, x, y, o0, o1, init=0.0):
+        run("v", lambda: v.tensor_tensor_scan(out[0], x[0], y[0], init, o0, o1), out, (x, y))
 
     def iota(out, pat, base=0, cm=0):
         run("g", lambda: g.iota(out[0], pat, base, cm, allow_small_or_imprecise_dtypes=True), out, ())
@@ -126,17 +136,17 @@ def rank_program(g, core, T, topo):
     def mm(out, prs):
         def call():
             r = None
-            for n, (l, x) in enumerate(prs):
-                r = te.matmul(out[0], l[0], x[0], n == 0, n == len(prs) - 1)
+            for n, p in enumerate(prs):
+                r = te.matmul((p[2] if len(p) > 2 else out)[0], p[0][0], p[1][0], n == 0, n == len(prs) - 1)
             return r
-        run("t", call, out, [x for p in prs for x in p])
+        run("t", call, out, [x for p in prs for x in p[:2]])
 
     def wrap(ps, f):
         for x in range(2):
             mm(a(ps, (x, 16, 2)), [(a("Zx%d" % x, (16 - 16 * e, 144 - 16 * e)), f(e)) for e in range(2)])
 
-    def tcol(n):
-        return lambda e: a(n, (16 * e, 256, 32))
+    def hold(out, x):
+        scan(out, a("WD"), x, A.mult, A.max)
 
     def pf(n):
         return a("PF", (n, n + 1))
@@ -144,33 +154,33 @@ def rank_program(g, core, T, topo):
     def pd(n):
         return a("PD", (n, n + 1))
 
-    order = [(rank + k) % 4 for k in range(4)]
-    for q in order:
-        dma("y", a("X0", (1024 * q, 1024 * q + 1024)), a("gen0", (1024 * q, 1024 * q + 1024)), "dx%d" % q)
-    dma("s", a("wti"), a("wt"), "dwt")
+    order = [(rank - k) % 4 for k in (0, 2, 1, 3)]
+    dma("y", a("wti"), a("wt"), "dwt")
     dma("s", a("kmi"), a("km"), "dkm")
     dma("s", a("thi"), a("th"), "dth")
+    for q in order:
+        dma("y", a("X0", (1024 * q, 1024 * q + 1024)), a("gen0", (1024 * q, 1024 * q + 1024)), "dx%d" % q)
     iota(a("ipart"), [[0, 1]], 0, 1)
     iota(a("jn"), [[32, 8]], 0, 1)
     iota(a("GM"), [[16, 8], [0, 16]])
     iota(a("IC"), [[1, 160]])
     for f, pt in ((5, [[0, 4], [1, 2]]), (6, [[0, 2], [1, 2], [0, 2]]), (7, [[1, 2], [0, 4]])):
         iota(a("CB", (), f), pt)
-    for f, c in ((8, 4096), (9, 1048576), (10, 1), (20, 16)):
-        iota(a("CTb", (), f), [[0, 8]], c)
-    iota(a("CTb", (), (21, 32)), [[0, 88]])
-    iota(a("BNbe"), [[32, 8], [0, 2]])
-    iota(a("BNeb"), [[0, 2], [32, 8]])
     iota(a("RSi"), [[0, 16], [1, 16]])
-    iota(a("FB"), [[0, 512]])
-    iota(a("P16"), [[16, 256]])
-    iota(a("F2"), [[0, 256]])
+    iota(a("BNeb"), [[0, 2], [32, 8]])
+    iota(a("BNbe"), [[32, 8], [0, 2]])
+    iota(a("PC"), [[16, 256]])
+    iota(a("IK8"), [[1, 256]])
+    iota(a("F2"), [[0, 256]], 1)
     iota(a("PX", (256, 272)), [[0, 16]], 512)
-    iota(a("IK"), [[1, 4], [4, 64]])
     iota(a("CJ"), [[16, 256]], 15)
     for t in range(ROUNDS):
-        for n, w in (("YT", 528), ("TT", 512), ("OT", 512)):
+        for n, w in (("YT", 528), ("TT", 512)):
             iota(a(n + str(t)), [[0, w]])
+    ms(a("FB"), 0.0)
+    ms(a("CTb", (), (21, 32)), 0.0)
+    for f, c in ((8, 4096.0), (9, 1048576.0), (10, 1.0), (11, P24), (20, 16.0)):
+        ms(a("CTb", (), f), c)
     ip = a("ipart")
     for n, m in enumerate((15, 112, 31, 111)):
         ts(a("PI", (n, n + 1)), ip, m, AND)
@@ -178,49 +188,67 @@ def rank_program(g, core, T, topo):
     ts(a("PI", (5, 6)), ip, 5, SHR)
     cp(pf(6), ip)
     cp(a("PF", (0, 6)), a("PI", (0, 6)))
-    ts(pd(0), pf(1), 15.0, A.add)
-    cp(a("wtf"), a("wti"))
-    cp(a("kmf"), a("kmi"))
-    ts(a("T4"), a("thi"), 4096.0, A.mult)
-    ts(a("WH"), a("GM"), pf(1), A.is_equal, a("wtf"), A.mult)
     ic = a("IC", (0, 144))
-    ts(a("Zd"), ic, pd(0), A.is_equal, 4096.0, A.mult)
-    ts(a("ID"), a("IC", (0, 128)), pf(6), A.is_equal)
-    ts(a("IDn"), a("IC", (0, 128)), pf(6), A.is_equal, -1.0, A.mult)
+    lin(pd(0), pf(1), 1.0, 15.0)
+    lin(pd(1), pf(3), 1.0, 16.0)
+    lin(pd(2), pf(4), -1.0, 1.0)
+    lin(pd(3), pf(0), -1.0, 0.0)
+    lin(pd(4), pf(0), -1.0, 4095.0 + ROUNDER)
+    lin(pd(15), pf(0), 1.0, 1.0)
     for f in range(5):
         ts(a("CB", (), f), a("jn"), f, SHR, 1, AND)
-    for n in range(4):
-        ts(pd(8 + n), pf(5), float(n), A.is_equal)
-    ms(a("CTb", (), 11), P24)
+    ts(a("BM"), a("GM"), pf(1), A.is_equal)
+    ts(a("IDf"), a("IC", (0, 128)), pf(6), A.is_equal)
+    ts(a("MQ"), a("IC", (0, 16)), pf(0), A.is_equal)
+    ts(a("PD", (8, 12)), a("IC", (0, 4)), pf(5), A.is_equal)
+    ts(a("Zd"), ic, pd(0), A.is_equal, 4096.0, A.mult)
+    ts(a("Zx"), ic, pd(1), A.is_equal)
     ts(a("CTb", (), (0, 8)), a("CB"), -P24, A.mult, P24, A.add)
     ts(a("CTb", (), (12, 20)), a("CB"), P24, A.mult)
+    cp(a("wtf"), a("wti"))
+    cp(a("kmf"), a("kmi"))
+    ts(a("WH"), a("BM"), a("wtf"), A.mult)
     tr(a("CTT"), a("CTb"))
+    ts(a("FJ"), a("RSi"), pf(0), A.not_equal)
+    ts(a("WJ"), a("RSi"), pd(15), A.is_equal, HOLD, A.mult)
+    ts(a("T4"), a("thi"), 4096.0, A.mult)
+    tt(a("WD"), a("FJ"), a("WJ"), A.max)
+    ac(a("ID"), a("IDf"))
+    lin(a("IDn"), a("IDf"), -1.0, 0.0)
+    lin(a("RS"), a("RSi"), -2 * P24, 2 * P24, AF.Relu)
+    lin(a("iT"), a("BNeb"), 1.0, pf(2))
+
+    def mq(n):
+        return a("MQ", (n, n + 1))
 
     def late():
-        lin(pd(3), pf(0), -1.0, 0.0)
-        lin(pd(4), pf(0), -1.0, 4095.0)
-        lin(a("RS"), a("RSi"), -2 * P24, 2 * P24, AF.Relu)
-        lin(a("iT"), a("BNeb"), 1.0, pf(2))
         ac(a("FB", (), 20), a("iT"))
+        lin(a("iT1"), a("iT"), 1.0, 1.0)
         for n in range(4):
-            run("s", lambda: s.activation(T.CL[:, :, 32 * n:32 * n + 32], T.CTT[:], COPY, scale=pd(8 + n)[0]),
-                a("CL", (), (32 * n, 32 * n + 32)), (a("CTT"), pd(8 + n)))
-        lin(a("rw"), a("BNbe"), 1.0, pf(2))
-        lin(a("CTR"), a("rw"), 16.0, float(4080 * 4096 + 15))
-        lin(a("PC"), a("P16"), 1.0, pf(0))
-        lin(a("W256"), a("PC", (0, 16)), 1.0, 256.0)
-        lin(a("IK8"), a("IK"), 1.0 / 256, 0.0)
-        ts(pd(1), pf(3), 16.0, A.add)
-        ts(pd(2), pf(4), 0.0, A.is_equal)
-        for n in range(3):
-            ts(pd(5 + n), pf(0), float(n), A.is_equal, -1.0 if n == 2 else 1.0, A.mult)
-        ts(a("Zx0"), ic, pd(1), A.is_equal, pd(2), A.mult)
-        ts(a("Zx1"), ic, pd(1), A.is_equal, pf(4), A.mult)
-        for n in range(3):
-            ts(a("BS%d" % n), a("GM"), pf(1), A.is_equal, pd(5 + n), A.mult)
-        tt(a("BSL"), a("BS1"), a("BS2"), A.subtract)
-    lo, hi, wc = (0, 256), (256, 512), a("ps3", (0, 16))
-    own, rest = (64 * rank, 64 * rank + 64), [c for c in ((0, 64 * rank), (64 * rank + 64, 256)) if c[0] < c[1]]
+            lin(a("CL", (), (32 * n, 32 * n + 32)), a("CTT"), pd(8 + n), 0.0, COPY)
+        lin(a("BNbe"), a("BNbe"), 1.0, pf(2))
+        lin(pd(6), mq(1), -1.0, 0.0)
+        lin(pd(7), mq(2), -16.0, 0.0)
+        lin(pd(17), mq(3), 1.0, mq(0))
+        lin(pd(12), mq(15), 1.0 - 1.0 / HOLD, 1.0 / HOLD)
+        lin(pd(14), mq(15), 1.0 - HOLD, HOLD)
+        lin(pd(18), mq(3), 15.0, pd(6))
+        lin(a("CTR"), a("BNbe"), 16.0, float(4080 * 4096 + 15))
+        lin(a("Zx0"), a("Zx"), pd(2), 0.0, COPY)
+        lin(pd(19), mq(2), 16.0, pd(18))
+        lin(a("Zx1"), a("Zx"), pf(4), 0.0, COPY)
+        for n, c in (("0", 17), ("1", 18), ("2", 7), ("L", 19)):
+            lin(a("BS" + n), a("BM"), pd(c), 0.0, COPY)
+
+    def later():
+        lin(a("IK8"), a("IK8"), 1.0 / 256, 0.0)
+        lin(a("PC"), a("PC"), 1.0, pf(0))
+        lin(a("IDfn"), a("IDf"), -1.0, 0.0)
+        lin(pd(20), pd(14), 257.0, 0.0)
+        lin(pd(13), pd(12), 0.125, 0.0)
+        lin(a("iW"), a("PC", (0, 16)), pd(14), pd(14))
+        lin(a("W256"), a("PC", (0, 16)), pd(14), pd(20))
+    lo, col15 = (0, 256), (15, 256, 16)
 
     for t in range(ROUNDS):
         xn, nx = "X%d" % t, "X%d" % (t + 1)
@@ -229,171 +257,228 @@ def rank_program(g, core, T, topo):
         def last(i):
             return a(xn, (16 * i[0] + 15, 16 * i[1], 16))
 
-        def second(i):
-            return (256 + i[0], 256 + i[1])
-        for ps, pcs in (("ps2", [own]), ("ps3", rest)):
-            for i in pcs:
-                mm(a(ps, i), [(a("WH"), last(i))])
-            for f in (lambda i: ac(a("R8", i, 0), last(i)),
-                      lambda i: ac(a("R8", i, 1), last(i)),
-                      lambda i: ac(a("R8", i, (2, 4)), a("R8", i, (0, 2))),
-                      lambda i: ac(a("R8", i, (4, 8)), a("R8", i, (0, 4))),
-                      lambda i: ac(a("XR", (16 * i[0], 16 * i[1], 2)), a("R8", i, ())),
-                      lambda i: cp(a("U1", i), a(ps, i)),
-                      lambda i: ts(a("U", i), a("U1", i), 4095, AND),
-                      lambda i: ts(a("ps6", i), a("U", i), a("kmf", (2 * t, 2 * t + 1)), A.mult),
-                      lambda i: tt(a("UU", i), a("U", i), a("U", i), A.mult),
-                      lambda i: ts(a("ps6", second(i)), a("U", i), a("kmf", (2 * t + 1, 2 * t + 2)), A.mult),
-                      lambda i: ts(a("UB", i), a("UU", i), 5, SHR),
-                      lambda i: tt(a("CA", 0, i), a("ps6", i), a("UB", i), A.add),
-                      lambda i: tt(a("CA", 1, i), a("ps6", second(i)), a("UB", i), A.add),
-                      lambda i: ts(a("CI", (), i), a("CA", (), i), 4095, AND),
-                      lambda i: cp(a("CU", (), i), a("CI", (), i)),
-                      lambda i: cp(a("XR", (16 * i[0] + 1, 16 * i[1], 2)), a("R8", i, ()))):
-                for i in pcs:
-                    f(i)
+        def quarter(n):
+            return (64 * order[n], 64 * order[n] + 64)
 
-        def chunk(h, g0, n, banks=()):
-            o = 256 * h + g0
-            d, x = (16 * o, 16 * (o + n)), (16 * g0, 16 * (g0 + n))
-            if not banks:
-                tt(a("DF", d), ind(win, a("CU", h, (g0, g0 + n))), a("XR", x), A.subtract)
-                ac(a("AD", d), a("DF", d), ABS)
-            else:
-                ac(a("DF", d), ind(win, a("CU", h, (g0, g0 + n))))
-                for j, b in enumerate(banks):
-                    dj, xj = (d[0] + 512 * j, d[0] + 512 * j + 512), (x[0] + 512 * j, x[0] + 512 * j + 512)
-                    mm(a(b, (0, 512)), [(a("ID"), a("DF", dj)), (a("IDn"), a("XR", xj))])
+        def hashes(i):
+            j = (256 + i[0], 256 + i[1])
+            mm(a("ps7", i), [(a("WH"), last(i))])
+            return [lambda: cp(a("U1", i), a("ps7", i)),
+                    lambda: ts(a("U", i), a("U1", i), 4095, AND),
+                    lambda: ts(a("ps6", i), a("U", i), a("kmf", (2 * t, 2 * t + 1)), A.mult),
+                    lambda: tt(a("UU", i), a("U", i), a("U", i), A.mult),
+                    lambda: ts(a("ps6", j), a("U", i), a("kmf", (2 * t + 1, 2 * t + 2)), A.mult),
+                    lambda: ts(a("UB", i), a("UU", i), 5, SHR),
+                    lambda: ts(a("HP", i), a("U", i), 127, AND),
+                    lambda: tt(a("CA", 0, i), a("ps6", i), a("UB", i), A.add),
+                    lambda: tt(a("CA", 1, i), a("ps6", j), a("UB", i), A.add),
+                    lambda: ts(a("W0", i), a("HP", i), pd(3), A.mult, pd(4), A.add),
+                    lambda: ts(a("CI", (), i), a("CA", (), i), 4095, AND),
+                    lambda: cp(a("CU", (), i), a("CI", (), i)),
+                    lambda: cp(a("CF", (), i), a("CI", (), i))]
+        for n in range(3):
+            i = quarter(n)
+            hs = hashes(i)
+            ac(a("R8", i, 0), last(i))
+            ac(a("R8", i, 1), last(i))
+            ac(a("R8", i, (2, 4)), a("R8", i, (0, 2)))
+            ac(a("R8", i, (4, 8)), a("R8", i, (0, 4)))
+            ac(a("XR", (16 * i[0], 16 * i[1], 2)), a("R8", i, ()))
+            for f in hs:
+                f()
+            cp(a("XR", (16 * i[0] + 1, 16 * i[1], 2)), a("R8", i, ()))
 
-            def end():
-                for j, b in enumerate(banks):
-                    ac(a("AD", (d[0] + 512 * j, d[0] + 512 * j + 512)), a(b, (0, 512)), ABS)
-                mm(a("ps%d" % h, (g0, g0 + n)), [(a("Zd", (15 - p, 143 - p)), a("AD", (d[0] + p, d[1], 16))) for p in range(16)])
-            return end
-        r0 = chunk(1, 64 * order[3], 64, ("ps6", "ps7"))
-        r1 = chunk(1, 64 * order[2] + 32, 32, ("ps4",))
-        for n, c in enumerate([(0, 64 * q, 64) for q in order] + [(1, 64 * q, 64) for q in order[:2]] + [(1, 64 * order[2], 32)]):
-            chunk(*c)()
-            if n == 2:
-                r0()
-            elif n == 4:
-                r1()
+        def span(h, i):
+            return (4096 * h + 16 * i[0], 4096 * h + 16 * i[1])
+
+        def keys(n, h):
+            return a("ps4", (0, 64)) if (n, h) == (2, 1) else a("ps%d" % n, (64 * h, 64 * h + 64))
+
+        def sums(n, h):
+            i = quarter(n)
+            d = span(h, i)
+            mm(keys(n, h), [(a("IDf"), a("CF", h, i))] + [(a("Zd", (15 - p, 143 - p)), a("AD", (d[0] + p, d[1], 16))) for p in range(16)])
+
+        def less(h, i):
+            tt(a("DF", span(h, i)), ind(win, a("CU", h, i)), a("XR", (16 * i[0], 16 * i[1])), A.subtract)
+
+        def absolute(h, i):
+            ac(a("AD", span(h, i)), a("DF", span(h, i)), ABS)
+
+        def plain(f, n, h, banks):
+            i = quarter(n)
+            d = span(h, i)[0]
+            f(a("DF", span(h, i)), ind(win, a("CU", h, i)))
+            for j, b in enumerate(banks):
+                x0 = 16 * i[0] + 512 * j
+                mm(a(b), [(a("ID"), a("DF", (d + 512 * j, d + 512 * j + 512)))]
+                   + ([(a("IDn"), a("R2", (64 * j, 64 * j + 64)), a(b, (x, 512, 8))) for x in range(8)] if n == 3
+                      else [(a("IDn"), a("XR", (x0, x0 + 512)))]))
+
+        def plain_end(n, h, banks):
+            d = span(h, quarter(n))[0]
+            for j, b in enumerate(banks):
+                ac(a("AD", (d + 512 * j, d + 512 * j + 512)), a(b), ABS)
+            sums(n, h)
+
+        def bests(n):
+            i = quarter(n)
+            return [lambda: ts(a("pen", 0, i), keys(n, 0), a("T4", (0, 1)), A.is_ge, 2 * P24, A.mult),
+                    lambda: tt(a("km0", i), keys(n, 0), a("pen", 0, i), A.max),
+                    lambda: ts(a("pen", 1, i), keys(n, 1), a("T4", (1, 2)), A.is_ge, 2 * P24, A.mult),
+                    lambda: tt(a("ps6", i), keys(n, 1), a("pen", 1, i), A.max),
+                    lambda: tt(a("km1", i), a("ps6", i), a("km0", i), A.min),
+                    lambda: tr(a("kt", i), a("km1", i)),
+                    lambda: scan(a("SC", i), a("RS", i), a("kt", i), A.max, A.min)]
+        q0, q1, q2 = quarter(0), quarter(1), quarter(2)
+        f0, l0 = q0[0] + OPT["first"], q2[1] - OPT["last"]
+        hs = hashes(quarter(3))
+        for x in range(2):
+            ac(a("R2", (x, 128, 2)), last(quarter(3)))
+        plain(ac, 0, 0, ("ps4", "ps5"))
+        less(1, (q0[0], f0))
+        for f in hs[:OPT["hs"]]:
+            f()
+        less(1, (f0, q0[1]))
+        for f in hs[OPT["hs"]:]:
+            f()
+        absolute(1, (q0[0], f0))
+        plain_end(0, 0, ("ps4", "ps5"))
+        absolute(1, (f0, q0[1]))
+        sums(0, 1)
+        plain(cp, 3, 1, ("ps7", "ps2"))
+        plain(ac, 3, 0, ("ps4", "ps5"))
+        less(0, q1)
+        plain_end(3, 1, ("ps7", "ps2"))
+        plain_end(3, 0, ("ps4", "ps5"))
+        absolute(0, q1)
+        sums(1, 0)
+        for n, h in ((1, 1), (2, 0)):
+            less(h, quarter(n))
+            absolute(h, quarter(n))
+            sums(n, h)
+        for i in ((q2[0], l0), (l0, q2[1])):
+            less(1, i)
+            absolute(1, i)
+        sums(2, 1)
         if t == 0:
             late()
-        for k in range(4):
-            ts(a("HP", (64 * k, 64 * k + 64)), a("U", (k, 256, 4)), 127, AND)
-        for h, sl in enumerate((lo, hi)):
-            ts(a("pen", sl), a("ps%d" % h, lo), a("T4", (h, h + 1)), A.is_ge, P24, A.mult)
-            tt(a("ps%d" % (5 - h), lo), a("ps%d" % h, lo), a("CI", h, ()), A.add)
-            if h == 0:
-                ts(a("W0"), a("HP"), pd(3), A.mult, pd(4), A.add)
-            tt(a("km%d" % h), a("ps%d" % (5 - h), lo), a("pen", sl), A.max)
-            tr(a("kt%d" % h), a("km%d" % h))
-            scan(a("SC%d" % h), a("RS"), a("kt%d" % h), A.max, A.min)
+        for fs in zip(bests(0), bests(3), bests(1)):
+            for f in fs:
+                f()
+        for f in bests(2):
+            f()
         for e in range(2):
-            c = (16 * e + 15, 256, 32)
-            tt(a("best", (8 * e, 8 * e + 8)), a("SC0", c), a("SC1", c), A.min)
+            cp(a("best", (8 * e, 8 * e + 8)), a("SC", (16 * e + 15, 256, 32)))
         be = a("best")
         ts(a("Jt"), be, 4, SHR, 255, AND)
         for f in range(8):
             ts(a("FI", (), f), be, 4 + f, SHR, 1, AND)
+        tt(a("FI", (), 11), a("Jt"), a("iT"), A.is_le)
         ts(a("FI", (), 8), be, 12, SHR, 255, AND)
         ts(a("FI", (), 9), be, 20, SHR, 31, AND)
         ts(a("FI", (), 10), be, 1, SHR, 7, AND)
-        tt(a("FI", (), 11), a("Jt"), a("iT"), A.is_le)
         ts(a("FB", (), (12, 20)), a("FI", (), (0, 8)), -1.0, A.mult, 1.0, A.add)
         cp(a("FB", (), (0, 12)), a("FI", (), (0, 12)))
+        tt(a("Jx"), a("Jt"), a("iT1"), A.max)
         tr(a("RT"), a("FB"))
-        for b in range(8):
+        for b in (0, 7, 1, 6, 2, 5, 3, 4):
+            w = 32 * b + 32
             for e in range(2):
-                w = (256 * e, 256 * e + 32 * b + 32)
-                mm(a("ps%d" % b, w), [(a("CL", b, ()), a("RT", w))])
-        ts(a("nb"), a("FI", (), 11), 256.0, A.mult)
-        tt(a("Jx"), a("Jt"), a("nb"), A.max)
-        for b in range(8):
+                mm(a("ps%d" % b, (w * e, w * e + w)), [(a("CL", b, ()), a("RT", (256 * e, 256 * e + w)))])
+            if b > 3:
+                ac(a("SH", b, (0, w)), a("ps%d" % b, (1, 2 * w, 2)))
+        if t == 0:
+            later()
+        for b in (0, 1, 7, 2, 6, 3, 5, 4):
+            w = 32 * b + 32
             for e in range(2):
-                red(a("ACC", (2 * b + e, 2 * b + e + 1)), a("ps%d" % b, (256 * e, 256 * e + 32 * b + 32)), A.min)
-        tt(a("AI"), a("ACC"), a("CTR"), A.min)
-        ts(a("pt"), a("AI"), 4, SHR, 255, AND)
-        ts(a("zt"), a("AI"), 15, AND)
-        cp(a("F2", (), 0), a("pt"))
-        ts(a("F2", (), 2), a("AI"), float(4080 * 4096), A.is_ge, 16.0, A.mult)
-        ts(a("F2", (), 1), a("zt"), -1.0, A.mult, 15.0, A.add)
+                if b > 3:
+                    scan(a("SCN", 2 * b + e, (128 - w // 2, 128)), a("ps%d" % b, (w * e, w * e + w, 2)),
+                         a("SH", b, (w // 2 * e, w // 2 * (e + 1))), A.min, A.min, 2 * P24)
+                else:
+                    red(a("SCN", 2 * b + e, (127, 128)), a("ps%d" % b, (w * e, w * e + w)), A.min)
+        wrap("ps0", lambda e: a("Jx", (8 * e, 8 * e + 8)))
+        tt(a("AI"), a("SCN", (), 127), a("CTR"), A.min)
+        ts(a("PZ", (), 0), a("AI"), 4, SHR, 255, AND)
+        ts(a("PZ", (), 1), a("AI"), 15, AND)
+        ts(a("PZ", (), 2), a("AI"), 3, SHR, 1, AND)
+        cp(a("LJ"), a("ps0", (0, 16)))
+        cp(a("F2", (), (0, 3)), a("PZ", (), (0, 3)))
         wrap("ps3", lambda e: a("F2", (e, 16, 2), 0))
         tr(a("RT2"), a("F2"))
-        mm(a("ps4", lo), [(a("BS0"), a("RT2"))])
-        mm(a("ps5", lo), [(a("BS1"), a("RT2"))])
-        mm(a("ps7", lo), [(a("BSL"), a("RT2"))])
-        mm(a("ps6", lo), [(a("BS2"), a("RT2"))])
-        wrap("ps0", lambda e: a("Jx", (8 * e, 8 * e + 8)))
-        cp(a("LV", 0, ()), wc)
+        for n, b in (("0", 4), ("1", 5), ("L", 7), ("2", 6)):
+            mm(a("ps%d" % b, lo), [(a("BS" + n), a("RT2"))])
+        cp(a("LV", 0, ()), a("ps3", (0, 16)))
         ac(a("PX", lo), a("ps4", lo))
         cp(a("YW", 0, ()), a("ps5", lo))
         cp(a("YB", 0, ()), a("ps5", lo))
-        n = 0
-        YT, TT, OT = ["%s%d" % (x, t) for x in ("YT", "TT", "OT")]
-        for lev in range(4):
-            L = a("LV", lev, ())
-            y0 = a("YB", lev, ())
-            if lev:
-                ac(y0, a("YW", n, ()))
-            for _ in range(3):
-                ac(a("PW", n + 1, ()), ind(a("PW", n, ()) if n else a("PX", lo), L))
-                tt(a("YW", n + 1, ()), ind(a("YW", n, ()), L), y0, A.add)
-                n += 1
-            if lev == 0:
-                cp(a("LJ"), a("ps0", (0, 16)))
-                ac(a("FJ"), ind(a("PX", (0, 272)), a("LJ")))
-                ac(a("R16"), a("ps6", lo))
-            tr(a("TC"), a("PW", n, ()))
-            wrap("ps3", tcol("TC"))
-            if lev == 0:
-                red(a("Lc"), a("ps7", lo), A.add)
-            elif lev == 1:
-                lin(a("L4"), a("Lc"), -1.0, 4095.0)
-                tr(a("TC2"), a("FJ"))
-                wrap("ps0", tcol("TC2"))
-                ts(a("sk2"), a("IK8"), a("Lc"), A.mult, 1.0 / 512 - 0.5, A.add)
-            elif lev == 2:
-                tt(a("NE"), a("ps0", (0, 16)), a("PC", (0, 16)), A.is_equal)
-                tt(a("wp"), a("W0"), a("sk2"), A.subtract)
+
+        def beside(n):
+            if n < 4:
+                ac(a("FJ", (64 * n, 64 * n + 64)), ind(a("PX", (0, 272)), a("LJ", (4 * n, 4 * n + 4))))
+            elif n == 4:
+                hold(a("WJ"), a("FJ"))
+            elif n == 5:
+                tt(a("NE"), a("WJ", col15), a("iW"), A.is_equal)
             else:
-                ts(a("ps6", lo), a("wp"), a("L4"), A.is_le, a("Lc"), A.mult)
                 tt(a("NTW"), a("NE"), a("W256"), A.mult)
-                tt(a("pp"), a("ps6", lo), a("wp"), A.add)
-            if lev < 3:
-                cp(a("LV", lev + 1, ()), wc)
-        yf = a("YW", 12, ())
-        lin(a("Yn"), yf, -1.0, 0.0)
-        tt(a("SLf"), wc, a("NTW"), A.max)
-        cp(a("RL"), wc)
-        cp(a("SL"), a("SLf"))
-        cp(ind(a(YT, (8, 520)), a("SL")), a("Yn"))
-        lin(a("Yc"), yf, -1.0, 4096.0)
-        scan(a("G"), a("R16"), a(YT, (7, 263)), A.add, A.add)
-        tt(a("sti"), ind(a("G", lo), a("RL")), a("Yc"), A.add)
-        tr(a("TS"), a("sti"))
-        ts(a("bk"), a("TS", (0, 256, 16)), 3, SHR)
-        ts(a("ps4", lo), a("sti"), 4097.0, A.mult)
-        ts(a("rb"), a("bk"), -256.0, A.add)
-        ts(a("so"), a("sti"), 15, AND)
-        wrap("ps3", lambda e: a("rb", (e, 16, 2)))
-        tt(a("Q"), a("ps4", lo), a("CJ"), A.add)
-        ts(a("ps5", lo), a("so"), pf(0), A.is_le)
+        for n in range(8):
+            L = a("LV", n, ())
+            ac(a("PW", n + 1, ()), ind(a("PW", n, ()) if n else a("PX", lo), L))
+            tt(a("YW", n + 1, ()), ind(a("YW", n, ()), L), a("YB", n, ()), A.add)
+            hold(a("WS", n, ()), a("PW", n + 1, ()))
+            if n < 7:
+                ac(a("YB", n + 1, ()), a("YW", n + 1, ()))
+                beside(n)
+                ts(a("LV", n + 1, ()), a("WS", n, col15), pd(12), A.mult, -1.0, A.add)
+        YT, TT = ["%s%d" % (x, t) for x in ("YT", "TT")]
+        yf = a("YW", 8, ())
+        ac(a("R16"), a("ps6", lo))
+        lin(a("Yc"), yf, -1.0, 4097.0)
+        run("s", lambda: s.activation(T.sg[:], T.ps7[:, 0:256], COPY, accum_out=T.Lc[:]),
+            (None, a("sg")[1] + a("Lc")[1]), (a("ps7", lo),))
+        for x in range(2):
+            lin(a("ps4", (x, 512, 2)), a("PC"), 4097.0, 4096.0)
+        lin(a("y1"), a("IK8"), a("Lc"), 1.0 / 512 - 0.5)
+        lin(a("L4"), a("Lc"), -1.0, 4095.5)
+        lin(a("y2"), a("y1"), 1.0, ROUNDER)
+        lin(a("Lh"), a("Lc"), 0.5, 0.0)
+        mm(a("ps1", lo), [(a("IDf"), a("W0")), (a("IDfn"), a("y2"))])
+        tt(a("SLf"), a("WS", 7, col15), a("NTW"), A.max)
+        ts(a("RL"), a("WS", 7, col15), pd(12), A.mult, -1.0, A.add)
+        ts(a("SL"), a("SLf"), pd(12), A.mult, -1.0, A.add)
+        cp(ind(a(YT, (8, 520)), a("SL")), yf)
+        scan(a("G"), a("R16"), a(YT, (7, 263)), A.add, A.subtract)
         ms(a("ps6", (0, 1)), 0.0)
-        ts(a("LU"), wc, 256.0, A.add)
-        tt(a("Qm"), a("ps5", lo), a("Q"), A.mult)
-        cp(ind(a(TT, (0, 512)), a("LU")), a("Q"))
-        cp(ind(a(OT, (0, 512)), a("LU")), a("Qm"))
+        tt(a("sti"), ind(a("G", lo), a("RL")), a("Yc"), A.add)
+        lin(a("Q"), a("sti"), 4097.0, -4097.0)
+        lin(a("sg"), a("ps1", lo), -1.0, a("L4"), AF.Sign)
+        lin(a("t2"), a("sg"), a("Lh"), a("Lh"))
+        mm(a("ps2", lo), [(a("IDf"), a("W0")), (a("IDfn"), a("y2")), (a("IDf"), a("t2"))])
+        hold(a("WF"), a("sti"))
+        ts(a("LI"), a("WF", col15), pd(13), A.mult, -0.5625, A.add)
+        cp(a("LU"), a("LI"))
+        tt(ind(a(TT, (0, 512)), a("LU")), a("Q"), a("CJ"), A.add)
+        parts = ((OPT["split"], 256), (0, OPT["split"]))
+
+        def twice(c, x=None):
+            return (2 * c[0], 2 * c[1]) if x is None else (2 * c[0] + x, 2 * c[1], 2)
+        for c in parts:
+            tt(a("ps5", twice(c)), a(TT, twice(c)), a("ps4", twice(c)), A.is_le)
         scan(a("ps6", (1, 257)), a(TT, (0, 512, 2)), a(TT, (1, 512, 2)), A.max, A.max)
-        tt(a("ps7", lo), a("ps6", lo), a(OT, (0, 512, 2)), A.max)
-        tt(a("ps5", lo), a("ps7", lo), a(OT, (1, 512, 2)), A.max)
-        tt(a("ci"), a("ps5", lo), a("PC"), A.subtract)
-        ts(a("ca"), a("ci"), 4095, AND)
-        cp(a("LL"), a("ca"))
-        ac(a("XLD", (1952, 4096)), ind(win, a("LL", (122, 256))))
-        cp(a("XLD", (0, 1952)), ind(win, a("LL", (0, 122))))
-        cp(a("CC"), a("pp"))
+        for f in (lambda c: tt(a("OT", twice(c)), a(TT, twice(c)), a("ps5", twice(c)), A.mult),
+                  lambda c: tt(a("ps7", c), a("ps6", c), a("OT", twice(c, 0)), A.max),
+                  lambda c: tt(a("ps3", c), a("ps7", c), a("OT", twice(c, 1)), A.max),
+                  lambda c: tt(a("ci", c), a("ps3", c), a("PC", c), A.subtract),
+                  lambda c: ts(a("ca", c), a("ci", c), 4095, AND),
+                  lambda c: cp(a("LL", c), a("ca", c))):
+            for c in parts:
+                f(c)
+        for f, c in zip((ac, cp), parts):
+            f(a("XLD", (16 * c[0], 16 * c[1])), ind(win, a("LL", c)))
+        for k in range(4):
+            cp(a("CC", (64 * k, 64 * k + 64)), a("ps2", (k, 256, 4)))
         mine = (1024 * rank, 1024 * rank + 1024)
 
         def child(f, k, c0, c1):
@@ -421,7 +506,7 @@ def rank_program(g, core, T, topo):
         for k in (1, 2, 3):
             fr = (rank - k) % 4
             done("", "a%d_%d" % (t, k), len(engines(T.cores[fr], k)), [], a(nx, (1024 * fr, 1024 * fr + 1024))[1])
-    for n, q in enumerate((rank, (rank + 2) % 4, (rank + 3) % 4, (rank + 1) % 4)):
+    for n, q in enumerate(order):
         c = (1024 * q, 1024 * q + 1024)
         dma("ys"[n % 2], a("y", c), a("X2", c), "dy%d" % q)
     for sm in sorted(total):

@@ -1,31 +1,33 @@
 import numpy as np
+from concourse.bass import DstId, RemoteDMATransfer
 from concourse.mybir import AluOpType as A, AxisListType, ActivationFunctionType as AF
 
 ROUNDS = 2
 SCRATCH = {}
 DTN = {"b": "bfloat16", "f": "float32", "i": "int32", "u": "uint16"}
 for _w in """X0 4096 b,X1 4096 b,X2 4096 b,XLD 4096 b,XR 4096 b,R8 256x8 b,R2 128 b,DF 8192 b,AD 8192 b,wti 1 i,kmi 4 i,thi 2 i,wtf 1 f,kmf 4 f,
-T4 2 f,BM 128 f,MQ 16 f,Zx 144 b,ipart 1 i,IC 160 f,GM 128 f,IK8 256 f,PC 256 f,CJ 256 f,BNbe 16 f,BNeb 16 f,PI 8 i,PF 8 f,PD 24 f,WH 128 b,Zd 144 b,
-ID 128 b,IDn 128 b,IDf 128 f,IDfn 128 f,Zx0 144 b,Zx1 144 b,BS0 128 b,BS1 128 b,BS2 128 b,BSL 128 b,jn 8 i,CB 8x8 i,CTb 8x32 b,CTT 8x32 b,CL 8x128 b,
-CTR 16 f,iT 16 f,iT1 16 f,iW 16 f,W256 16 f,WD 256 b,
-U1 256 i,U 256 i,UU 256 i,UB 256 i,CA 2x256 i,CI 2x256 i,CU 2x256 u,CF 2x256 f,HP 256 i,W0 256 f,pen 2x256 f,km0 256 f,km1 256 f,kt 256 f,SC 256 f,
+T4 2 f,MQ 16 f,Zx 144 b,ipart 1 i,IC 160 f,GM 128 f,IK8 256 f,PC 256 f,CJ 256 f,BNbe 16 f,BNeb 16 f,PI 8 i,PF 8 f,PD 24 f,WH 128 b,Zd 144 b,
+ID 128 b,IDn 128 b,IDf 128 f,IDfn 128 f,SE 128 f,SEn 128 f,Zx0 144 b,Zx1 144 b,jn 8 i,CB 8x8 i,CTb 8x32 b,CTT 8x32 b,CL 8x128 b,
+CTR 16 f,iT 16 f,iT1 16 f,iW 16 f,W256 16 f,WD 256 b,RP 256 b,LC 256 b,LO 256 b,WL 256 f,LE 16 u,
+U1 256 i,U 256 i,UU 256 i,UB 256 i,CA 2x256 i,CI 2x256 i,CU 2x256 u,CF 2x256 f,HP 256 i,W0 256 f,pen 2x256 f,km2 2x256 f,kt 2x256 f,SC 2x256 f,
 RSi 256 b,RS 256 f,best 16 i,Jt 16 i,Jx 16 b,LJ 16 u,PX 272 b,FJ 256 b,WJ 256 b,NE 16 f,FI 16x32 i,FB 16x32 b,RT 512 b,SH 8x256 f,SCN 16x128 f,
-AI 16 i,PZ 16x4 i,F2 16x16 b,RT2 256 b,R16 256 f,NTW 16 f,SLf 16 f,SL 16 u,RL 16 u,Lc 1 f,L4 1 f,Lh 1 f,y1 256 f,y2 256 f,
-sg 256 f,t2 256 f,CC 256 u,G 256 f,Yc 256 f,sti 256 f,WF 256 f,LI 16 i,Q 256 f,LU 16 u,ci 256 i,ca 256 i,LL 256 u,PW 9x256 b,YW 9x256 f,YB 8x256 f,WS 8x256 b,
-LV 8x16 u,YT0 528 f,TT0 512 f,YT1 528 f,TT1 512 f,OT 512 f,OB 6x1024 b""".replace("\n", "").split(","):
+AI 16 i,PZ 2x16 i,FP 2x256 b,FQ 2x256 b,Y0 2x256 b,R16 256 f,NTW 16 f,SLf 16 f,SL 16 u,RL 16 u,Lc 4 f,y1 256 f,y2 256 f,
+sg 256 f,t2 256 f,CC 256 u,G 256 f,Yc 256 f,sti 256 f,WF 256 f,LI 16 i,Q 256 f,LU 16 u,ci 256 i,ca 256 i,LL 256 u,PW 13x256 b,YW 13x256 f,
+WS 13x256 b,LV 12x16 u,YT0 528 f,TT0 512 f,YT1 528 f,TT1 512 f,OT 512 f,OB 6x1024 b""".replace("\n", "").split(","):
     _n, _s, _d = _w.split()
     SCRATCH[_n] = ("sbuf", [128] + [int(z) for z in _s.split("x")], DTN[_d])
 for _b in range(8):
     SCRATCH["ps%d" % _b] = ("psum", [128, 512], "float32")
-SEMAPHORES = (["cv", "cs", "ct", "cg", "dwt", "dkm", "dth"] + ["d%s%d" % (x, q) for x in "xy" for q in range(4)]
+SEMAPHORES = (["cv", "cs", "ct", "cg", "dwt", "dkm", "dth", "le", "e1", "e2", "e3"] + ["d%s%d" % (x, q) for x in "xy" for q in range(4)]
               + ["%s%d_%d" % (x, t, k) for x in "al" for t in range(ROUNDS) for k in (1, 2, 3)])
 P24 = 16777216.0
 ROUNDER = 12582912.0
 HOLD = 8192.0
+STEPS = 12
 COPY, ABS = AF.Copy, AF.Abs
 SHR, AND = A.arith_shift_right, A.bitwise_and
 NUM = {n: np.arange(int(np.prod(s[1][1:]))).reshape(s[1][1:]) for n, s in SCRATCH.items()}
-OPT = dict(split=122, first=32, last=32, hs=2)
+OPT = dict(split=128, last=32, lag1=3, lag2=8, cut=7)
 
 
 def rank_program(g, core, T, topo):
@@ -145,8 +147,8 @@ def rank_program(g, core, T, topo):
         for x in range(2):
             mm(a(ps, (x, 16, 2)), [(a("Zx%d" % x, (16 - 16 * e, 144 - 16 * e)), f(e)) for e in range(2)])
 
-    def hold(out, x):
-        scan(out, a("WD"), x, A.mult, A.max)
+    def hold(out, x, o=A.max):
+        scan(out, a("WD"), x, A.mult, o)
 
     def pf(n):
         return a("PF", (n, n + 1))
@@ -154,16 +156,24 @@ def rank_program(g, core, T, topo):
     def pd(n):
         return a("PD", (n, n + 1))
 
-    order = [(rank - k) % 4 for k in (0, 2, 1, 3)]
+    def lc(n):
+        return a("Lc", (n, n + 1))
+
+    def weave(*lists):
+        for n in range(max(len(x) for x in lists)):
+            for x in lists:
+                if n < len(x) and x[n]:
+                    x[n]()
+
     dma("y", a("wti"), a("wt"), "dwt")
     dma("s", a("kmi"), a("km"), "dkm")
     dma("s", a("thi"), a("th"), "dth")
-    for q in order:
+    for q in range(4):
         dma("y", a("X0", (1024 * q, 1024 * q + 1024)), a("gen0", (1024 * q, 1024 * q + 1024)), "dx%d" % q)
     iota(a("ipart"), [[0, 1]], 0, 1)
-    iota(a("jn"), [[32, 8]], 0, 1)
     iota(a("GM"), [[16, 8], [0, 16]])
     iota(a("IC"), [[1, 160]])
+    iota(a("jn"), [[32, 8]], 0, 1)
     for f, pt in ((5, [[0, 4], [1, 2]]), (6, [[0, 2], [1, 2], [0, 2]]), (7, [[1, 2], [0, 4]])):
         iota(a("CB", (), f), pt)
     iota(a("RSi"), [[0, 16], [1, 16]])
@@ -171,13 +181,13 @@ def rank_program(g, core, T, topo):
     iota(a("BNbe"), [[32, 8], [0, 2]])
     iota(a("PC"), [[16, 256]])
     iota(a("IK8"), [[1, 256]])
-    iota(a("F2"), [[0, 256]], 1)
+    iota(a("FB"), [[0, 512]])
+    iota(a("FP"), [[0, 512]])
     iota(a("PX", (256, 272)), [[0, 16]], 512)
     iota(a("CJ"), [[16, 256]], 15)
     for t in range(ROUNDS):
         for n, w in (("YT", 528), ("TT", 512)):
             iota(a(n + str(t)), [[0, w]])
-    ms(a("FB"), 0.0)
     ms(a("CTb", (), (21, 32)), 0.0)
     for f, c in ((8, 4096.0), (9, 1048576.0), (10, 1.0), (11, P24), (20, 16.0)):
         ms(a("CTb", (), f), c)
@@ -191,113 +201,133 @@ def rank_program(g, core, T, topo):
     ic = a("IC", (0, 144))
     lin(pd(0), pf(1), 1.0, 15.0)
     lin(pd(1), pf(3), 1.0, 16.0)
+    lin(pd(15), pf(0), 1.0, 1.0)
     lin(pd(2), pf(4), -1.0, 1.0)
     lin(pd(3), pf(0), -1.0, 0.0)
-    lin(pd(4), pf(0), -1.0, 4095.0 + ROUNDER)
-    lin(pd(15), pf(0), 1.0, 1.0)
+    lin(pd(4), pf(0), -1.0, 4096.0 + ROUNDER)
     for f in range(5):
         ts(a("CB", (), f), a("jn"), f, SHR, 1, AND)
-    ts(a("BM"), a("GM"), pf(1), A.is_equal)
     ts(a("IDf"), a("IC", (0, 128)), pf(6), A.is_equal)
     ts(a("MQ"), a("IC", (0, 16)), pf(0), A.is_equal)
     ts(a("PD", (8, 12)), a("IC", (0, 4)), pf(5), A.is_equal)
     ts(a("Zd"), ic, pd(0), A.is_equal, 4096.0, A.mult)
-    ts(a("Zx"), ic, pd(1), A.is_equal)
-    ts(a("CTb", (), (0, 8)), a("CB"), -P24, A.mult, P24, A.add)
-    ts(a("CTb", (), (12, 20)), a("CB"), P24, A.mult)
     cp(a("wtf"), a("wti"))
     cp(a("kmf"), a("kmi"))
-    ts(a("WH"), a("BM"), a("wtf"), A.mult)
-    tr(a("CTT"), a("CTb"))
-    ts(a("FJ"), a("RSi"), pf(0), A.not_equal)
-    ts(a("WJ"), a("RSi"), pd(15), A.is_equal, HOLD, A.mult)
-    ts(a("T4"), a("thi"), 4096.0, A.mult)
-    tt(a("WD"), a("FJ"), a("WJ"), A.max)
+    ts(a("Zx"), ic, pd(1), A.is_equal)
+    ts(a("WH"), a("GM"), pf(1), A.is_equal, a("wtf"), A.mult)
     ac(a("ID"), a("IDf"))
     lin(a("IDn"), a("IDf"), -1.0, 0.0)
-    lin(a("RS"), a("RSi"), -2 * P24, 2 * P24, AF.Relu)
-    lin(a("iT"), a("BNeb"), 1.0, pf(2))
-
-    def mq(n):
-        return a("MQ", (n, n + 1))
+    q15 = a("MQ", (15, 16))
+    spare = [lambda: ts(a("CTb", (), (0, 8)), a("CB"), -P24, A.mult, P24, A.add),
+             lambda: ts(a("CTb", (), (12, 20)), a("CB"), P24, A.mult),
+             lambda: ts(a("FJ"), a("RSi"), pf(0), A.not_equal),
+             lambda: ts(a("WJ"), a("RSi"), pd(15), A.is_equal, HOLD, A.mult),
+             lambda: tr(a("CTT"), a("CTb")),
+             lambda: tt(a("WD"), a("FJ"), a("WJ"), A.max),
+             lambda: ts(a("SE"), a("GM"), pf(1), A.is_equal, q15, A.mult),
+             lambda: ts(a("T4"), a("thi"), 4096.0, A.mult)]
 
     def late():
-        ac(a("FB", (), 20), a("iT"))
-        lin(a("iT1"), a("iT"), 1.0, 1.0)
+        lin(a("iT"), a("BNeb"), 1.0, pf(2))
+        lin(a("BNbe"), a("BNbe"), 1.0, pf(2))
         for n in range(4):
             lin(a("CL", (), (32 * n, 32 * n + 32)), a("CTT"), pd(8 + n), 0.0, COPY)
-        lin(a("BNbe"), a("BNbe"), 1.0, pf(2))
-        lin(pd(6), mq(1), -1.0, 0.0)
-        lin(pd(7), mq(2), -16.0, 0.0)
-        lin(pd(17), mq(3), 1.0, mq(0))
-        lin(pd(12), mq(15), 1.0 - 1.0 / HOLD, 1.0 / HOLD)
-        lin(pd(14), mq(15), 1.0 - HOLD, HOLD)
-        lin(pd(18), mq(3), 15.0, pd(6))
+            if n == 0:
+                ac(a("FB", (), 20), a("iT"))
+                lin(a("iT1"), a("iT"), 1.0, 1.0)
+        lin(pd(12), q15, 1.0 - 1.0 / HOLD, 1.0 / HOLD)
+        lin(pd(14), q15, 1.0 - HOLD, HOLD)
         lin(a("CTR"), a("BNbe"), 16.0, float(4080 * 4096 + 15))
         lin(a("Zx0"), a("Zx"), pd(2), 0.0, COPY)
-        lin(pd(19), mq(2), 16.0, pd(18))
         lin(a("Zx1"), a("Zx"), pf(4), 0.0, COPY)
-        for n, c in (("0", 17), ("1", 18), ("2", 7), ("L", 19)):
-            lin(a("BS" + n), a("BM"), pd(c), 0.0, COPY)
-
-    def later():
+        lin(a("RP"), a("RSi"), 1.0, 0.0, AF.Sign)
         lin(a("IK8"), a("IK8"), 1.0 / 256, 0.0)
         lin(a("PC"), a("PC"), 1.0, pf(0))
-        lin(a("IDfn"), a("IDf"), -1.0, 0.0)
+
+    def later():
         lin(pd(20), pd(14), 257.0, 0.0)
-        lin(pd(13), pd(12), 0.125, 0.0)
+        lin(a("IDfn"), a("IDf"), -1.0, 0.0)
+        lin(a("SEn"), a("SE"), -1.0, 0.0)
+        lin(pd(13), pd(12), -0.125, 0.0)
         lin(a("iW"), a("PC", (0, 16)), pd(14), pd(14))
         lin(a("W256"), a("PC", (0, 16)), pd(14), pd(20))
     lo, col15 = (0, 256), (15, 256, 16)
+
+    def to(k):
+        return T.cores[(rank + k) % 4]
+
+    def engines(src, k):
+        dst = T.cores[(T.rank_of(src) + k) % 4]
+        es = topo.engines(src, dst)
+        if topo.chip(src) == topo.chip(dst):
+            es = [x for x in es if x not in topo.engines(src, T.cores[(T.rank_of(src) + 1) % 4])]
+        return es
+
+    def share(src, k):
+        es = engines(src, k)
+        return es if k == 2 else es[len(es) // 2 * (k // 2):][:len(es) // 2]
 
     for t in range(ROUNDS):
         xn, nx = "X%d" % t, "X%d" % (t + 1)
         win = a(xn, (0, 4096))
 
         def last(i):
-            return a(xn, (16 * i[0] + 15, 16 * i[1], 16))
+            return a("LC", i) if t else a(xn, (16 * i[0] + 15, 16 * i[1], 16))
 
         def quarter(n):
-            return (64 * order[n], 64 * order[n] + 64)
+            return (64 * n, 64 * n + 64)
 
         def hashes(i):
             j = (256 + i[0], 256 + i[1])
-            mm(a("ps7", i), [(a("WH"), last(i))])
-            return [lambda: cp(a("U1", i), a("ps7", i)),
+            return [lambda: mm(a("ps7", i), [(a("WH"), last(i))]),
+                    lambda: cp(a("U1", i), a("ps7", i)),
                     lambda: ts(a("U", i), a("U1", i), 4095, AND),
-                    lambda: ts(a("ps6", i), a("U", i), a("kmf", (2 * t, 2 * t + 1)), A.mult),
                     lambda: tt(a("UU", i), a("U", i), a("U", i), A.mult),
-                    lambda: ts(a("ps6", j), a("U", i), a("kmf", (2 * t + 1, 2 * t + 2)), A.mult),
+                    lambda: ts(a("ps6", i), a("U", i), a("kmf", (2 * t, 2 * t + 1)), A.mult),
                     lambda: ts(a("UB", i), a("UU", i), 5, SHR),
-                    lambda: ts(a("HP", i), a("U", i), 127, AND),
+                    lambda: ts(a("ps6", j), a("U", i), a("kmf", (2 * t + 1, 2 * t + 2)), A.mult),
                     lambda: tt(a("CA", 0, i), a("ps6", i), a("UB", i), A.add),
                     lambda: tt(a("CA", 1, i), a("ps6", j), a("UB", i), A.add),
-                    lambda: ts(a("W0", i), a("HP", i), pd(3), A.mult, pd(4), A.add),
-                    lambda: ts(a("CI", (), i), a("CA", (), i), 4095, AND),
-                    lambda: cp(a("CU", (), i), a("CI", (), i)),
-                    lambda: cp(a("CF", (), i), a("CI", (), i))]
-        for n in range(3):
-            i = quarter(n)
-            hs = hashes(i)
-            ac(a("R8", i, 0), last(i))
-            ac(a("R8", i, 1), last(i))
-            ac(a("R8", i, (2, 4)), a("R8", i, (0, 2)))
-            ac(a("R8", i, (4, 8)), a("R8", i, (0, 4)))
-            ac(a("XR", (16 * i[0], 16 * i[1], 2)), a("R8", i, ()))
-            for f in hs:
-                f()
+                    lambda: ts(a("CI", 0, i), a("CA", 0, i), 4095, AND),
+                    lambda: ts(a("CI", 1, i), a("CA", 1, i), 4095, AND),
+                    lambda: cp(a("CU", 0, i), a("CI", 0, i)),
+                    lambda: cp(a("CU", 1, i), a("CI", 1, i))]
+
+        def repeats(i):
+            return [lambda: ac(a("R8", i, 0), last(i)),
+                    lambda: ac(a("R8", i, 1), last(i)),
+                    lambda: ac(a("R8", i, (2, 4)), a("R8", i, (0, 2))),
+                    lambda: ac(a("R8", i, (4, 8)), a("R8", i, (0, 4))),
+                    lambda: ac(a("XR", (16 * i[0], 16 * i[1], 2)), a("R8", i, ()))]
+
+        def odd(i):
             cp(a("XR", (16 * i[0] + 1, 16 * i[1], 2)), a("R8", i, ()))
+        twice0 = [lambda x=x: ac(a("R2", (x, 128, 2)), last(quarter(0))) for x in range(2)]
+        if t == 0:
+            weave(repeats(quarter(1)), twice0)
+            lin(a("RS"), a("RSi"), -2 * P24, 2 * P24, AF.Relu)
+            weave(repeats(quarter(2)), repeats(quarter(3)))
+            weave(spare)
+            rest = hashes((128, 256))
+            weave(hashes(quarter(0)), [None] * OPT["lag1"] + hashes(quarter(1)), [None] * OPT["lag2"] + rest[:OPT["cut"]])
+            rest = rest[OPT["cut"]:]
+        else:
+            weave(repeats(quarter(1)), repeats((128, 256)), twice0)
+            ac(a("XR", (16 * 128 + 1, 4096, 2)), a("R8", (128, 256), ()))
+            weave(hashes((0, 128)), hashes((128, 256)))
+            rest = []
+        odd(quarter(1))
 
         def span(h, i):
             return (4096 * h + 16 * i[0], 4096 * h + 16 * i[1])
 
-        def keys(n, h):
-            return a("ps4", (0, 64)) if (n, h) == (2, 1) else a("ps%d" % n, (64 * h, 64 * h + 64))
+        def keys(h, i):
+            return a("ps%d" % (2 * h + 2 if i[0] == 192 else h), i)
 
         def sums(n, h):
             i = quarter(n)
             d = span(h, i)
-            mm(keys(n, h), [(a("IDf"), a("CF", h, i))] + [(a("Zd", (15 - p, 143 - p)), a("AD", (d[0] + p, d[1], 16))) for p in range(16)])
+            mm(keys(h, i), [(a("IDf"), a("CF", h, i))] + [(a("Zd", (15 - p, 143 - p)), a("AD", (d[0] + p, d[1], 16))) for p in range(16)])
 
         def less(h, i):
             tt(a("DF", span(h, i)), ind(win, a("CU", h, i)), a("XR", (16 * i[0], 16 * i[1])), A.subtract)
@@ -305,71 +335,71 @@ def rank_program(g, core, T, topo):
         def absolute(h, i):
             ac(a("AD", span(h, i)), a("DF", span(h, i)), ABS)
 
-        def plain(f, n, h, banks):
-            i = quarter(n)
-            d = span(h, i)[0]
-            f(a("DF", span(h, i)), ind(win, a("CU", h, i)))
-            for j, b in enumerate(banks):
-                x0 = 16 * i[0] + 512 * j
-                mm(a(b), [(a("ID"), a("DF", (d + 512 * j, d + 512 * j + 512)))]
-                   + ([(a("IDn"), a("R2", (64 * j, 64 * j + 64)), a(b, (x, 512, 8))) for x in range(8)] if n == 3
-                      else [(a("IDn"), a("XR", (x0, x0 + 512)))]))
+        def plain(h):
+            ac(a("DF", span(h, quarter(0))), ind(win, a("CU", h, quarter(0))))
 
-        def plain_end(n, h, banks):
-            d = span(h, quarter(n))[0]
+        def plain_less(h, banks):
             for j, b in enumerate(banks):
-                ac(a("AD", (d + 512 * j, d + 512 * j + 512)), a(b), ABS)
-            sums(n, h)
+                d = 4096 * h + 512 * j
+                mm(a(b), [(a("ID"), a("DF", (d, d + 512)))]
+                   + [(a("IDn"), a("R2", (64 * j, 64 * j + 64)), a(b, (x, 512, 8))) for x in range(8)])
 
-        def bests(n):
-            i = quarter(n)
-            return [lambda: ts(a("pen", 0, i), keys(n, 0), a("T4", (0, 1)), A.is_ge, 2 * P24, A.mult),
-                    lambda: tt(a("km0", i), keys(n, 0), a("pen", 0, i), A.max),
-                    lambda: ts(a("pen", 1, i), keys(n, 1), a("T4", (1, 2)), A.is_ge, 2 * P24, A.mult),
-                    lambda: tt(a("ps6", i), keys(n, 1), a("pen", 1, i), A.max),
-                    lambda: tt(a("km1", i), a("ps6", i), a("km0", i), A.min),
-                    lambda: tr(a("kt", i), a("km1", i)),
-                    lambda: scan(a("SC", i), a("RS", i), a("kt", i), A.max, A.min)]
-        q0, q1, q2 = quarter(0), quarter(1), quarter(2)
-        f0, l0 = q0[0] + OPT["first"], q2[1] - OPT["last"]
-        hs = hashes(quarter(3))
-        for x in range(2):
-            ac(a("R2", (x, 128, 2)), last(quarter(3)))
-        plain(ac, 0, 0, ("ps4", "ps5"))
-        less(1, (q0[0], f0))
-        for f in hs[:OPT["hs"]]:
-            f()
-        less(1, (f0, q0[1]))
-        for f in hs[OPT["hs"]:]:
-            f()
-        absolute(1, (q0[0], f0))
-        plain_end(0, 0, ("ps4", "ps5"))
-        absolute(1, (f0, q0[1]))
-        sums(0, 1)
-        plain(cp, 3, 1, ("ps7", "ps2"))
-        plain(ac, 3, 0, ("ps4", "ps5"))
-        less(0, q1)
-        plain_end(3, 1, ("ps7", "ps2"))
-        plain_end(3, 0, ("ps4", "ps5"))
-        absolute(0, q1)
+        def plain_end(h, banks):
+            for j, b in enumerate(banks):
+                d = 4096 * h + 512 * j
+                ac(a("AD", (d, d + 512)), a(b), ABS)
+            sums(0, h)
+
+        def bests(h, i):
+            return [lambda: ts(a("pen", h, i), keys(h, i), a("T4", (h, h + 1)), A.is_ge, 2 * P24, A.mult),
+                    lambda: tt(a("km2", h, i), keys(h, i), a("pen", h, i), A.max),
+                    lambda: tr(a("kt", h, i), a("km2", h, i)),
+                    lambda: scan(a("SC", h, i), a("RS", i), a("kt", h, i), A.max, A.min)]
+        q1, q2, q3 = quarter(1), quarter(2), quarter(3)
+        l0 = 256 - OPT["last"]
+        plain(0)
+        plain_less(0, ("ps4", "ps5"))
+        if rest:
+            weave([lambda x=x: less(0, (x, x + 16)) for x in range(64, 128, 16)], rest[0::2], rest[1::2])
+            odd((128, 256))
+        else:
+            less(0, (64, 96))
+            less(0, (96, 128))
+        cp(a("CF", 0, ()), a("CI", 0, ()))
+        absolute(0, (64, 96))
+        absolute(0, (96, 128))
+        less(1, q1)
+        cp(a("CF", 1, ()), a("CI", 1, ()))
         sums(1, 0)
-        for n, h in ((1, 1), (2, 0)):
-            less(h, quarter(n))
-            absolute(h, quarter(n))
-            sums(n, h)
-        for i in ((q2[0], l0), (l0, q2[1])):
-            less(1, i)
-            absolute(1, i)
+        plain_end(0, ("ps4", "ps5"))
+        plain(1)
+        less(0, q2)
+        absolute(1, q1)
+        plain_less(1, ("ps3", "ps7"))
+        sums(1, 1)
+        less(1, q2)
+        absolute(0, q2)
+        plain_end(1, ("ps3", "ps7"))
+        sums(2, 0)
+        less(0, q3)
+        absolute(1, q2)
         sums(2, 1)
+        less(1, (192, l0))
+        absolute(0, q3)
+        sums(3, 0)
+        less(1, (l0, 256))
+        absolute(1, (192, l0))
+        absolute(1, (l0, 256))
+        sums(3, 1)
         if t == 0:
             late()
-        for fs in zip(bests(0), bests(3), bests(1)):
-            for f in fs:
-                f()
-        for f in bests(2):
-            f()
+        weave(bests(0, (0, 192)), bests(1, (0, 192)))
+        halves = ((0, 128), (128, 256))
+        weave(bests(0, q3), bests(1, q3), [lambda c=c: ts(a("HP", c), a("U", c), 127, AND) for c in halves]
+              + [lambda c=c: ts(a("W0", c), a("HP", c), pd(3), A.mult, pd(4), A.add) for c in halves])
         for e in range(2):
-            cp(a("best", (8 * e, 8 * e + 8)), a("SC", (16 * e + 15, 256, 32)))
+            c = (16 * e + 15, 256, 32)
+            tt(a("best", (8 * e, 8 * e + 8)), a("SC", 0, c), a("SC", 1, c), A.min)
         be = a("best")
         ts(a("Jt"), be, 4, SHR, 255, AND)
         for f in range(8):
@@ -379,84 +409,113 @@ def rank_program(g, core, T, topo):
         ts(a("FI", (), 9), be, 20, SHR, 31, AND)
         ts(a("FI", (), 10), be, 1, SHR, 7, AND)
         ts(a("FB", (), (12, 20)), a("FI", (), (0, 8)), -1.0, A.mult, 1.0, A.add)
-        cp(a("FB", (), (0, 12)), a("FI", (), (0, 12)))
         tt(a("Jx"), a("Jt"), a("iT1"), A.max)
+        cp(a("FB", (), (0, 12)), a("FI", (), (0, 12)))
+        ms(a("ps6", (0, 1)), 0.0)
         tr(a("RT"), a("FB"))
-        for b in (0, 7, 1, 6, 2, 5, 3, 4):
-            w = 32 * b + 32
+        banks = ["ps%d" % b for b in (0, 1, 2, 3, 4, 5, 7)]
+        bk = {0: (banks[0], 0), 1: (banks[0], 64)}
+        bk.update({b: (banks[b - 1], 0) for b in range(2, 8)})
+        for b in (0, 1, 7, 2, 6, 3, 5, 4):
+            w, (ps, o) = 32 * b + 32, bk[b]
             for e in range(2):
-                mm(a("ps%d" % b, (w * e, w * e + w)), [(a("CL", b, ()), a("RT", (256 * e, 256 * e + w)))])
+                mm(a(ps, (o + w * e, o + w * e + w)), [(a("CL", b, ()), a("RT", (256 * e, 256 * e + w)))])
             if b > 3:
-                ac(a("SH", b, (0, w)), a("ps%d" % b, (1, 2 * w, 2)))
+                ac(a("SH", b, (0, w)), a(ps, (1, 2 * w, 2)))
         if t == 0:
             later()
-        for b in (0, 1, 7, 2, 6, 3, 5, 4):
-            w = 32 * b + 32
+        for b in (0, 1, 2, 7, 3, 6, 5, 4):
+            w, (ps, o) = 32 * b + 32, bk[b]
             for e in range(2):
                 if b > 3:
-                    scan(a("SCN", 2 * b + e, (128 - w // 2, 128)), a("ps%d" % b, (w * e, w * e + w, 2)),
+                    scan(a("SCN", 2 * b + e, (128 - w // 2, 128)), a(ps, (w * e, w * e + w, 2)),
                          a("SH", b, (w // 2 * e, w // 2 * (e + 1))), A.min, A.min, 2 * P24)
                 else:
-                    red(a("SCN", 2 * b + e, (127, 128)), a("ps%d" % b, (w * e, w * e + w)), A.min)
+                    red(a("SCN", 2 * b + e, (127, 128)), a(ps, (o + w * e, o + w * e + w)), A.min)
         wrap("ps0", lambda e: a("Jx", (8 * e, 8 * e + 8)))
         tt(a("AI"), a("SCN", (), 127), a("CTR"), A.min)
-        ts(a("PZ", (), 0), a("AI"), 4, SHR, 255, AND)
-        ts(a("PZ", (), 1), a("AI"), 15, AND)
-        ts(a("PZ", (), 2), a("AI"), 3, SHR, 1, AND)
         cp(a("LJ"), a("ps0", (0, 16)))
-        cp(a("F2", (), (0, 3)), a("PZ", (), (0, 3)))
-        wrap("ps3", lambda e: a("F2", (e, 16, 2), 0))
-        tr(a("RT2"), a("F2"))
-        for n, b in (("0", 4), ("1", 5), ("L", 7), ("2", 6)):
-            mm(a("ps%d" % b, lo), [(a("BS" + n), a("RT2"))])
-        cp(a("LV", 0, ()), a("ps3", (0, 16)))
-        ac(a("PX", lo), a("ps4", lo))
-        cp(a("YW", 0, ()), a("ps5", lo))
-        cp(a("YB", 0, ()), a("ps5", lo))
+        ts(a("PZ", 0, ()), a("AI"), 4, SHR, 255, AND)
+        ts(a("PZ", 1, ()), a("AI"), 15, AND)
+        ts(a("FP", 0, (0, 256, 16)), a("PZ", 0, ()), 1.0, A.add)
+        ts(a("FP", 1, (0, 256, 16)), a("PZ", 1, ()), -1.0, A.mult, 15.0, A.add)
+        wrap("ps3", lambda e: a("FP", 0, (16 * e, 256, 32)))
+        for n in range(2):
+            scan(a("FQ", n, ()), a("RP"), a("FP", n, ()), A.mult, A.add)
+        tr(a("PX", lo), a("FQ", 0, ()))
+        ts(a("LV", 0, ()), a("ps3", (0, 16)), -1.0, A.add)
+        for n in range(2):
+            tr(a("Y0", n, ()), a("FQ", 1, ()))
 
-        def beside(n):
-            if n < 4:
-                ac(a("FJ", (64 * n, 64 * n + 64)), ind(a("PX", (0, 272)), a("LJ", (4 * n, 4 * n + 4))))
-            elif n == 4:
-                hold(a("WJ"), a("FJ"))
-            elif n == 5:
-                tt(a("NE"), a("WJ", col15), a("iW"), A.is_equal)
+        y0 = a("Y0", 0, ())
+        terms = ((a("W0"), 0), (a("y2"), 1), (a("t2"), 0))
+
+        def places():
+            mm(a("ps2", lo), [(a("IDfn" if n else "IDf"), x) for x, n in terms])
+            if t == 0:
+                for k in range(4):
+                    mm(a("ps5", (64 * k, 64 * k + 64)),
+                       [(a("SEn" if n else "SE"), a(x, (k, 256, 4))) for x, n in (("W0", 0), ("y2", 1), ("t2", 0))])
+        by_scalar = [
+            lambda: run("s", lambda: s.activation(T.sg[:], y0[0], ABS, bias=-8.0, accum_out=lc(0)[0]),
+                        (None, a("sg")[1] + lc(0)[1]), (y0,)),
+            lambda: lin(lc(1), lc(0), 1.0, 2048.0),
+            lambda: [lin(a("y1"), a("IK8"), lc(1), 1.0 / 512 - 0.5), lin(lc(2), lc(0), -1.0, 2048.5)],
+            lambda: [lin(a("y2"), a("y1"), 1.0, ROUNDER), lin(lc(3), lc(0), 0.5, 1024.0),
+                     mm(a("ps1", lo), [(a("IDf"), a("W0")), (a("IDfn"), a("y2"))])],
+            lambda: ac(a("FJ", (0, 128)), ind(a("PX", (0, 272)), a("LJ", (0, 8)))),
+            lambda: ac(a("FJ", (128, 256)), ind(a("PX", (0, 272)), a("LJ", (8, 16)))),
+            lambda: lin(a("sg"), a("ps1", lo), -1.0, lc(2), AF.Sign),
+            lambda: [lin(a("t2"), a("sg"), lc(3), lc(3)), places()],
+            lambda: lin(a("R16"), y0, -2.0, 16.0, AF.Relu),
+            lambda: lin(a("ps4", (0, 512, 2)), a("PC"), 4097.0, 4096.0),
+            lambda: lin(a("ps4", (1, 512, 2)), a("PC"), 4097.0, 4096.0)]
+        by_vector = {7: lambda: hold(a("WJ"), a("FJ")),
+                     8: lambda: tt(a("NE"), a("WJ", col15), a("iW"), A.is_equal),
+                     9: lambda: tt(a("NTW"), a("NE"), a("W256"), A.mult)}
+
+        def summed(n, m, c):
+            o = 2 * n - 3 - m
+            tt(a("YW", n, c), ind(a("YW", o, ()) if o > 0 else y0, a("LV", m, (c[0] // 16, c[1] // 16))),
+               a("YW", m, c) if m else a("Y0", 1, c), A.add)
+        for n in range(1, STEPS + 1):
+            ac(a("PW", n, ()), ind(a("PW", n - 1, ()) if n > 1 else a("PX", lo), a("LV", max(n - 2, 0), ())))
+            if n < STEPS:
+                by_scalar[n - 1]()
+            if n < STEPS - 1:
+                if n == 1:
+                    summed(n, n - 1, lo)
+                hold(a("WS", n, ()), a("PW", n, ()))
+                if n > 1:
+                    summed(n, n - 1, (0, 128))
+                ts(a("LV", n, ()), a("WS", n, col15), pd(12), A.mult, -1.0, A.add)
+                if n > 1:
+                    summed(n, n - 1, (128, 256))
+                if n in by_vector:
+                    by_vector[n]()
             else:
-                tt(a("NTW"), a("NE"), a("W256"), A.mult)
-        for n in range(8):
-            L = a("LV", n, ())
-            ac(a("PW", n + 1, ()), ind(a("PW", n, ()) if n else a("PX", lo), L))
-            tt(a("YW", n + 1, ()), ind(a("YW", n, ()), L), a("YB", n, ()), A.add)
-            hold(a("WS", n, ()), a("PW", n + 1, ()))
-            if n < 7:
-                ac(a("YB", n + 1, ()), a("YW", n + 1, ()))
-                beside(n)
-                ts(a("LV", n + 1, ()), a("WS", n, col15), pd(12), A.mult, -1.0, A.add)
+                summed(n, STEPS - 2, lo)
         YT, TT = ["%s%d" % (x, t) for x in ("YT", "TT")]
-        yf = a("YW", 8, ())
-        ac(a("R16"), a("ps6", lo))
+        yf, root = a("YW", STEPS, ()), a("WS", STEPS, col15)
         lin(a("Yc"), yf, -1.0, 4097.0)
-        run("s", lambda: s.activation(T.sg[:], T.ps7[:, 0:256], COPY, accum_out=T.Lc[:]),
-            (None, a("sg")[1] + a("Lc")[1]), (a("ps7", lo),))
-        for x in range(2):
-            lin(a("ps4", (x, 512, 2)), a("PC"), 4097.0, 4096.0)
-        lin(a("y1"), a("IK8"), a("Lc"), 1.0 / 512 - 0.5)
-        lin(a("L4"), a("Lc"), -1.0, 4095.5)
-        lin(a("y2"), a("y1"), 1.0, ROUNDER)
-        lin(a("Lh"), a("Lc"), 0.5, 0.0)
-        mm(a("ps1", lo), [(a("IDf"), a("W0")), (a("IDfn"), a("y2"))])
-        tt(a("SLf"), a("WS", 7, col15), a("NTW"), A.max)
-        ts(a("RL"), a("WS", 7, col15), pd(12), A.mult, -1.0, A.add)
+        hold(a("WS", STEPS, ()), a("PW", STEPS, ()))
+        kids = [lambda k=k: ts(a("CC", (64 * k, 64 * k + 64)), a("ps2", (k, 256, 4)), -1.0, A.add) for k in range(4)]
+        kids[0]()
+        tt(a("SLf"), root, a("NTW"), A.max)
+        ts(a("RL"), root, pd(12), A.mult, -1.0, A.add)
+        kids[1]()
         ts(a("SL"), a("SLf"), pd(12), A.mult, -1.0, A.add)
+        kids[2]()
+        kids[3]()
         cp(ind(a(YT, (8, 520)), a("SL")), yf)
-        scan(a("G"), a("R16"), a(YT, (7, 263)), A.add, A.subtract)
-        ms(a("ps6", (0, 1)), 0.0)
-        tt(a("sti"), ind(a("G", lo), a("RL")), a("Yc"), A.add)
-        lin(a("Q"), a("sti"), 4097.0, -4097.0)
-        lin(a("sg"), a("ps1", lo), -1.0, a("L4"), AF.Sign)
-        lin(a("t2"), a("sg"), a("Lh"), a("Lh"))
-        mm(a("ps2", lo), [(a("IDf"), a("W0")), (a("IDfn"), a("y2")), (a("IDf"), a("t2"))])
-        hold(a("WF"), a("sti"))
+        if t == 0:
+            hold(a("WL"), a("ps5", lo))
+        scan(a("G"), a("R16"), a(YT, (7, 263)), A.add, A.add)
+        if t == 0:
+            ts(a("LE"), a("WL", col15), pd(12), A.mult, -1.0, A.add)
+        tt(a("sti"), ind(a("G", lo), a("RL")), a("Yc"), A.subtract)
+        lin(a("Q"), a("sti"), -4097.0, -4097.0)
+        hold(a("WF"), a("sti"), A.min)
         ts(a("LI"), a("WF", col15), pd(13), A.mult, -0.5625, A.add)
         cp(a("LU"), a("LI"))
         tt(ind(a(TT, (0, 512)), a("LU")), a("Q"), a("CJ"), A.add)
@@ -466,9 +525,10 @@ def rank_program(g, core, T, topo):
             return (2 * c[0], 2 * c[1]) if x is None else (2 * c[0] + x, 2 * c[1], 2)
         for c in parts:
             tt(a("ps5", twice(c)), a(TT, twice(c)), a("ps4", twice(c)), A.is_le)
+        tt(a("OT", twice(parts[0])), a(TT, twice(parts[0])), a("ps5", twice(parts[0])), A.mult)
         scan(a("ps6", (1, 257)), a(TT, (0, 512, 2)), a(TT, (1, 512, 2)), A.max, A.max)
-        for f in (lambda c: tt(a("OT", twice(c)), a(TT, twice(c)), a("ps5", twice(c)), A.mult),
-                  lambda c: tt(a("ps7", c), a("ps6", c), a("OT", twice(c, 0)), A.max),
+        tt(a("OT", twice(parts[1])), a(TT, twice(parts[1])), a("ps5", twice(parts[1])), A.mult)
+        for f in (lambda c: tt(a("ps7", c), a("ps6", c), a("OT", twice(c, 0)), A.max),
                   lambda c: tt(a("ps3", c), a("ps7", c), a("OT", twice(c, 1)), A.max),
                   lambda c: tt(a("ci", c), a("ps3", c), a("PC", c), A.subtract),
                   lambda c: ts(a("ca", c), a("ci", c), 4095, AND),
@@ -477,27 +537,27 @@ def rank_program(g, core, T, topo):
                 f(c)
         for f, c in zip((ac, cp), parts):
             f(a("XLD", (16 * c[0], 16 * c[1])), ind(win, a("LL", c)))
-        for k in range(4):
-            cp(a("CC", (64 * k, 64 * k + 64)), a("ps2", (k, 256, 4)))
-        mine = (1024 * rank, 1024 * rank + 1024)
+        mine, laid = (1024 * rank, 1024 * rank + 1024), a("XLD", (0, 4096))
+        if t + 1 < ROUNDS:
+            cp(a("LO", (64, 192)), ind(laid, a("LE", (4, 12))))
+            ac(a("LO", quarter(3)), ind(laid, a("LE", (12, 16))))
+            ac(a("LC", quarter(rank)), ind(laid, a("LE", (0, 4))))
+            need("g", a("LO", (64, 256))[1], [])
+            g.remote_dma_fused([RemoteDMATransfer(dst_ids=[DstId(rid=topo.addr(to(k))[0], pnc=topo.addr(to(k))[1])],
+                                                  dma_engine_mask=sum(1 << x for x in share(core, k)), remote_sem=T.sem["e%d" % k],
+                                                  src=a("LO", quarter(k))[0], dst=a("LC", quarter(rank))[0]) for k in (1, 2, 3)],
+                               local_sem=T.sem.le)
+            total["le"] = sum(len(share(core, k)) for k in (1, 2, 3))
+            for k in (1, 2, 3):
+                fr = (rank - k) % 4
+                done("", "e%d" % k, len(share(T.cores[fr], k)), [], a("LC", quarter(fr))[1])
+        for k in (1, 3, 2, 0):
+            for f, c0 in ((cp, 0), (ac, 512)):
+                out = a("OB", 3 * t + k - 1, (c0, c0 + 512)) if k else a(nx, (mine[0] + c0, mine[0] + c0 + 512))
+                f(out, ind(laid, a("CC", (64 * k + c0 // 16, 64 * k + c0 // 16 + 32))))
 
-        def child(f, k, c0, c1):
-            out = a("OB", 3 * t + k - 1, (c0, c1)) if k else a(nx, (mine[0] + c0, mine[0] + c1))
-            f(out, ind(a("XLD", (0, 4096)), a("CC", (64 * k + c0 // 16, 64 * k + c1 // 16))))
-        for k in (1, 3):
-            child(cp, k, 0, 512)
-            child(ac, k, 512, 1024)
-        child(cp, 2, 0, 1024)
-        child(ac, 0, 0, 1024)
-
-        def engines(src, k):
-            to = T.cores[(T.rank_of(src) + k) % 4]
-            es = topo.engines(src, to)
-            if topo.chip(src) == topo.chip(to):
-                es = [x for x in es if x not in topo.engines(src, T.cores[(T.rank_of(src) + 1) % 4])]
-            return es
         for k in (1, 3, 2):
-            rid, pid, _ = topo.addr(T.cores[(rank + k) % 4])
+            rid, pid, _ = topo.addr(to(k))
             es = engines(core, k)
             ob = a("OB", 3 * t + k - 1, ())
             need("g", ob[1], [])
@@ -506,9 +566,9 @@ def rank_program(g, core, T, topo):
         for k in (1, 2, 3):
             fr = (rank - k) % 4
             done("", "a%d_%d" % (t, k), len(engines(T.cores[fr], k)), [], a(nx, (1024 * fr, 1024 * fr + 1024))[1])
-    for n, q in enumerate(order):
-        c = (1024 * q, 1024 * q + 1024)
-        dma("ys"[n % 2], a("y", c), a("X2", c), "dy%d" % q)
+    for n, k in enumerate((0, 1, 2, 3)):
+        c = (1024 * ((rank - k) % 4), 1024 * ((rank - k) % 4) + 1024)
+        dma("ys"[n % 2], a("y", c), a("X2", c), "dy%d" % n)
     for sm in sorted(total):
         if know["g"].get(sm, 0) < total[sm]:
             g.wait_ge(T.sem[sm], total[sm])

@@ -5,29 +5,30 @@ from concourse.mybir import AluOpType as A, AxisListType, ActivationFunctionType
 ROUNDS = 2
 SCRATCH = {}
 DTN = {"b": "bfloat16", "f": "float32", "i": "int32", "u": "uint16"}
-for _w in """X0 4096 b,X1 4096 b,X2 4096 b,XLD 4096 b,XR 4096 b,R8 256x8 b,R2 128 b,DF 8192 b,AD 8192 b,wti 1 i,kmi 4 i,thi 2 i,wtf 1 f,kmf 4 f,
-T4 2 f,MQ 16 f,Zx 144 b,ipart 1 i,IC 160 f,GM 128 f,IK8 256 f,PC 256 f,CJ 256 f,BNbe 16 f,BNeb 16 f,PI 8 i,PF 8 f,PD 24 f,WH 128 b,Zd 144 b,
+for _w in """X0 4096 b,X1 4096 b,X2 4096 b,XLD 4096 b,XR 4096 b,R2 128 b,DF 8192 b,AD 8192 b,wti 1 i,kmi 4 i,thi 2 i,wtf 1 f,kmf 4 f,
+T4 4 f,MQ 16 f,Zx 144 b,ipart 1 i,IC 160 f,GM 128 f,IK8 256 f,PC 256 f,CJ 256 f,BNbe 16 f,BNeb 16 f,PI 8 i,PF 8 f,PD 24 f,WH 128 b,Zd 144 b,
 ID 128 b,IDn 128 b,IDf 128 f,IDfn 128 f,SE 128 f,SEn 128 f,Zx0 144 b,Zx1 144 b,jn 8 i,CB 8x8 i,CTb 8x32 b,CTT 8x32 b,CL 8x128 b,
 CTR 16 f,iT 16 f,iT1 16 f,iW 16 f,W256 16 f,WD 256 b,RP 256 b,LC 256 b,LO 256 b,WL 256 f,LE 16 u,
-U1 256 i,U 256 i,UU 256 i,UB 256 i,CA 2x256 i,CI 2x256 i,CU 2x256 u,CF 2x256 f,HP 256 i,W0 256 f,pen 2x256 f,km2 2x256 f,kt 2x256 f,SC 2x256 f,
+U1 256 i,U 256 i,UU 256 i,UB 256 i,CA 2x256 i,CI 2x256 i,CU 2x256 u,CF 2x256 f,HP 256 f,W0 256 f,pen 2x256 f,km2 2x256 f,kt 2x256 f,SC 2x256 f,
 RSi 256 b,RS 256 f,best 16 i,Jt 16 i,Jx 16 b,LJ 16 u,PX 272 b,FJ 256 b,WJ 256 b,NE 16 f,FI 16x32 i,FB 16x32 b,RT 512 b,SH 8x256 f,SCN 16x128 f,
 AI 16 i,PZ 2x16 i,FP 2x256 b,FQ 2x256 b,Y0 2x256 b,R16 256 f,NTW 16 f,SLf 16 f,SL 16 u,RL 16 u,Lc 4 f,y1 256 f,y2 256 f,
-sg 256 f,t2 256 f,CC 256 u,G 256 f,Yc 256 f,sti 256 f,WF 256 f,LI 16 i,Q 256 f,LU 16 u,ci 256 i,ca 256 i,LL 256 u,PW 13x256 b,YW 13x256 f,
-WS 13x256 b,LV 12x16 u,YT0 528 f,TT0 512 f,YT1 528 f,TT1 512 f,OT 512 f,OB 6x1024 b""".replace("\n", "").split(","):
+sg 256 f,t2 256 f,CC 256 u,G 256 f,Yc 256 f,sti 256 f,WF 256 f,y3 256 f,Q 256 f,LU 16 u,ci 256 i,ca 256 i,LL 256 u,PW 13x256 b,YW 13x256 f,
+WS 13x256 b,LV 12x16 u,PE 512 b,YT0 1040 f,TT0 512 f,YT1 1040 f,TT1 512 f,OT 512 f,OB 6x1024 b""".replace("\n", "").split(","):
     _n, _s, _d = _w.split()
     SCRATCH[_n] = ("sbuf", [128] + [int(z) for z in _s.split("x")], DTN[_d])
 for _b in range(8):
     SCRATCH["ps%d" % _b] = ("psum", [128, 512], "float32")
-SEMAPHORES = (["cv", "cs", "ct", "cg", "dwt", "dkm", "dth", "le", "e1", "e2", "e3"] + ["d%s%d" % (x, q) for x in "xy" for q in range(4)]
-              + ["%s%d_%d" % (x, t, k) for x in "al" for t in range(ROUNDS) for k in (1, 2, 3)])
+SEMAPHORES = (["cv", "cs", "ct", "cg", "dwt", "dkm", "dth", "e_l1", "e_1", "e_2", "e_3"] + ["d%s%d" % (x, q) for x in "xy" for q in range(4)]
+              + ["m%d_%s%d" % (t, x, k) for t in range(ROUNDS) for k in (1, 2, 3) for x in ("", "l")])
 P24 = 16777216.0
 ROUNDER = 12582912.0
 HOLD = 8192.0
-STEPS = 12
+LAST = 9
+STEPS = LAST + 2
 COPY, ABS = AF.Copy, AF.Abs
 SHR, AND = A.arith_shift_right, A.bitwise_and
 NUM = {n: np.arange(int(np.prod(s[1][1:]))).reshape(s[1][1:]) for n, s in SCRATCH.items()}
-OPT = dict(split=128, last=32, lag1=3, lag2=8, cut=7)
+OPT = dict(split=(124, 128), last=32, lag1=2, lag2=8, cut=7, lt=4, help=(8, 16), sp=3)
 
 
 def rank_program(g, core, T, topo):
@@ -135,11 +136,12 @@ def rank_program(g, core, T, topo):
     def iota(out, pat, base=0, cm=0):
         run("g", lambda: g.iota(out[0], pat, base, cm, allow_small_or_imprecise_dtypes=True), out, ())
 
-    def mm(out, prs):
+    def mm(out, prs, start=True, stop=True, each=False):
         def call():
             r = None
             for n, p in enumerate(prs):
-                r = te.matmul((p[2] if len(p) > 2 else out)[0], p[0][0], p[1][0], n == 0, n == len(prs) - 1)
+                r = te.matmul((p[2] if len(p) > 2 else out)[0], p[0][0], p[1][0], each or start and n == 0,
+                              each or stop and n == len(prs) - 1)
             return r
         run("t", call, out, [x for p in prs for x in p[:2]])
 
@@ -185,8 +187,10 @@ def rank_program(g, core, T, topo):
     iota(a("FP"), [[0, 512]])
     iota(a("PX", (256, 272)), [[0, 16]], 512)
     iota(a("CJ"), [[16, 256]], 15)
+    iota(a("PE", (256, 384)), [[2, 128]], 258)
+    iota(a("PE", (384, 512)), [[4, 128]], 516)
     for t in range(ROUNDS):
-        for n, w in (("YT", 528), ("TT", 512)):
+        for n, w in (("YT", 1040), ("TT", 512)):
             iota(a(n + str(t)), [[0, w]])
     ms(a("CTb", (), (21, 32)), 0.0)
     for f, c in ((8, 4096.0), (9, 1048576.0), (10, 1.0), (11, P24), (20, 16.0)):
@@ -204,7 +208,8 @@ def rank_program(g, core, T, topo):
     lin(pd(15), pf(0), 1.0, 1.0)
     lin(pd(2), pf(4), -1.0, 1.0)
     lin(pd(3), pf(0), -1.0, 0.0)
-    lin(pd(4), pf(0), -1.0, 4096.0 + ROUNDER)
+    lin(pd(4), pf(0), 1.0, -4096.0 - ROUNDER)
+    lin(pd(5), pf(0), 128.0, 0.0)
     for f in range(5):
         ts(a("CB", (), f), a("jn"), f, SHR, 1, AND)
     ts(a("IDf"), a("IC", (0, 128)), pf(6), A.is_equal)
@@ -225,33 +230,33 @@ def rank_program(g, core, T, topo):
              lambda: tr(a("CTT"), a("CTb")),
              lambda: tt(a("WD"), a("FJ"), a("WJ"), A.max),
              lambda: ts(a("SE"), a("GM"), pf(1), A.is_equal, q15, A.mult),
-             lambda: ts(a("T4"), a("thi"), 4096.0, A.mult)]
-
-    def late():
-        lin(a("iT"), a("BNeb"), 1.0, pf(2))
-        lin(a("BNbe"), a("BNbe"), 1.0, pf(2))
-        for n in range(4):
-            lin(a("CL", (), (32 * n, 32 * n + 32)), a("CTT"), pd(8 + n), 0.0, COPY)
-            if n == 0:
-                ac(a("FB", (), 20), a("iT"))
-                lin(a("iT1"), a("iT"), 1.0, 1.0)
-        lin(pd(12), q15, 1.0 - 1.0 / HOLD, 1.0 / HOLD)
-        lin(pd(14), q15, 1.0 - HOLD, HOLD)
-        lin(a("CTR"), a("BNbe"), 16.0, float(4080 * 4096 + 15))
-        lin(a("Zx0"), a("Zx"), pd(2), 0.0, COPY)
-        lin(a("Zx1"), a("Zx"), pf(4), 0.0, COPY)
-        lin(a("RP"), a("RSi"), 1.0, 0.0, AF.Sign)
-        lin(a("IK8"), a("IK8"), 1.0 / 256, 0.0)
-        lin(a("PC"), a("PC"), 1.0, pf(0))
+             lambda: ts(a("T4", (0, 2)), a("thi"), 4096.0, A.mult)]
+    late = ([lambda: lin(a("T4", (2, 4)), a("T4", (0, 2)), -2 * P24, 2 * P24),
+             lambda: lin(a("iT"), a("BNeb"), 1.0, pf(2)),
+             lambda: lin(a("BNbe"), a("BNbe"), 1.0, pf(2))]
+            + [lambda n=n: lin(a("CL", (), (32 * n, 32 * n + 32)), a("CTT"), pd(8 + n), 0.0, COPY) for n in range(4)]
+            + [lambda: ac(a("FB", (), 20), a("iT")),
+               lambda: lin(a("iT1"), a("iT"), 1.0, 1.0),
+               lambda: lin(pd(12), q15, 1.0 - 1.0 / HOLD, 1.0 / HOLD),
+               lambda: lin(pd(14), q15, 1.0 - HOLD, HOLD),
+               lambda: lin(a("CTR"), a("BNbe"), 16.0, float(4080 * 4096 + 15)),
+               lambda: lin(a("Zx0"), a("Zx"), pd(2), 0.0, COPY),
+               lambda: lin(a("Zx1"), a("Zx"), pf(4), 0.0, COPY),
+               lambda: lin(a("RP"), a("RSi"), 1.0, 0.0, AF.Sign)])
 
     def later():
+        lin(a("IK8"), a("IK8"), 1.0 / 256, 0.0)
+        lin(a("PC"), a("PC"), 1.0, pf(0))
         lin(pd(20), pd(14), 257.0, 0.0)
         lin(a("IDfn"), a("IDf"), -1.0, 0.0)
         lin(a("SEn"), a("SE"), -1.0, 0.0)
         lin(pd(13), pd(12), -0.125, 0.0)
         lin(a("iW"), a("PC", (0, 16)), pd(14), pd(14))
         lin(a("W256"), a("PC", (0, 16)), pd(14), pd(20))
-    lo, col15 = (0, 256), (15, 256, 16)
+    lo, col15, halves = (0, 256), (15, 256, 16), ((0, 128), (128, 256))
+
+    def quarter(n):
+        return (64 * n, 64 * n + 64)
 
     def to(k):
         return T.cores[(rank + k) % 4]
@@ -263,9 +268,27 @@ def rank_program(g, core, T, topo):
             es = [x for x in es if x not in topo.engines(src, T.cores[(T.rank_of(src) + 1) % 4])]
         return es
 
-    def share(src, k):
-        es = engines(src, k)
-        return es if k == 2 else es[len(es) // 2 * (k // 2):][:len(es) // 2]
+    def way(src, dst):
+        return 2 if topo.chip(src) == topo.chip(dst) else int(topo.die(src) == topo.die(dst))
+
+    def send(ks, name, src, dst):
+        def share(c, k):
+            alike = {m: [x for x in ks if engines(c, x) == engines(c, m)] for m in ks}
+            n = min(len(engines(c, m)) // len(alike[m]) for m in ks)
+            return engines(c, k)[n * alike[k].index(k):][:n]
+        need("g", [x for k in ks for x in src(k)[1]], [])
+        ws = [(topo.addr(to(k)), sum(1 << x for x in share(core, k)), T.sem["%s_%d" % (name, k)], src(k)[0]) for k in ks]
+        left = "%s_l%d" % (name, ks[0])
+        if len(ks) == 1:
+            ad, mask, sem, x = ws[0]
+            g.remote_dma(dst(rank)[0], x, sem, T.sem[left], ad[1], ad[0], mask)
+        else:
+            g.remote_dma_fused([RemoteDMATransfer(dst_ids=[DstId(rid=ad[0], pnc=ad[1])], dma_engine_mask=mask, remote_sem=sem,
+                                                  src=x, dst=dst(rank)[0]) for ad, mask, sem, x in ws], local_sem=T.sem[left])
+        total[left] = sum(len(share(core, k)) for k in ks)
+        for k in ks:
+            fr = (rank - k) % 4
+            done("", "%s_%d" % (name, k), len(share(T.cores[fr], k)), [], dst(fr)[1])
 
     for t in range(ROUNDS):
         xn, nx = "X%d" % t, "X%d" % (t + 1)
@@ -273,9 +296,6 @@ def rank_program(g, core, T, topo):
 
         def last(i):
             return a("LC", i) if t else a(xn, (16 * i[0] + 15, 16 * i[1], 16))
-
-        def quarter(n):
-            return (64 * n, 64 * n + 64)
 
         def hashes(i):
             j = (256 + i[0], 256 + i[1])
@@ -293,30 +313,30 @@ def rank_program(g, core, T, topo):
                     lambda: cp(a("CU", 0, i), a("CI", 0, i)),
                     lambda: cp(a("CU", 1, i), a("CI", 1, i))]
 
-        def repeats(i):
-            return [lambda: ac(a("R8", i, 0), last(i)),
-                    lambda: ac(a("R8", i, 1), last(i)),
-                    lambda: ac(a("R8", i, (2, 4)), a("R8", i, (0, 2))),
-                    lambda: ac(a("R8", i, (4, 8)), a("R8", i, (0, 4))),
-                    lambda: ac(a("XR", (16 * i[0], 16 * i[1], 2)), a("R8", i, ()))]
-
-        def odd(i):
-            cp(a("XR", (16 * i[0] + 1, 16 * i[1], 2)), a("R8", i, ()))
+        def repeats(n):
+            for j in range(2):
+                i, b = (64 * n + 32 * j, 64 * n + 32 * j + 32), "ps%d" % ((2 * n + 2) % 6 + j)
+                mm(a(b), [(a("ID"), last(i), a(b, (x, 512, 16))) for x in range(16)], each=True)
+                ac(a("XR", (16 * i[0], 16 * i[1])), a(b))
         twice0 = [lambda x=x: ac(a("R2", (x, 128, 2)), last(quarter(0))) for x in range(2)]
         if t == 0:
-            weave(repeats(quarter(1)), twice0)
             lin(a("RS"), a("RSi"), -2 * P24, 2 * P24, AF.Relu)
-            weave(repeats(quarter(2)), repeats(quarter(3)))
-            weave(spare)
-            rest = hashes((128, 256))
-            weave(hashes(quarter(0)), [None] * OPT["lag1"] + hashes(quarter(1)), [None] * OPT["lag2"] + rest[:OPT["cut"]])
+            weave(twice0)
+            weave(spare[:OPT["sp"]])
+            rest = hashes(halves[1])
+            weave(hashes(quarter(0)), spare[OPT["sp"]:], [None] * OPT["lag1"] + hashes(quarter(1)), [None] * OPT["lag2"] + rest[:OPT["cut"]],
+                  [None] * OPT["lag1"] + [lambda: repeats(1)], [None] * OPT["lag2"] + [lambda: repeats(2)])
             rest = rest[OPT["cut"]:]
         else:
-            weave(repeats(quarter(1)), repeats((128, 256)), twice0)
-            ac(a("XR", (16 * 128 + 1, 4096, 2)), a("R8", (128, 256), ()))
-            weave(hashes((0, 128)), hashes((128, 256)))
+            hs = [hashes(c) for c in halves]
+            weave(*[x[:1] for x in hs])
+            weave(twice0)
+            for n in range(1, 4):
+                repeats(n)
+            weave(*[x[1:] for x in hs])
+            for h in range(2):
+                cp(a("CF", h, ()), a("CI", h, ()))
             rest = []
-        odd(quarter(1))
 
         def span(h, i):
             return (4096 * h + 16 * i[0], 4096 * h + 16 * i[1])
@@ -324,10 +344,13 @@ def rank_program(g, core, T, topo):
         def keys(h, i):
             return a("ps%d" % (2 * h + 2 if i[0] == 192 else h), i)
 
+        def column(n, h):
+            return [(a("IDf"), a("CF", h, quarter(n)))]
+
         def sums(n, h):
-            i = quarter(n)
-            d = span(h, i)
-            mm(keys(h, i), [(a("IDf"), a("CF", h, i))] + [(a("Zd", (15 - p, 143 - p)), a("AD", (d[0] + p, d[1], 16))) for p in range(16)])
+            d = span(h, quarter(n))
+            mm(keys(h, quarter(n)), (column(n, h) if n < 3 else [])
+               + [(a("Zd", (15 - p, 143 - p)), a("AD", (d[0] + p, d[1], 16))) for p in range(16)], start=n < 3)
 
         def less(h, i):
             tt(a("DF", span(h, i)), ind(win, a("CU", h, i)), a("XR", (16 * i[0], 16 * i[1])), A.subtract)
@@ -336,7 +359,10 @@ def rank_program(g, core, T, topo):
             ac(a("AD", span(h, i)), a("DF", span(h, i)), ABS)
 
         def plain(h):
-            ac(a("DF", span(h, quarter(0))), ind(win, a("CU", h, quarter(0))))
+            x = 64 - OPT["help"][t] * h
+            if x < 64:
+                cp(a("DF", span(h, (x, 64))), ind(win, a("CU", h, (x, 64))))
+            ac(a("DF", span(h, (0, x))), ind(win, a("CU", h, (0, x))))
 
         def plain_less(h, banks):
             for j, b in enumerate(banks):
@@ -351,25 +377,29 @@ def rank_program(g, core, T, topo):
             sums(0, h)
 
         def bests(h, i):
-            return [lambda: ts(a("pen", h, i), keys(h, i), a("T4", (h, h + 1)), A.is_ge, 2 * P24, A.mult),
+            return [lambda: ts(a("pen", h, i), keys(h, i), a("T4", (h, h + 1)), A.is_ge, 2 * P24, A.mult) if i[0] < 192 else
+                    lin(a("pen", h, i), keys(h, i), 2 * P24, a("T4", (2 + h, 3 + h)), AF.Relu),
                     lambda: tt(a("km2", h, i), keys(h, i), a("pen", h, i), A.max),
                     lambda: tr(a("kt", h, i), a("km2", h, i)),
                     lambda: scan(a("SC", h, i), a("RS", i), a("kt", h, i), A.max, A.min)]
         q1, q2, q3 = quarter(1), quarter(2), quarter(3)
         l0 = 256 - OPT["last"]
         plain(0)
+        if t == 0:
+            repeats(3)
         plain_less(0, ("ps4", "ps5"))
         if rest:
-            weave([lambda x=x: less(0, (x, x + 16)) for x in range(64, 128, 16)], rest[0::2], rest[1::2])
-            odd((128, 256))
+            weave([lambda c=c: less(0, c) for c in ((64, 80), (80, 96), (96, 128))], rest[0::2], rest[1::2])
         else:
             less(0, (64, 96))
             less(0, (96, 128))
-        cp(a("CF", 0, ()), a("CI", 0, ()))
+        if t == 0:
+            cp(a("CF", 0, ()), a("CI", 0, ()))
         absolute(0, (64, 96))
         absolute(0, (96, 128))
         less(1, q1)
-        cp(a("CF", 1, ()), a("CI", 1, ()))
+        if t == 0:
+            cp(a("CF", 1, ()), a("CI", 1, ()))
         sums(1, 0)
         plain_end(0, ("ps4", "ps5"))
         plain(1)
@@ -380,6 +410,8 @@ def rank_program(g, core, T, topo):
         less(1, q2)
         absolute(0, q2)
         plain_end(1, ("ps3", "ps7"))
+        for h in range(2):
+            mm(keys(h, q3), column(3, h), stop=False)
         sums(2, 0)
         less(0, q3)
         absolute(1, q2)
@@ -392,11 +424,17 @@ def rank_program(g, core, T, topo):
         absolute(1, (l0, 256))
         sums(3, 1)
         if t == 0:
-            late()
+            weave(late[:OPT["lt"]])
         weave(bests(0, (0, 192)), bests(1, (0, 192)))
-        halves = ((0, 128), (128, 256))
-        weave(bests(0, q3), bests(1, q3), [lambda c=c: ts(a("HP", c), a("U", c), 127, AND) for c in halves]
-              + [lambda c=c: ts(a("W0", c), a("HP", c), pd(3), A.mult, pd(4), A.add) for c in halves])
+        weave(bests(0, q3), bests(1, q3))
+        if t == 0:
+            weave(late[OPT["lt"]:])
+        mm(a("ps6", lo), [(a("WH"), last(lo))])
+        lin(a("y1"), a("ps6", lo), 1.0 / 128, 1.0 / 256 - 0.5)
+        lin(a("W0"), a("ps6", lo), pd(3), 0.0, COPY)
+        lin(a("y2"), a("y1"), 1.0, ROUNDER)
+        lin(a("y1"), a("y2"), 1.0, -ROUNDER)
+        lin(a("HP"), a("y1"), pd(5), 0.0, COPY)
         for e in range(2):
             c = (16 * e + 15, 256, 32)
             tt(a("best", (8 * e, 8 * e + 8)), a("SC", 0, c), a("SC", 1, c), A.min)
@@ -409,29 +447,26 @@ def rank_program(g, core, T, topo):
         ts(a("FI", (), 9), be, 20, SHR, 31, AND)
         ts(a("FI", (), 10), be, 1, SHR, 7, AND)
         ts(a("FB", (), (12, 20)), a("FI", (), (0, 8)), -1.0, A.mult, 1.0, A.add)
-        tt(a("Jx"), a("Jt"), a("iT1"), A.max)
         cp(a("FB", (), (0, 12)), a("FI", (), (0, 12)))
-        ms(a("ps6", (0, 1)), 0.0)
-        tr(a("RT"), a("FB"))
-        banks = ["ps%d" % b for b in (0, 1, 2, 3, 4, 5, 7)]
-        bk = {0: (banks[0], 0), 1: (banks[0], 64)}
-        bk.update({b: (banks[b - 1], 0) for b in range(2, 8)})
-        for b in (0, 1, 7, 2, 6, 3, 5, 4):
-            w, (ps, o) = 32 * b + 32, bk[b]
-            for e in range(2):
-                mm(a(ps, (o + w * e, o + w * e + w)), [(a("CL", b, ()), a("RT", (256 * e, 256 * e + w)))])
-            if b > 3:
+        for e in range(2):
+            tr(a("RT", (256 * e, 256 * e + 256)), a("FB", (8 * e, 8 * e + 8), ()))
+        tt(a("Jx"), a("Jt"), a("iT1"), A.max)
+        def pieces(bs):
+            for b, e in [(0, 0), (1, 0), (0, 1), (1, 1)] + [(b, e) for b in bs for e in range(2)]:
+                w = 32 * b + 32
+                yield (b, e, "ps%d" % e, 32 * b, w) if b < 2 else (b, e, "ps%d" % b, w * e, w)
+        for b, e, ps, o, w in pieces((2, 7, 3, 6, 5, 4)):
+            mm(a(ps, (o, o + w)), [(a("CL", b, ()), a("RT", (256 * e, 256 * e + w)))])
+            if b > 3 and e:
                 ac(a("SH", b, (0, w)), a(ps, (1, 2 * w, 2)))
         if t == 0:
             later()
-        for b in (0, 1, 2, 7, 3, 6, 5, 4):
-            w, (ps, o) = 32 * b + 32, bk[b]
-            for e in range(2):
-                if b > 3:
-                    scan(a("SCN", 2 * b + e, (128 - w // 2, 128)), a(ps, (w * e, w * e + w, 2)),
-                         a("SH", b, (w // 2 * e, w // 2 * (e + 1))), A.min, A.min, 2 * P24)
-                else:
-                    red(a("SCN", 2 * b + e, (127, 128)), a(ps, (o + w * e, o + w * e + w)), A.min)
+        for b, e, ps, o, w in pieces((2, 3, 7, 6, 5, 4)):
+            if b > 3:
+                scan(a("SCN", 2 * b + e, (128 - w // 2, 128)), a(ps, (o, o + w, 2)),
+                     a("SH", b, (w // 2 * e, w // 2 * (e + 1))), A.min, A.min, 2 * P24)
+            else:
+                red(a("SCN", 2 * b + e, (127, 128)), a(ps, (o, o + w)), A.min)
         wrap("ps0", lambda e: a("Jx", (8 * e, 8 * e + 8)))
         tt(a("AI"), a("SCN", (), 127), a("CTR"), A.min)
         cp(a("LJ"), a("ps0", (0, 16)))
@@ -448,127 +483,116 @@ def rank_program(g, core, T, topo):
             tr(a("Y0", n, ()), a("FQ", 1, ()))
 
         y0 = a("Y0", 0, ())
-        terms = ((a("W0"), 0), (a("y2"), 1), (a("t2"), 0))
+        terms = (("W0", 0), ("HP", 0), ("y3", 1), ("t2", 0))
 
         def places():
-            mm(a("ps2", lo), [(a("IDfn" if n else "IDf"), x) for x, n in terms])
-            if t == 0:
+            mm(a("ps2", lo), [(a("IDf"), a("t2"))], start=False)
+            if t + 1 < ROUNDS:
                 for k in range(4):
-                    mm(a("ps5", (64 * k, 64 * k + 64)),
-                       [(a("SEn" if n else "SE"), a(x, (k, 256, 4))) for x, n in (("W0", 0), ("y2", 1), ("t2", 0))])
+                    mm(a("ps0", quarter(k)), [(a("SEn" if n else "SE"), a(x, (k, 256, 4))) for x, n in terms])
         by_scalar = [
-            lambda: run("s", lambda: s.activation(T.sg[:], y0[0], ABS, bias=-8.0, accum_out=lc(0)[0]),
-                        (None, a("sg")[1] + lc(0)[1]), (y0,)),
-            lambda: lin(lc(1), lc(0), 1.0, 2048.0),
-            lambda: [lin(a("y1"), a("IK8"), lc(1), 1.0 / 512 - 0.5), lin(lc(2), lc(0), -1.0, 2048.5)],
-            lambda: [lin(a("y2"), a("y1"), 1.0, ROUNDER), lin(lc(3), lc(0), 0.5, 1024.0),
-                     mm(a("ps1", lo), [(a("IDf"), a("W0")), (a("IDfn"), a("y2"))])],
             lambda: ac(a("FJ", (0, 128)), ind(a("PX", (0, 272)), a("LJ", (0, 8)))),
             lambda: ac(a("FJ", (128, 256)), ind(a("PX", (0, 272)), a("LJ", (8, 16)))),
-            lambda: lin(a("sg"), a("ps1", lo), -1.0, lc(2), AF.Sign),
-            lambda: [lin(a("t2"), a("sg"), lc(3), lc(3)), places()],
+            lambda: run("s", lambda: s.activation(T.sg[:], y0[0], ABS, bias=-8.0, accum_out=lc(0)[0]),
+                        (None, a("sg")[1] + lc(0)[1]), (y0,)),
+            lambda: [lin(lc(1), lc(0), 1.0, 2048.0), lin(lc(2), lc(0), -1.0, 2048.5), lin(lc(3), lc(0), 0.5, 1024.0)],
+            lambda: lin(a("y1"), a("IK8"), lc(1), 1.0 / 512 - 0.5),
+            lambda: lin(a("y2"), a("y1"), 1.0, ROUNDER),
+            lambda: [lin(a("y3"), a("y2"), 1.0, pd(4))]
+            + [mm(a(b, lo), [(a("IDfn" if n else "IDf"), a(x)) for x, n in terms[:3]], stop=b == "ps1") for b in ("ps1", "ps2")],
             lambda: lin(a("R16"), y0, -2.0, 16.0, AF.Relu),
-            lambda: lin(a("ps4", (0, 512, 2)), a("PC"), 4097.0, 4096.0),
-            lambda: lin(a("ps4", (1, 512, 2)), a("PC"), 4097.0, 4096.0)]
-        by_vector = {7: lambda: hold(a("WJ"), a("FJ")),
-                     8: lambda: tt(a("NE"), a("WJ", col15), a("iW"), A.is_equal),
-                     9: lambda: tt(a("NTW"), a("NE"), a("W256"), A.mult)}
+            lambda: lin(a("ps4", (0, 512, 2)), a("PC"), 4097.0, 4096.0)]
+        by_vector = {4: lambda: hold(a("WJ"), a("FJ")),
+                     5: lambda: tt(a("NE"), a("WJ", col15), a("iW"), A.is_equal),
+                     6: lambda: tt(a("NTW"), a("NE"), a("W256"), A.mult)}
 
-        def summed(n, m, c):
-            o = 2 * n - 3 - m
-            tt(a("YW", n, c), ind(a("YW", o, ()) if o > 0 else y0, a("LV", m, (c[0] // 16, c[1] // 16))),
-               a("YW", m, c) if m else a("Y0", 1, c), A.add)
-        for n in range(1, STEPS + 1):
+        def summed(n, m, rest, c):
+            tt(a("YW", n, c), ind(rest, a("LV", m, (c[0] // 16, c[1] // 16))), a("YW", m, c) if m else a("Y0", 1, c), A.add)
+        for n in range(1, LAST + 1):
             ac(a("PW", n, ()), ind(a("PW", n - 1, ()) if n > 1 else a("PX", lo), a("LV", max(n - 2, 0), ())))
-            if n < STEPS:
-                by_scalar[n - 1]()
-            if n < STEPS - 1:
-                if n == 1:
-                    summed(n, n - 1, lo)
-                hold(a("WS", n, ()), a("PW", n, ()))
-                if n > 1:
-                    summed(n, n - 1, (0, 128))
-                ts(a("LV", n, ()), a("WS", n, col15), pd(12), A.mult, -1.0, A.add)
-                if n > 1:
-                    summed(n, n - 1, (128, 256))
-                if n in by_vector:
-                    by_vector[n]()
-            else:
-                summed(n, STEPS - 2, lo)
+            if n > 1:
+                by_scalar[n - 2]()
+            rest = a("YW", n - 2, ()) if n > 2 else y0
+            if n == 1:
+                summed(n, 0, rest, lo)
+            hold(a("WS", n, ()), a("PW", n, ()))
+            if n > 1:
+                summed(n, n - 1, rest, halves[0])
+            ts(a("LV", n, ()), a("WS", n, col15), pd(12), A.mult, -1.0, A.add)
+            if n == LAST:
+                tt(a("SLf"), a("WS", n, col15), a("NTW"), A.max)
+            if n > 1:
+                summed(n, n - 1, rest, halves[1])
+            if n in by_vector:
+                by_vector[n]()
+        ts(a("SL"), a("SLf"), pd(12), A.mult, -1.0, A.add)
+        ac(a("PW", LAST + 1, ()), ind(a("PW", LAST, ()), a("LV", LAST - 1, ())))
+        by_scalar[LAST - 1]()
+        cp(a("YW", 0, ()), a("YW", LAST, ()))
+        ac(a("PE", lo), ind(a("PW", LAST + 1, ()), a("LV", LAST, ())))
+        summed(LAST + 1, LAST, a("YW", 0, ()), lo)
+        ac(a("PW", 0, ()), ind(a("PE", (0, 512)), a("SL")))
+        ac(a("PW", STEPS, ()), ind(a("PE", lo), a("LV", LAST, ())))
+        lin(a("sg"), a("ps1", lo), -1.0, lc(2), AF.Sign)
+        hold(a("WS", 0, ()), a("PW", 0, ()))
+        summed(STEPS, LAST, a("YW", LAST + 1, ()), lo)
         YT, TT = ["%s%d" % (x, t) for x in ("YT", "TT")]
         yf, root = a("YW", STEPS, ()), a("WS", STEPS, col15)
+        lin(a("t2"), a("sg"), lc(3), lc(3))
+        places()
         lin(a("Yc"), yf, -1.0, 4097.0)
+        lin(a("ps4", (1, 512, 2)), a("PC"), 4097.0, 4096.0)
+        ts(a("LU"), a("WS", 0, col15), pd(12), A.mult, -1.0, A.add)
         hold(a("WS", STEPS, ()), a("PW", STEPS, ()))
-        kids = [lambda k=k: ts(a("CC", (64 * k, 64 * k + 64)), a("ps2", (k, 256, 4)), -1.0, A.add) for k in range(4)]
-        kids[0]()
-        tt(a("SLf"), root, a("NTW"), A.max)
+        cp(ind(a(YT, (8, 1032)), a("LU")), yf)
         ts(a("RL"), root, pd(12), A.mult, -1.0, A.add)
-        kids[1]()
-        ts(a("SL"), a("SLf"), pd(12), A.mult, -1.0, A.add)
-        kids[2]()
-        kids[3]()
-        cp(ind(a(YT, (8, 520)), a("SL")), yf)
-        if t == 0:
-            hold(a("WL"), a("ps5", lo))
         scan(a("G"), a("R16"), a(YT, (7, 263)), A.add, A.add)
-        if t == 0:
-            ts(a("LE"), a("WL", col15), pd(12), A.mult, -1.0, A.add)
         tt(a("sti"), ind(a("G", lo), a("RL")), a("Yc"), A.subtract)
         lin(a("Q"), a("sti"), -4097.0, -4097.0)
+        lin(a("ps6", (0, 1)), pf(0), 0.0, 0.0)
+        kids = [lambda k=k: ts(a("CC", quarter(k)), a("ps2", (k, 256, 4)), -1.0, A.add) for k in range(4)]
+        weave(kids[:2])
         hold(a("WF"), a("sti"), A.min)
-        ts(a("LI"), a("WF", col15), pd(13), A.mult, -0.5625, A.add)
-        cp(a("LU"), a("LI"))
+        kids[2]()
+        ts(a("LU"), a("WF", col15), pd(13), A.mult, -0.5625, A.add)
+        kids[3]()
         tt(ind(a(TT, (0, 512)), a("LU")), a("Q"), a("CJ"), A.add)
-        parts = ((OPT["split"], 256), (0, OPT["split"]))
 
         def twice(c, x=None):
             return (2 * c[0], 2 * c[1]) if x is None else (2 * c[0] + x, 2 * c[1], 2)
-        for c in parts:
+        for c in halves[::-1]:
             tt(a("ps5", twice(c)), a(TT, twice(c)), a("ps4", twice(c)), A.is_le)
-        tt(a("OT", twice(parts[0])), a(TT, twice(parts[0])), a("ps5", twice(parts[0])), A.mult)
+        tt(a("OT", twice(halves[1])), a(TT, twice(halves[1])), a("ps5", twice(halves[1])), A.mult)
         scan(a("ps6", (1, 257)), a(TT, (0, 512, 2)), a(TT, (1, 512, 2)), A.max, A.max)
-        tt(a("OT", twice(parts[1])), a(TT, twice(parts[1])), a("ps5", twice(parts[1])), A.mult)
+        tt(a("OT", twice(halves[0])), a(TT, twice(halves[0])), a("ps5", twice(halves[0])), A.mult)
         for f in (lambda c: tt(a("ps7", c), a("ps6", c), a("OT", twice(c, 0)), A.max),
                   lambda c: tt(a("ps3", c), a("ps7", c), a("OT", twice(c, 1)), A.max),
                   lambda c: tt(a("ci", c), a("ps3", c), a("PC", c), A.subtract),
                   lambda c: ts(a("ca", c), a("ci", c), 4095, AND),
                   lambda c: cp(a("LL", c), a("ca", c))):
-            for c in parts:
-                f(c)
-        for f, c in zip((ac, cp), parts):
+            for n in (2, 3, 0, 1):
+                f(quarter(n))
+        if t + 1 < ROUNDS:
+            hold(a("WL"), a("ps0", lo))
+        for f, c in ((ac, (OPT["split"][t], 256)), (cp, (0, OPT["split"][t]))):
             f(a("XLD", (16 * c[0], 16 * c[1])), ind(win, a("LL", c)))
-        mine, laid = (1024 * rank, 1024 * rank + 1024), a("XLD", (0, 4096))
+        if t + 1 < ROUNDS:
+            ts(a("LE"), a("WL", col15), pd(12), A.mult, -1.0, A.add)
+        mine, laid = 1024 * rank, a("XLD", (0, 4096))
         if t + 1 < ROUNDS:
             cp(a("LO", (64, 192)), ind(laid, a("LE", (4, 12))))
             ac(a("LO", quarter(3)), ind(laid, a("LE", (12, 16))))
             ac(a("LC", quarter(rank)), ind(laid, a("LE", (0, 4))))
-            need("g", a("LO", (64, 256))[1], [])
-            g.remote_dma_fused([RemoteDMATransfer(dst_ids=[DstId(rid=topo.addr(to(k))[0], pnc=topo.addr(to(k))[1])],
-                                                  dma_engine_mask=sum(1 << x for x in share(core, k)), remote_sem=T.sem["e%d" % k],
-                                                  src=a("LO", quarter(k))[0], dst=a("LC", quarter(rank))[0]) for k in (1, 2, 3)],
-                               local_sem=T.sem.le)
-            total["le"] = sum(len(share(core, k)) for k in (1, 2, 3))
-            for k in (1, 2, 3):
-                fr = (rank - k) % 4
-                done("", "e%d" % k, len(share(T.cores[fr], k)), [], a("LC", quarter(fr))[1])
-        for k in (1, 3, 2, 0):
-            for f, c0 in ((cp, 0), (ac, 512)):
-                out = a("OB", 3 * t + k - 1, (c0, c0 + 512)) if k else a(nx, (mine[0] + c0, mine[0] + c0 + 512))
-                f(out, ind(laid, a("CC", (64 * k + c0 // 16, 64 * k + c0 // 16 + 32))))
-
-        for k in (1, 3, 2):
-            rid, pid, _ = topo.addr(to(k))
-            es = engines(core, k)
-            ob = a("OB", 3 * t + k - 1, ())
-            need("g", ob[1], [])
-            g.remote_dma(a(nx, mine)[0], ob[0], T.sem["a%d_%d" % (t, k)], T.sem["l%d_%d" % (t, k)], pid, rid, sum(1 << x for x in es))
-            total["l%d_%d" % (t, k)] = len(es)
-        for k in (1, 2, 3):
-            fr = (rank - k) % 4
-            done("", "a%d_%d" % (t, k), len(engines(T.cores[fr], k)), [], a(nx, (1024 * fr, 1024 * fr + 1024))[1])
-    for n, k in enumerate((0, 1, 2, 3)):
-        c = (1024 * ((rank - k) % 4), 1024 * ((rank - k) % 4) + 1024)
-        dma("ys"[n % 2], a("y", c), a("X2", c), "dy%d" % n)
-    for sm in sorted(total):
+            send((1, 2, 3), "e", lambda k: a("LO", quarter(k)), lambda r: a("LC", quarter(r)))
+        for k in sorted((1, 2, 3), key=lambda k: way(core, to(k))) + [0]:
+            for f, b in ((cp, 0), (ac, 512)):
+                out = a("OB", 3 * t + k - 1, (b, b + 512)) if k else a(nx, (mine + b, mine + b + 512))
+                f(out, ind(laid, a("CC", (64 * k + b // 16, 64 * k + b // 16 + 32))))
+            if k:
+                send((k,), "m%d" % t, lambda k: a("OB", 3 * t + k - 1, ()), lambda r: a(nx, (1024 * r, 1024 * r + 1024)))
+    first, second, near = sorted(((rank - k) % 4 for k in (1, 2, 3)), key=lambda r: way(T.cores[r], core))
+    for n, r in enumerate((rank, first, near, second)):
+        dma("ys"[n % 2], a("y", (1024 * r, 1024 * r + 1024)), a("X2", (1024 * r, 1024 * r + 1024)), "dy%d" % n)
+    for sm in sorted(total, key=lambda x: (x[:2] == "dy", x)):
         if know["g"].get(sm, 0) < total[sm]:
             g.wait_ge(T.sem[sm], total[sm])

@@ -5,15 +5,15 @@ from concourse.mybir import AluOpType as A, AxisListType, ActivationFunctionType
 ROUNDS = 2
 SCRATCH = {}
 DTN = {"b": "bfloat16", "f": "float32", "i": "int32", "u": "uint16"}
-for _w in """X0 4096 b,X1 4096 b,X2 4096 b,XLD 4096 b,XR 4096 b,R2 128 b,DF 8192 b,AD 8192 b,wti 1 i,kmi 4 i,thi 2 i,wtf 1 f,kmf 4 f,
-T4 4 f,MQ 16 f,Zx 144 b,ipart 1 i,IC 160 f,GM 128 f,IK8 256 f,PC 256 f,CJ 256 f,BNbe 16 f,BNeb 16 f,PI 8 i,PF 8 f,PD 24 f,WH 128 b,Zd 144 b,
-ID 128 b,IDn 128 b,IDf 128 f,IDfn 128 f,SE 128 f,SEn 128 f,Zx0 144 b,Zx1 144 b,jn 8 i,CB 8x8 i,CTb 8x32 b,CTT 8x32 b,CL 8x128 b,
-CTR 16 f,iT 16 f,iT1 16 f,iW 16 f,W256 16 f,WD 256 b,RP 256 b,LC 256 b,LO 256 b,WL 256 f,LE 16 u,
-U1 256 i,U 256 i,UU 256 i,UB 256 i,CA 2x256 i,CI 2x256 i,CU 2x256 u,CF 2x256 f,HP 256 f,W0 256 f,pen 2x256 f,km2 2x256 f,kt 2x256 f,SC 2x256 f,
-RSi 256 b,RS 256 f,best 16 i,Jt 16 i,Jx 16 b,LJ 16 u,PX 272 b,FJ 256 b,WJ 256 b,NE 16 f,FI 16x32 i,FB 16x32 b,RT 512 b,SH 8x256 f,SCN 16x128 f,
-AI 16 i,PZ 2x16 i,FP 2x256 b,FQ 2x256 b,Y0 2x256 b,R16 256 f,NTW 16 f,SLf 16 f,SL 16 u,RL 16 u,Lc 4 f,y1 256 f,y2 256 f,
-sg 256 f,t2 256 f,CC 256 u,G 256 f,Yc 256 f,sti 256 f,WF 256 f,y3 256 f,Q 256 f,LU 16 u,ci 256 i,ca 256 i,LL 256 u,PW 13x256 b,YW 13x256 f,
-WS 13x256 b,LV 12x16 u,PE 512 b,YT0 1040 f,TT0 512 f,YT1 1040 f,TT1 512 f,OT 512 f,OB 6x1024 b""".replace("\n", "").split(","):
+for _w in """X0 4096 b,X1 4096 b,X2 4096 b,XLD 4096 b,XR 4096 b,R2 512 b,DF 8192 b,AD 8192 b,wti 1 i,kmi 4 i,thi 2 i,wtf 1 f,kmf 4 f,
+T4 4 f,MQ 16 f,Zx 144 b,ipart 1 i,IC 160 f,GM 128 f,IK8 256 f,PC 256 f,CJ 256 f,PI 8 i,PF 8 f,PD 24 f,WH 128 b,Zj 160 b,
+ID 128 b,IDn 128 b,IDf 128 f,IDfn 128 f,SE 128 f,SEn 128 f,Zx0 144 b,Zx1 144 b,jn 8 i,CB 8x4 i,CTb 8x32 b,CTT 8x32 b,CL 8x128 b,
+PM 128 f,ONE 128 b,DT 4x128 b,TI 4 i,WK 3x16 b,G8 8 f,CTR 128 f,iT 2x16 f,BO 16 f,W256 16 f,WD 256 b,RP 256 b,LC 256 b,LO 256 b,WL 256 f,LE 16 u,
+U1 256 i,U 256 i,UU 256 i,UB 256 i,CA 2x256 i,CI 2x256 i,CU 2x256 u,CF 2x256 f,HP 256 f,W0 256 f,pen 4x128 b,SC 2x256 f,
+RSi 256 b,RS 128 f,best 16 i,Jt 16 i,LJ 16 u,PX 512 b,FJ 256 b,WJ 256 b,FI 16x8 i,FB 4x4x32 b,RT 512 b,SH 8x256 f,SCN 16x128 i,
+PZ 2x16 i,FP 2x256 b,FQ 2x256 b,Y0 768 b,C16 256 f,PB 256 f,NTW 16 f,SLf 24 f,NI 3x16 i,RL 16 u,Lc 4 f,y1 256 f,y2 256 f,
+sg 256 f,t2 256 f,CC 256 u,G 256 f,Yc 256 f,sti 256 f,WF 256 f,y3 256 f,Q 256 f,LU 3x16 u,ci 256 i,ca 256 i,LL 256 u,PW 3x512 b,ZW 4x512 f,
+RW 656 b,PT 512 b,ZT 480 f,YV 512 f,WS 3x256 b,LV 10x16 u,YT 4x528 f,TT0 512 f,TT1 512 f,OT 2x512 i,OB 6x1024 b""".replace("\n", "").split(","):
     _n, _s, _d = _w.split()
     SCRATCH[_n] = ("sbuf", [128] + [int(z) for z in _s.split("x")], DTN[_d])
 for _b in range(8):
@@ -22,13 +22,15 @@ SEMAPHORES = (["cv", "cs", "ct", "cg", "dwt", "dkm", "dth", "e_l1", "e_1", "e_2"
               + ["m%d_%s%d" % (t, x, k) for t in range(ROUNDS) for k in (1, 2, 3) for x in ("", "l")])
 P24 = 16777216.0
 ROUNDER = 12582912.0
-HOLD = 8192.0
-LAST = 9
-STEPS = LAST + 2
+HOLD = 65536.0
+BLOCK, STEPS = 32, 7
+WAKE, GATHER, SCATTER = 270, 1.4, 3.8
 COPY, ABS = AF.Copy, AF.Abs
 SHR, AND = A.arith_shift_right, A.bitwise_and
 NUM = {n: np.arange(int(np.prod(s[1][1:]))).reshape(s[1][1:]) for n, s in SCRATCH.items()}
-OPT = dict(split=(124, 128), last=32, lag1=2, lag2=8, cut=7, lt=4, help=(8, 16), sp=3)
+OPT = dict(split=(110, 110), help=(32, 32), passes=(None, 100, None), load=(3000, 3700, 4400, 5100), ahead=(3800, 3800, 3800),
+           bulk=(3000, 4800, 3500), store=4000, pieces=((0, 32), (32, 64)), first=(0, 1), lag=2, mid=(7, 7), late=2, behind=0, flags=(0, 2, 3, 4, 5, 6, 7, 9), parts=0, order=(0, 1, 2, 3),
+           tails=((0, 96), (96, 192)), skew=2, cols=((192, 256), (128, 192), (64, 128), (0, 64)))
 
 
 def rank_program(g, core, T, topo):
@@ -45,22 +47,21 @@ def rank_program(g, core, T, topo):
         return ap, [(n, NUM[n][ix].reshape(-1))]
 
     def ind(w, o):
-        return w[0].indirect(o[0]), w[1] + o[1]
+        return w[0].indirect(o[0]), w[1] + o[1], 16 * o[1][0][1].size
     eng = {"v": v, "s": s, "t": te, "g": g, "y": g.sync}
     cnt, total, know, snap, ev = {}, {}, {e: {} for e in eng}, {}, []
     wr = {n: np.full(NUM[n].size, -1) for n in NUM}
     rd = {n: {} for n in NUM}
     bank = {n: {} for n in NUM if n[:2] == "ps"}
 
-    def need(e, reads, writes):
+    def need(e, reads, writes, adds=False):
         ids, own = set(), "c" + e
         for w, lst in ((0, reads), (1, writes)):
             for n, c in lst:
-                ids.update(np.unique(wr[n][c]).tolist())
+                ids.update(i for i in np.unique(wr[n][c]).tolist() if not (w and adds and ev[i][0] == own))
                 if w:
-                    for sm, r in rd[n].items():
-                        if sm != own:
-                            ids.update(np.unique(r[c]).tolist())
+                    for r in rd[n].values():
+                        ids.update(np.unique(r[c]).tolist())
                 if n in bank:
                     ids.update(i for sm, i in bank[n].items() if sm != own)
         nd, kn = {}, know[e]
@@ -87,54 +88,151 @@ def rank_program(g, core, T, topo):
             if n in bank:
                 bank[n][sm] = len(ev) - 1
 
-    def run(e, call, out, ins):
-        reads = [z for x in ins if isinstance(x, tuple) for z in x[1]]
-        need(e, reads, out[1])
-        sm = "c" + e
-        cnt[sm] = cnt.get(sm, 0) + 1
-        call().then_inc(T.sem[sm], 1)
-        done(e, sm, cnt[sm], reads, out[1])
+    calls = []
 
-    def dma(e, out, in_, sm):
-        need(e, in_[1], out[1])
-        eng[e].dma_start(out[0], in_[0]).then_inc(T.sem[sm], 16)
-        done(e, sm, 16, in_[1], out[1])
+    def run(e, call, out, ins, cycles, adds=False):
+        reads = [z for x in ins if isinstance(x, tuple) for z in x[1]]
+
+        def issue():
+            need(e, reads, out[1], adds)
+            sm = "c" + e
+            cnt[sm] = cnt.get(sm, 0) + 1
+            call().then_inc(T.sem[sm], 1)
+            done(e, sm, cnt[sm], reads, out[1])
+        calls.append((e, issue, reads, out[1], cycles, cycles, [], adds))
+
+    def dma(e, out, in_, sm, cycles):
+        def issue():
+            need(e, in_[1], out[1])
+            eng[e].dma_start(out[0], in_[0]).then_inc(T.sem[sm], 16)
+            done(e, sm, 16, in_[1], out[1])
+        calls.append((e, issue, in_[1], out[1], 60, cycles, [], False))
+
+    def issue_all():
+        w = {n: np.full(NUM[n].size, -1) for n in NUM}
+        r = {n: [] for n in NUM}
+        pe, pre = {}, []
+        for i, (e, _, reads, writes, _, _, before, adds) in enumerate(calls):
+            p = {j: calls[j][4] - calls[j][5] for j in before}
+            for n, c in writes:
+                keep = []
+                for j, c2 in r[n]:
+                    m = np.isin(c2, c)
+                    if m.any():
+                        p[j] = WAKE
+                    if not m.all():
+                        keep.append((j, c2[~m]))
+                r[n] = keep
+                if e == "t":
+                    p.setdefault(pe.get(n, -1), 0)
+                    pe[n] = i
+                p.update({j: 0 if adds and calls[j][0] == e else WAKE for j in np.unique(w[n][c]).tolist()})
+            for n, c in reads:
+                p.update({j: WAKE for j in np.unique(w[n][c]).tolist()})
+                r[n].append((i, c))
+            for n, c in writes:
+                w[n][c] = i
+            p.pop(-1, None)
+            p.pop(i, None)
+            pre.append(p)
+        post = [{} for c in calls]
+        for i, p in enumerate(pre):
+            for j, d in p.items():
+                post[j][i] = d
+
+        def place(order, deps, back):
+            end, busy = {}, {}
+            for i in order:
+                e, hold, span = calls[i][0], calls[i][4], calls[i][5]
+                uses = [(e, span - hold if back else 0, hold, None)] + [(n, -WAKE, span + 2 * WAKE, e) for n in
+                                                                        {n for n, c in calls[i][2] + calls[i][3] if n in bank}]
+                at, moved = max([0.0] + [end[j] + d for j, d in deps[i].items()]), True
+                while moved:
+                    moved = False
+                    for n, off, length, own in uses:
+                        for x, y, who in busy.get(n, ()):
+                            if y > at + off + 0.01 and x < at + off + length and (own is None or who != own):
+                                at, moved = y - off, True
+                end[i] = at + span
+                for n, off, length, own in uses:
+                    busy.setdefault(n, []).append((at + off, at + off + length, e) if own is None else (at, at + span, e))
+            return end
+
+        def eager(order, wait):
+            rank_, left, ready = {i: n for n, i in enumerate(order)}, [len(p) for p in pre], [0.0] * len(calls)
+            end, free, held, some = {}, {}, {}, [i for i in order if not pre[i]]
+            banks = [{n for n, x in c[2] + c[3] if n in bank} for c in calls]
+            while some:
+                at = {i: max([free.get(calls[i][0], 0.0), ready[i]] + [held[n][1] + WAKE for n in banks[i] if n in held and held[n][0] != calls[i][0]])
+                      for i in some}
+                i = min(some, key=lambda i: at[i])
+                i = min((j for j in some if calls[j][0] == calls[i][0] and at[j] <= at[i] + wait), key=lambda j: rank_[j])
+                some.remove(i)
+                free[calls[i][0]], end[i] = at[i] + calls[i][4], at[i] + calls[i][5]
+                for n in banks[i]:
+                    held[n] = (calls[i][0], end[i])
+                for j, d in post[i].items():
+                    ready[j], left[j] = max(ready[j], end[i] + d), left[j] - 1
+                    if left[j] == 0:
+                        some.append(j)
+            return end
+        order, best = list(range(len(calls))), None
+        for n, wait in enumerate(OPT["passes"]):
+            end = place(order, pre, False) if wait is None else eager(order, wait)
+            if best is None or max(end.values()) < max(best.values()):
+                best = end
+            back = place(sorted(order, key=lambda i: (-end[i], -i)), post, True)
+            order = sorted(order, key=lambda i: (-back[i], i))
+        OPT["est"] = max(best.values())
+        for i in sorted(order, key=lambda i: (best[i] - calls[i][5], i)):
+            calls[i][1]()
 
     def z(x):
         return x[0] if isinstance(x, tuple) else x
 
+    def size(out, x, rate, fixed=60):
+        if len(out) > 2:
+            return fixed + SCATTER * out[2]
+        if len(x) > 2:
+            return fixed + GATHER * x[2]
+        return max(64, rate * x[1][0][1].size)
+
+    def fast(*xs):
+        return 0.5 if all(SCRATCH[x[1][0][0]][2] in ("bfloat16", "uint16") for x in xs) else 1
+
     def ts(out, x, s1, o0, s2=None, o1=None):
         if o1 is None:
-            run("v", lambda: v.tensor_scalar(out[0], x[0], z(s1), None, o0), out, (x, s1))
+            run("v", lambda: v.tensor_scalar(out[0], x[0], z(s1), None, o0), out, (x, s1), size(out, x, fast(out, x)))
         else:
-            run("v", lambda: v.tensor_scalar(out[0], x[0], z(s1), z(s2), o0, o1), out, (x, s1, s2))
+            run("v", lambda: v.tensor_scalar(out[0], x[0], z(s1), z(s2), o0, o1), out, (x, s1, s2), size(out, x, fast(out, x)))
 
     def tt(out, x, y, o):
-        run("v", lambda: v.tensor_tensor(out[0], x[0], y[0], o), out, (x, y))
+        run("v", lambda: v.tensor_tensor(out[0], x[0], y[0], o), out, (x, y),
+            size(out, x, 1 if x[1][0][0] in bank or y[1][0][0] in bank else 2))
 
     def cp(out, x):
-        run("v", lambda: v.tensor_copy(out[0], x[0]), out, (x,))
+        run("v", lambda: v.tensor_copy(out[0], x[0]), out, (x,), size(out, x, fast(out, x)))
 
     def ac(out, x, f=COPY):
-        run("s", lambda: s.activation(out[0], x[0], f), out, (x,))
+        run("s", lambda: s.activation(out[0], x[0], f), out, (x,), size(out, x, 1, 78))
 
     def lin(out, x, scale, bias, f=AF.Identity):
-        run("s", lambda: s.activation(out[0], x[0], f, bias=z(bias), scale=z(scale)), out, (x, bias, scale))
+        run("s", lambda: s.activation(out[0], x[0], f, bias=z(bias), scale=z(scale)), out, (x, bias, scale), size(out, x, 1, 78))
 
     def tr(out, x):
-        run("v", lambda: v.transpose(out[0], x[0]), out, (x,))
+        run("v", lambda: v.transpose(out[0], x[0]), out, (x,), size(out, x, fast(x)))
 
     def ms(out, c):
-        run("v", lambda: v.memset(out[0], c), out, ())
+        run("v", lambda: v.memset(out[0], c), out, (), size(out, out, fast(out)))
 
     def red(out, x, o):
-        run("v", lambda: v.tensor_reduce(out[0], x[0], AxisListType.X, o), out, (x,))
+        run("v", lambda: v.tensor_reduce(out[0], x[0], AxisListType.X, o), out, (x,), size(out, x, 1))
 
     def scan(out, x, y, o0, o1, init=0.0):
-        run("v", lambda: v.tensor_tensor_scan(out[0], x[0], y[0], init, o0, o1), out, (x, y))
+        run("v", lambda: v.tensor_tensor_scan(out[0], x[0], y[0], z(init), o0, o1), out, (x, y, init), size(out, x, fast(out, x, y)))
 
     def iota(out, pat, base=0, cm=0):
-        run("g", lambda: g.iota(out[0], pat, base, cm, allow_small_or_imprecise_dtypes=True), out, ())
+        run("g", lambda: g.iota(out[0], pat, base, cm, allow_small_or_imprecise_dtypes=True), out, (), 156 + 2 * out[1][0][1].size)
 
     def mm(out, prs, start=True, stop=True, each=False):
         def call():
@@ -143,14 +241,11 @@ def rank_program(g, core, T, topo):
                 r = te.matmul((p[2] if len(p) > 2 else out)[0], p[0][0], p[1][0], each or start and n == 0,
                               each or stop and n == len(prs) - 1)
             return r
-        run("t", call, out, [x for p in prs for x in p[:2]])
+        run("t", call, out, [x for p in prs for x in p[:2]],
+            sum(max(min(64, p[0][1][0][1].size), p[1][1][0][1].size) * (0.5 if fast(p[1]) < 1 else 2) for p in prs), not start)
 
-    def wrap(ps, f):
-        for x in range(2):
-            mm(a(ps, (x, 16, 2)), [(a("Zx%d" % x, (16 - 16 * e, 144 - 16 * e)), f(e)) for e in range(2)])
-
-    def hold(out, x, o=A.max):
-        scan(out, a("WD"), x, A.mult, o)
+    def hold(out, x, o=A.max, c=(0, 256)):
+        scan(out, a("WD", c), x, A.mult, o)
 
     def pf(n):
         return a("PF", (n, n + 1))
@@ -167,92 +262,114 @@ def rank_program(g, core, T, topo):
                 if n < len(x) and x[n]:
                     x[n]()
 
-    dma("y", a("wti"), a("wt"), "dwt")
-    dma("s", a("kmi"), a("km"), "dkm")
-    dma("s", a("thi"), a("th"), "dth")
-    for q in range(4):
-        dma("y", a("X0", (1024 * q, 1024 * q + 1024)), a("gen0", (1024 * q, 1024 * q + 1024)), "dx%d" % q)
-    iota(a("ipart"), [[0, 1]], 0, 1)
+    dma("y", a("wti"), a("wt"), "dwt", 2300)
+    dma("s", a("kmi"), a("km"), "dkm", 2300)
+    dma("s", a("thi"), a("th"), "dth", 2500)
+    for n, q in enumerate(OPT["order"]):
+        dma("y", a("X0", (1024 * q, 1024 * q + 1024)), a("gen0", (1024 * q, 1024 * q + 1024)), "dx%d" % q, OPT["load"][n])
+        calls[-1][6].append(len(calls) - 2 - 2 * (n == 0))
+    ip, q15 = a("ipart"), a("MQ", (15, 16))
+    iota(ip, [[0, 1]], 0, 1)
     iota(a("GM"), [[16, 8], [0, 16]])
     iota(a("IC"), [[1, 160]])
-    iota(a("jn"), [[32, 8]], 0, 1)
-    for f, pt in ((5, [[0, 4], [1, 2]]), (6, [[0, 2], [1, 2], [0, 2]]), (7, [[1, 2], [0, 4]])):
-        iota(a("CB", (), f), pt)
-    iota(a("RSi"), [[0, 16], [1, 16]])
-    iota(a("BNeb"), [[0, 2], [32, 8]])
-    iota(a("BNbe"), [[32, 8], [0, 2]])
-    iota(a("PC"), [[16, 256]])
-    iota(a("IK8"), [[1, 256]])
-    iota(a("FB"), [[0, 512]])
-    iota(a("FP"), [[0, 512]])
-    iota(a("PX", (256, 272)), [[0, 16]], 512)
-    iota(a("CJ"), [[16, 256]], 15)
-    iota(a("PE", (256, 384)), [[2, 128]], 258)
-    iota(a("PE", (384, 512)), [[4, 128]], 516)
-    for t in range(ROUNDS):
-        for n, w in (("YT", 1040), ("TT", 512)):
-            iota(a(n + str(t)), [[0, w]])
-    ms(a("CTb", (), (21, 32)), 0.0)
-    for f, c in ((8, 4096.0), (9, 1048576.0), (10, 1.0), (11, P24), (20, 16.0)):
-        ms(a("CTb", (), f), c)
-    ip = a("ipart")
     for n, m in enumerate((15, 112, 31, 111)):
         ts(a("PI", (n, n + 1)), ip, m, AND)
     ts(a("PI", (4, 5)), ip, 4, SHR, 1, AND)
     ts(a("PI", (5, 6)), ip, 5, SHR)
     cp(pf(6), ip)
     cp(a("PF", (0, 6)), a("PI", (0, 6)))
-    ic = a("IC", (0, 144))
-    lin(pd(0), pf(1), 1.0, 15.0)
-    lin(pd(1), pf(3), 1.0, 16.0)
-    lin(pd(15), pf(0), 1.0, 1.0)
-    lin(pd(2), pf(4), -1.0, 1.0)
-    lin(pd(3), pf(0), -1.0, 0.0)
-    lin(pd(4), pf(0), 1.0, -4096.0 - ROUNDER)
-    lin(pd(5), pf(0), 128.0, 0.0)
-    for f in range(5):
-        ts(a("CB", (), f), a("jn"), f, SHR, 1, AND)
     ts(a("IDf"), a("IC", (0, 128)), pf(6), A.is_equal)
-    ts(a("MQ"), a("IC", (0, 16)), pf(0), A.is_equal)
-    ts(a("PD", (8, 12)), a("IC", (0, 4)), pf(5), A.is_equal)
-    ts(a("Zd"), ic, pd(0), A.is_equal, 4096.0, A.mult)
     cp(a("wtf"), a("wti"))
     cp(a("kmf"), a("kmi"))
-    ts(a("Zx"), ic, pd(1), A.is_equal)
     ts(a("WH"), a("GM"), pf(1), A.is_equal, a("wtf"), A.mult)
     ac(a("ID"), a("IDf"))
     lin(a("IDn"), a("IDf"), -1.0, 0.0)
-    q15 = a("MQ", (15, 16))
-    spare = [lambda: ts(a("CTb", (), (0, 8)), a("CB"), -P24, A.mult, P24, A.add),
-             lambda: ts(a("CTb", (), (12, 20)), a("CB"), P24, A.mult),
-             lambda: ts(a("FJ"), a("RSi"), pf(0), A.not_equal),
-             lambda: ts(a("WJ"), a("RSi"), pd(15), A.is_equal, HOLD, A.mult),
-             lambda: tr(a("CTT"), a("CTb")),
-             lambda: tt(a("WD"), a("FJ"), a("WJ"), A.max),
-             lambda: ts(a("SE"), a("GM"), pf(1), A.is_equal, q15, A.mult),
-             lambda: ts(a("T4", (0, 2)), a("thi"), 4096.0, A.mult)]
-    late = ([lambda: lin(a("T4", (2, 4)), a("T4", (0, 2)), -2 * P24, 2 * P24),
-             lambda: lin(a("iT"), a("BNeb"), 1.0, pf(2)),
-             lambda: lin(a("BNbe"), a("BNbe"), 1.0, pf(2))]
-            + [lambda n=n: lin(a("CL", (), (32 * n, 32 * n + 32)), a("CTT"), pd(8 + n), 0.0, COPY) for n in range(4)]
-            + [lambda: ac(a("FB", (), 20), a("iT")),
-               lambda: lin(a("iT1"), a("iT"), 1.0, 1.0),
-               lambda: lin(pd(12), q15, 1.0 - 1.0 / HOLD, 1.0 / HOLD),
-               lambda: lin(pd(14), q15, 1.0 - HOLD, HOLD),
-               lambda: lin(a("CTR"), a("BNbe"), 16.0, float(4080 * 4096 + 15)),
-               lambda: lin(a("Zx0"), a("Zx"), pd(2), 0.0, COPY),
-               lambda: lin(a("Zx1"), a("Zx"), pf(4), 0.0, COPY),
-               lambda: lin(a("RP"), a("RSi"), 1.0, 0.0, AF.Sign)])
 
-    def later():
+    def for_probes():
+        lin(pd(6), pf(4), 4.0, pf(5))
+        lin(pd(0), pd(6), 16.0, pf(0))
+        for x, m in enumerate((4064, 31)):
+            ts(a("TI", (2 * x, 2 * x + 2)), a("thi"), m, AND)
+            ts(a("T4", (2 * x, 2 * x + 2)), a("TI", (2 * x, 2 * x + 2)), -4 * P24, A.mult, 2 * P24 * x, A.add)
+        ts(a("PM"), a("IC", (0, 128)), pd(0), A.is_equal)
+        ts(a("G8"), a("IC", (0, 8)), pd(6), A.is_equal)
+        iota(a("ONE"), [[0, 128]], 1)
+        for n in range(4):
+            lin(a("DT", n, ()), a("PM"), a("T4", (n, n + 1)), 0.0, COPY)
+        for n, x in enumerate((1.0, 2.0, -1.0)):
+            lin(a("WK", n, (0, 8)), a("G8"), 4096.0 * x, 0.0)
+            lin(a("WK", n, (8, 16)), a("G8"), 4 * P24 * x, 0.0)
+        iota(a("RSi"), [[0, 16], [1, 16]])
+        lin(a("RS"), a("RSi", (0, 128)), -2 * P24, 2 * P24, AF.Relu)
+
+    def for_links():
+        iota(a("iT"), [[1, 2], [128, 2], [0, 8]], 0, 1)
+        iota(a("FB"), [[0, 512]])
+        iota(a("FB", (), (), 20), [[128, 2], [0, 8]], 0, 1)
+        iota(a("FB", (), (), 21), [[0, 16]], 1)
+        iota(a("jn"), [[32, 8]])
+        iota(a("CTb", (), 21), [[-16 * BLOCK, 8]], 4096)
+        ms(a("CTb", (), (22, 32)), 0.0)
+        for f, c in ((16, 4096.0), (17, 1048576.0), (18, 1.0), (19, P24), (20, 16.0)):
+            ms(a("CTb", (), f), c)
+        ts(a("jn"), a("jn"), pf(2), A.add)
+        for f in range(4):
+            ts(a("CB", (), f), a("jn"), 2 * f, SHR, 3, AND)
+        for x in range(4):
+            ts(a("CTb", (), (4 * x, 4 * x + 4)), a("CB"), float(x), A.not_equal, P24, A.mult)
+        tr(a("CTT"), a("CTb"))
+        ts(a("PD", (8, 12)), a("IC", (0, 4)), pf(5), A.is_equal)
+        for n in range(4):
+            lin(a("CL", (), (32 * n, 32 * n + 32)), a("CTT"), pd(8 + n), 0.0, COPY)
+        lin(pd(16), pf(2), 16.0, float(4081 * 4096 + 15))
+        lin(a("CTR"), a("IC", (0, 128)), 0.0, pd(16))
+        iota(a("FP"), [[0, 512]])
+        iota(a("BO"), [[BLOCK, 8], [0, 2]], -256)
+        lin(a("RP"), a("RSi"), 1.0, 0.0, AF.Sign)
+        lin(pd(1), pf(3), 1.0, 16.0)
+        lin(pd(2), pf(4), -1.0, 1.0)
+        ts(a("Zx"), a("IC", (0, 144)), pd(1), A.is_equal)
+        lin(a("Zx0"), a("Zx"), pd(2), 0.0, COPY)
+        lin(a("Zx1"), a("Zx"), pf(4), 0.0, COPY)
+        lin(pd(7), pf(6), 1.0, 9.0)
+        ts(pd(17), pf(2), 22.0, A.is_equal)
+        ts(a("Zj"), a("IC"), pd(7), A.is_equal, pd(17), A.mult)
+
+    def for_chains():
+        lin(pd(15), pf(0), 1.0, 1.0)
+        ts(a("MQ"), a("IC", (0, 16)), pf(0), A.is_equal)
+        ts(a("FJ"), a("RSi"), pf(0), A.not_equal)
+        ts(a("WJ"), a("RSi"), pd(15), A.is_equal, HOLD, A.mult)
+        tt(a("WD"), a("FJ"), a("WJ"), A.max)
+        lin(pd(12), q15, 1.0 - 1.0 / HOLD, 1.0 / HOLD)
+        lin(pd(14), q15, 1.0 - HOLD, HOLD)
+        iota(a("PX", (256, 512)), [[1, 256]])
+        iota(a("Y0", (256, 512)), [[0, 256]])
+        iota(a("PW", (), (256, 512)), [[0, 3], [1, 256]])
+        iota(a("ZW", (), (256, 512)), [[0, 1024]])
+        iota(a("PC"), [[16, 256]])
+        iota(a("IK8"), [[1, 256]])
+        iota(a("RW", (0, 256)), [[1, 256]], 1)
+        iota(a("YV", (0, 256)), [[0, 256]])
+        iota(a("CJ"), [[16, 256]], 15)
         lin(a("IK8"), a("IK8"), 1.0 / 256, 0.0)
         lin(a("PC"), a("PC"), 1.0, pf(0))
         lin(pd(20), pd(14), 257.0, 0.0)
+        lin(pd(4), pf(0), 1.0, -4096.0 - ROUNDER)
         lin(a("IDfn"), a("IDf"), -1.0, 0.0)
+        ts(a("SE"), a("GM"), pf(1), A.is_equal, q15, A.mult)
         lin(a("SEn"), a("SE"), -1.0, 0.0)
         lin(pd(13), pd(12), -0.125, 0.0)
-        lin(a("iW"), a("PC", (0, 16)), pd(14), pd(14))
         lin(a("W256"), a("PC", (0, 16)), pd(14), pd(20))
+        lin(pd(21), pd(14), 256.0, 0.0)
+        lin(a("PB"), a("PC"), 4097.0, 4096.0 - P24)
+        iota(a("RW", (448, 528)), [[2, 80]], 258)
+        iota(a("PT", (0, 256)), [[1, 256]], -256)
+        iota(a("ZT", (0, 256)), [[0, 256]])
+        iota(a("C16"), [[0, 256]], 16)
+        for t in range(ROUNDS):
+            iota(a("YT", (2 * t, 2 * t + 2), (0, 272)), [[0, 544]])
+            iota(a("TT%d" % t), [[0, 512]])
     lo, col15, halves = (0, 256), (15, 256, 16), ((0, 128), (128, 256))
 
     def quarter(n):
@@ -271,186 +388,173 @@ def rank_program(g, core, T, topo):
     def way(src, dst):
         return 2 if topo.chip(src) == topo.chip(dst) else int(topo.die(src) == topo.die(dst))
 
+    def share(c, ks, k):
+        alike = {m: [x for x in ks if engines(c, x) == engines(c, m)] for m in ks}
+        n = min(len(engines(c, m)) // len(alike[m]) for m in ks)
+        return engines(c, k)[n * alike[k].index(k):][:n]
+
     def send(ks, name, src, dst):
-        def share(c, k):
-            alike = {m: [x for x in ks if engines(c, x) == engines(c, m)] for m in ks}
-            n = min(len(engines(c, m)) // len(alike[m]) for m in ks)
-            return engines(c, k)[n * alike[k].index(k):][:n]
-        need("g", [x for k in ks for x in src(k)[1]], [])
-        ws = [(topo.addr(to(k)), sum(1 << x for x in share(core, k)), T.sem["%s_%d" % (name, k)], src(k)[0]) for k in ks]
-        left = "%s_l%d" % (name, ks[0])
-        if len(ks) == 1:
-            ad, mask, sem, x = ws[0]
-            g.remote_dma(dst(rank)[0], x, sem, T.sem[left], ad[1], ad[0], mask)
-        else:
-            g.remote_dma_fused([RemoteDMATransfer(dst_ids=[DstId(rid=ad[0], pnc=ad[1])], dma_engine_mask=mask, remote_sem=sem,
-                                                  src=x, dst=dst(rank)[0]) for ad, mask, sem, x in ws], local_sem=T.sem[left])
-        total[left] = sum(len(share(core, k)) for k in ks)
-        for k in ks:
+        reads = [x for k in ks for x in src(k)[1]]
+        ws = [(topo.addr(to(k)), sum(1 << x for x in share(core, ks, k)), T.sem["%s_%d" % (name, k)], src(k)[0]) for k in ks]
+        left, there = "%s_l%d" % (name, ks[0]), dst(rank)[0]
+
+        def issue():
+            need("g", reads, [])
+            if len(ks) == 1:
+                ad, mask, sem, x = ws[0]
+                g.remote_dma(there, x, sem, T.sem[left], ad[1], ad[0], mask)
+            else:
+                g.remote_dma_fused([RemoteDMATransfer(dst_ids=[DstId(rid=ad[0], pnc=ad[1])], dma_engine_mask=mask, remote_sem=sem,
+                                                      src=x, dst=there) for ad, mask, sem, x in ws], local_sem=T.sem[left])
+            total[left] = sum(len(share(core, ks, k)) for k in ks)
+        calls.append(("g", issue, reads, [], 300, 300, sent[-1:], False))
+        sent.append(len(calls) - 1)
+
+    def land(name, ks, dst, cycles):
+        for k in (1, 2, 3):
             fr = (rank - k) % 4
-            done("", "%s_%d" % (name, k), len(share(T.cores[fr], k)), [], dst(fr)[1])
+            n = len(share(T.cores[fr], ks(k), k))
+            calls.append(("w%s%d" % (name, k), lambda k=k, n=n, w=dst(fr)[1]: done("", "%s_%d" % (name, k), n, [], w), [], dst(fr)[1], 0,
+                          cycles[way(T.cores[fr], core)], sent[-1:], False))
+    sent = []
 
     for t in range(ROUNDS):
         xn, nx = "X%d" % t, "X%d" % (t + 1)
         win = a(xn, (0, 4096))
+        own = rank if t else 0
+        vb = own // 2 if OPT["first"][t] else 1
+        sb = 1 - vb
+        s0, v0, aid = 128 * sb, 128 * vb, 128 - OPT["help"][t]
 
         def last(i):
             return a("LC", i) if t else a(xn, (16 * i[0] + 15, 16 * i[1], 16))
 
         def hashes(i):
             j = (256 + i[0], 256 + i[1])
-            return [lambda: mm(a("ps7", i), [(a("WH"), last(i))]),
-                    lambda: cp(a("U1", i), a("ps7", i)),
-                    lambda: ts(a("U", i), a("U1", i), 4095, AND),
-                    lambda: tt(a("UU", i), a("U", i), a("U", i), A.mult),
-                    lambda: ts(a("ps6", i), a("U", i), a("kmf", (2 * t, 2 * t + 1)), A.mult),
-                    lambda: ts(a("UB", i), a("UU", i), 5, SHR),
-                    lambda: ts(a("ps6", j), a("U", i), a("kmf", (2 * t + 1, 2 * t + 2)), A.mult),
-                    lambda: tt(a("CA", 0, i), a("ps6", i), a("UB", i), A.add),
-                    lambda: tt(a("CA", 1, i), a("ps6", j), a("UB", i), A.add),
-                    lambda: ts(a("CI", 0, i), a("CA", 0, i), 4095, AND),
-                    lambda: ts(a("CI", 1, i), a("CA", 1, i), 4095, AND),
-                    lambda: cp(a("CU", 0, i), a("CI", 0, i)),
-                    lambda: cp(a("CU", 1, i), a("CI", 1, i))]
+            b = "ps%d" % (7 if t or OPT["order"].index(i[0] // 64) % 2 else 3)
+            return ([lambda: mm(a(b, i), [(a("WH"), last(i))]) if t == 0 or i[0] == 64 * own else None,
+                     lambda: cp(a("U1", i), a(b, i)),
+                     lambda: ts(a("U", i), a("U1", i), 4095, AND),
+                     lambda: tt(a("UU", i), a("U", i), a("U", i), A.mult),
+                     lambda: ts(a("UB", i), a("UU", i), 5, SHR),
+                     lambda: ts(a("ps6", i), a("U", i), a("kmf", (2 * t, 2 * t + 1)), A.mult),
+                     lambda: ts(a("ps6", j), a("U", i), a("kmf", (2 * t + 1, 2 * t + 2)), A.mult)]
+                    + [lambda h=h, f=f: f(h) for h in range(2) for f in (
+                        lambda h: tt(a("CA", h, i), a("ps6", j if h else i), a("UB", i), A.add),
+                        lambda h: ts(a("CI", h, i), a("CA", h, i), 4095, AND),
+                        lambda h: cp(a("CU", h, i), a("CI", h, i)))])
 
-        def repeats(n):
-            for j in range(2):
-                i, b = (64 * n + 32 * j, 64 * n + 32 * j + 32), "ps%d" % ((2 * n + 2) % 6 + j)
-                mm(a(b), [(a("ID"), last(i), a(b, (x, 512, 16))) for x in range(16)], each=True)
-                ac(a("XR", (16 * i[0], 16 * i[1])), a(b))
-        twice0 = [lambda x=x: ac(a("R2", (x, 128, 2)), last(quarter(0))) for x in range(2)]
-        if t == 0:
-            lin(a("RS"), a("RSi"), -2 * P24, 2 * P24, AF.Relu)
-            weave(twice0)
-            weave(spare[:OPT["sp"]])
-            rest = hashes(halves[1])
-            weave(hashes(quarter(0)), spare[OPT["sp"]:], [None] * OPT["lag1"] + hashes(quarter(1)), [None] * OPT["lag2"] + rest[:OPT["cut"]],
-                  [None] * OPT["lag1"] + [lambda: repeats(1)], [None] * OPT["lag2"] + [lambda: repeats(2)])
-            rest = rest[OPT["cut"]:]
+        def repeats(i, b):
+            n = 16 * (i[1] - i[0])
+            mm(a(b, (0, n)), [(a("ID"), last(i), a(b, (x, n, 16))) for x in range(16)], each=True)
+            ac(a("XR", (16 * i[0], 16 * i[1])), a(b, (0, n)))
+        helped = [(s0 + x, s0 + min(x + 32, 128)) for x in range(aid, 128, 32)]
+        v1, v2 = (64 * own, 64 * (own ^ 1)) if own // 2 == vb else (v0, v0 + 64)
+        xr = [(v1, v1 + 32), (v1 + 32, v1 + 64)] + helped + [(v2, v2 + 32), (v2 + 32, v2 + 64)]
+        if t:
+            far = [quarter(x) for x in (2 * sb, 2 * sb + 1, own ^ 1)]
+            weave(hashes(quarter(own)))
+            mm((None, [x for i in far for x in a("ps7", i)[1]]), [(a("WH"), last(i), a("ps7", i)) for i in far], each=True)
+            weave(*[hashes(i) for i in far])
         else:
-            hs = [hashes(c) for c in halves]
-            weave(*[x[:1] for x in hs])
-            weave(twice0)
-            for n in range(1, 4):
-                repeats(n)
-            weave(*[x[1:] for x in hs])
-            for h in range(2):
-                cp(a("CF", h, ()), a("CI", h, ()))
-            rest = []
+            weave(*[[None] * (OPT["late"] * n) + hashes(quarter(q)) for n, q in enumerate(OPT["order"])])
+        for n in (2 * sb, 2 * sb + 1):
+            for x in range(2):
+                ac(a("R2", (128 * n + x, 128 * n + 128, 2)), last(quarter(n)))
+        for n, i in enumerate(xr):
+            repeats(i, "ps%d" % ((4 + n) % 6))
+        if t == 0:
+            for_probes()
 
         def span(h, i):
             return (4096 * h + 16 * i[0], 4096 * h + 16 * i[1])
 
-        def keys(h, i):
-            return a("ps%d" % (2 * h + 2 if i[0] == 192 else h), i)
+        def keys(b, h, c=(0, 256)):
+            return a("ps%d" % (2 * b + h), c)
 
-        def column(n, h):
-            return [(a("IDf"), a("CF", h, quarter(n)))]
+        def opened(b, h):
+            mm(keys(b, h, (128, 256)), [(a("ONE"), a("DT", 2 * x + h, ())) for x in range(2)], stop=False)
+            o, x = a("CF", h, halves[b]), a("CI", h, halves[b])
+            run("g", lambda: g.affine_select(o[0], x[0], [[0, 128]], A.is_ge, 0.0, 0, 0), o, (x,), 205 + 256)
+            mm(keys(b, h, (0, 128)), [(a("CF", h, halves[b]), a("PM"))], False, False)
 
-        def sums(n, h):
-            d = span(h, quarter(n))
-            mm(keys(h, quarter(n)), (column(n, h) if n < 3 else [])
-               + [(a("Zd", (15 - p, 143 - p)), a("AD", (d[0] + p, d[1], 16))) for p in range(16)], start=n < 3)
+        def sums(b, h, x, w, stop, i=None):
+            i = i or halves[b]
+            d, ps = span(h, i), T["ps%d" % (2 * b + h)]
+            mm(keys(b, h), [(a(x, (d[0] + p, d[1], 16)), a("WK", w, ()), (ps[i[0] % 128:(i[1] - 1) % 128 + 1, p:256:16],))
+                            for p in range(16)], False, stop)
 
         def less(h, i):
             tt(a("DF", span(h, i)), ind(win, a("CU", h, i)), a("XR", (16 * i[0], 16 * i[1])), A.subtract)
 
-        def absolute(h, i):
-            ac(a("AD", span(h, i)), a("DF", span(h, i)), ABS)
+        def plain(h, i, b):
+            d, n = span(h, i), 16 * (i[1] - i[0])
+            return [lambda: ac(a("DF", d), ind(win, a("CU", h, i))),
+                    lambda: mm(a(b, (0, n)), [(a("IDn"), a("R2", (2 * i[0], 2 * i[1])), a(b, (x, n, 8))) for x in range(8)], stop=False),
+                    lambda: mm(a(b, (0, n)), [(a("ID"), a("DF", d))], False),
+                    lambda: ac(a("AD", d), a(b, (0, n)), ABS)]
 
-        def plain(h):
-            x = 64 - OPT["help"][t] * h
-            if x < 64:
-                cp(a("DF", span(h, (x, 64))), ind(win, a("CU", h, (x, 64))))
-            ac(a("DF", span(h, (0, x))), ind(win, a("CU", h, (0, x))))
+        def ended(b, h):
+            parts = [i for x, i in by_v if x] if b == vb and h and OPT["parts"] else [None]
+            for i in parts[:-1]:
+                sums(b, h, "AD", 1, False, i)
+            if b == vb:
+                sums(b, h, "DF", 2, False)
+            sums(b, h, "AD", int(b == vb), True, parts[-1])
+            bests(b, h)
 
-        def plain_less(h, banks):
-            for j, b in enumerate(banks):
-                d = 4096 * h + 512 * j
-                mm(a(b), [(a("ID"), a("DF", (d, d + 512)))]
-                   + [(a("IDn"), a("R2", (64 * j, 64 * j + 64)), a(b, (x, 512, 8))) for x in range(8)])
+        def bests(b, h):
+            ac(a("pen", 2 * b + h, ()), keys(b, h, (128, 256)), AF.Relu)
+            tt(a("CF", h, halves[b]), keys(b, h, (0, 128)), a("pen", 2 * b + h, ()), A.max)
+            scan(a("SC", h, halves[b]), a("RS"), a("CF", h, halves[b]), A.max, A.min)
 
-        def plain_end(h, banks):
-            for j, b in enumerate(banks):
-                d = 4096 * h + 512 * j
-                ac(a("AD", (d, d + 512)), a(b), ABS)
-            sums(0, h)
+        by_s = [(h, (s0 + x, s0 + min(x + 32, w))) for h, w in ((0, aid), (1, 128)) for x in range(0, w, 32)]
+        by_v = ([(0, (v1, v1 + 64))] + [(0, i) for i in helped] + [(0, (v2, v2 + 64)), (1, (v1, v1 + 64))]
+                + [(1, (v2 + x, v2 + y)) for x, y in OPT["pieces"]])
+        by_s = [plain(h, i, "ps%d" % (4 + n % 4)) for n, (h, i) in enumerate(by_s)]
+        lag = OPT["lag"]
 
-        def bests(h, i):
-            return [lambda: ts(a("pen", h, i), keys(h, i), a("T4", (h, h + 1)), A.is_ge, 2 * P24, A.mult) if i[0] < 192 else
-                    lin(a("pen", h, i), keys(h, i), 2 * P24, a("T4", (2 + h, 3 + h)), AF.Relu),
-                    lambda: tt(a("km2", h, i), keys(h, i), a("pen", h, i), A.max),
-                    lambda: tr(a("kt", h, i), a("km2", h, i)),
-                    lambda: scan(a("SC", h, i), a("RS", i), a("kt", h, i), A.max, A.min)]
-        q1, q2, q3 = quarter(1), quarter(2), quarter(3)
-        l0 = 256 - OPT["last"]
-        plain(0)
+        def after(h, i):
+            if i in helped:
+                ac(a("AD", span(h, i)), a("DF", span(h, i)), ABS)
+            else:
+                ts(a("AD", span(h, i)), a("DF", span(h, i)), 0.0, A.max)
+        for n in range(len(by_s) + lag):
+            if n < len(by_s):
+                weave(by_s[n][:3])
+            if n >= lag:
+                by_s[n - lag][3]()
+            if n < len(by_v):
+                less(*by_v[n])
+            if 0 < n <= len(by_v):
+                after(*by_v[n - 1])
+            if n < 2:
+                opened(sb, n)
+                opened(vb, n)
+            if n == OPT["mid"][0]:
+                ended(sb, 0)
+            if n == OPT["mid"][1]:
+                ended(vb, 0)
+        ended(sb, 1)
+        ended(vb, 1)
         if t == 0:
-            repeats(3)
-        plain_less(0, ("ps4", "ps5"))
-        if rest:
-            weave([lambda c=c: less(0, c) for c in ((64, 80), (80, 96), (96, 128))], rest[0::2], rest[1::2])
-        else:
-            less(0, (64, 96))
-            less(0, (96, 128))
-        if t == 0:
-            cp(a("CF", 0, ()), a("CI", 0, ()))
-        absolute(0, (64, 96))
-        absolute(0, (96, 128))
-        less(1, q1)
-        if t == 0:
-            cp(a("CF", 1, ()), a("CI", 1, ()))
-        sums(1, 0)
-        plain_end(0, ("ps4", "ps5"))
-        plain(1)
-        less(0, q2)
-        absolute(1, q1)
-        plain_less(1, ("ps3", "ps7"))
-        sums(1, 1)
-        less(1, q2)
-        absolute(0, q2)
-        plain_end(1, ("ps3", "ps7"))
-        for h in range(2):
-            mm(keys(h, q3), column(3, h), stop=False)
-        sums(2, 0)
-        less(0, q3)
-        absolute(1, q2)
-        sums(2, 1)
-        less(1, (192, l0))
-        absolute(0, q3)
-        sums(3, 0)
-        less(1, (l0, 256))
-        absolute(1, (192, l0))
-        absolute(1, (l0, 256))
-        sums(3, 1)
-        if t == 0:
-            weave(late[:OPT["lt"]])
-        weave(bests(0, (0, 192)), bests(1, (0, 192)))
-        weave(bests(0, q3), bests(1, q3))
-        if t == 0:
-            weave(late[OPT["lt"]:])
-        mm(a("ps6", lo), [(a("WH"), last(lo))])
-        lin(a("y1"), a("ps6", lo), 1.0 / 128, 1.0 / 256 - 0.5)
-        lin(a("W0"), a("ps6", lo), pd(3), 0.0, COPY)
-        lin(a("y2"), a("y1"), 1.0, ROUNDER)
-        lin(a("y1"), a("y2"), 1.0, -ROUNDER)
-        lin(a("HP"), a("y1"), pd(5), 0.0, COPY)
-        for e in range(2):
-            c = (16 * e + 15, 256, 32)
-            tt(a("best", (8 * e, 8 * e + 8)), a("SC", 0, c), a("SC", 1, c), A.min)
+            for_links()
         be = a("best")
+        tt(be, a("SC", 0, col15), a("SC", 1, col15), A.min)
+        for f in range(4):
+            ts(a("FI", (), f), be, 4 + 2 * f, SHR, 3, AND)
         ts(a("Jt"), be, 4, SHR, 255, AND)
-        for f in range(8):
-            ts(a("FI", (), f), be, 4 + f, SHR, 1, AND)
-        tt(a("FI", (), 11), a("Jt"), a("iT"), A.is_le)
-        ts(a("FI", (), 8), be, 12, SHR, 255, AND)
-        ts(a("FI", (), 9), be, 20, SHR, 31, AND)
-        ts(a("FI", (), 10), be, 1, SHR, 7, AND)
-        ts(a("FB", (), (12, 20)), a("FI", (), (0, 8)), -1.0, A.mult, 1.0, A.add)
-        cp(a("FB", (), (0, 12)), a("FI", (), (0, 12)))
+        ts(a("FI", (), 4), be, 12, SHR, 255, AND)
+        ts(a("FI", (), 5), be, 20, SHR, 31, AND)
+        ts(a("FI", (), 6), be, 1, SHR, 7, AND)
+        for x in range(4):
+            ts(a("FB", (), (), (4 * x, 4 * x + 4)), a("FI", (), (0, 4)), float(x), A.is_equal)
+        tt(a("FB", (), (), 19), a("Jt"), a("iT", 0, ()), A.is_le)
+        tt(a("FB", (), (), 22), a("Jt"), a("iT", 1, ()), A.max)
+        cp(a("FB", (), (), (16, 19)), a("FI", (), (4, 7)))
         for e in range(2):
-            tr(a("RT", (256 * e, 256 * e + 256)), a("FB", (8 * e, 8 * e + 8), ()))
-        tt(a("Jx"), a("Jt"), a("iT1"), A.max)
+            mm(a("ps%d" % (4 + e), lo), [(a("FB", 2 * b + e, (), ()), a("ID"), a("ps%d" % (4 + e), halves[b])) for b in range(2)], each=True)
+            (cp, ac)[e](a("RT", (256 * e, 256 * e + 256)), a("ps%d" % (4 + e), lo))
         def pieces(bs):
             for b, e in [(0, 0), (1, 0), (0, 1), (1, 1)] + [(b, e) for b in bs for e in range(2)]:
                 w = 32 * b + 32
@@ -459,140 +563,164 @@ def rank_program(g, core, T, topo):
             mm(a(ps, (o, o + w)), [(a("CL", b, ()), a("RT", (256 * e, 256 * e + w)))])
             if b > 3 and e:
                 ac(a("SH", b, (0, w)), a(ps, (1, 2 * w, 2)))
-        if t == 0:
-            later()
         for b, e, ps, o, w in pieces((2, 3, 7, 6, 5, 4)):
             if b > 3:
                 scan(a("SCN", 2 * b + e, (128 - w // 2, 128)), a(ps, (o, o + w, 2)),
-                     a("SH", b, (w // 2 * e, w // 2 * (e + 1))), A.min, A.min, 2 * P24)
+                     a("SH", b, (w // 2 * e, w // 2 * (e + 1))), A.min, A.min, pd(16))
             else:
-                red(a("SCN", 2 * b + e, (127, 128)), a(ps, (o, o + w)), A.min)
-        wrap("ps0", lambda e: a("Jx", (8 * e, 8 * e + 8)))
-        tt(a("AI"), a("SCN", (), 127), a("CTR"), A.min)
-        cp(a("LJ"), a("ps0", (0, 16)))
-        ts(a("PZ", 0, ()), a("AI"), 4, SHR, 255, AND)
-        ts(a("PZ", 1, ()), a("AI"), 15, AND)
-        ts(a("FP", 0, (0, 256, 16)), a("PZ", 0, ()), 1.0, A.add)
+                scan(a("SCN", 2 * b + e, (128 - w, 128)), a(ps, (o, o + w)), a("CTR", (0, w)), A.min, A.min, pd(16))
+        ts(a("PZ", 0, ()), a("SCN", (), 127), 4, SHR, 255, AND)
+        ts(a("PZ", 1, ()), a("SCN", (), 127), 15, AND)
+        tt(a("FP", 0, (0, 256, 16)), a("PZ", 0, ()), a("BO"), A.add)
         ts(a("FP", 1, (0, 256, 16)), a("PZ", 1, ()), -1.0, A.mult, 15.0, A.add)
-        wrap("ps3", lambda e: a("FP", 0, (16 * e, 256, 32)))
+        for x in range(2):
+            mm(a("ps3", (x, 16, 2)), [(a("Zx%d" % x, (16 - 16 * e, 144 - 16 * e)), a("FP", 0, (16 * e, 256, 32))) for e in range(2)])
         for n in range(2):
             scan(a("FQ", n, ()), a("RP"), a("FP", n, ()), A.mult, A.add)
         tr(a("PX", lo), a("FQ", 0, ()))
-        ts(a("LV", 0, ()), a("ps3", (0, 16)), -1.0, A.add)
-        for n in range(2):
-            tr(a("Y0", n, ()), a("FQ", 1, ()))
+        ts(a("LV", 0, ()), a("ps3", (0, 16)), 256.0, A.add)
+        for n in (0, 512):
+            tr(a("Y0", (n, n + 256)), a("FQ", 1, ()))
+        if t == 0:
+            for_chains()
+            lin(pd(3), pf(0), -1.0, 0.0)
+            lin(pd(5), pf(0), 128.0, 0.0)
 
-        y0 = a("Y0", 0, ())
-        terms = (("W0", 0), ("HP", 0), ("y3", 1), ("t2", 0))
+        y0 = a("Y0", lo)
 
-        def places():
-            mm(a("ps2", lo), [(a("IDf"), a("t2"))], start=False)
-            if t + 1 < ROUNDS:
-                for k in range(4):
-                    mm(a("ps0", quarter(k)), [(a("SEn" if n else "SE"), a(x, (k, 256, 4))) for x, n in terms])
-        by_scalar = [
-            lambda: ac(a("FJ", (0, 128)), ind(a("PX", (0, 272)), a("LJ", (0, 8)))),
-            lambda: ac(a("FJ", (128, 256)), ind(a("PX", (0, 272)), a("LJ", (8, 16)))),
-            lambda: run("s", lambda: s.activation(T.sg[:], y0[0], ABS, bias=-8.0, accum_out=lc(0)[0]),
-                        (None, a("sg")[1] + lc(0)[1]), (y0,)),
-            lambda: [lin(lc(1), lc(0), 1.0, 2048.0), lin(lc(2), lc(0), -1.0, 2048.5), lin(lc(3), lc(0), 0.5, 1024.0)],
-            lambda: lin(a("y1"), a("IK8"), lc(1), 1.0 / 512 - 0.5),
-            lambda: lin(a("y2"), a("y1"), 1.0, ROUNDER),
-            lambda: [lin(a("y3"), a("y2"), 1.0, pd(4))]
-            + [mm(a(b, lo), [(a("IDfn" if n else "IDf"), a(x)) for x, n in terms[:3]], stop=b == "ps1") for b in ("ps1", "ps2")],
-            lambda: lin(a("R16"), y0, -2.0, 16.0, AF.Relu),
-            lambda: lin(a("ps4", (0, 512, 2)), a("PC"), 4097.0, 4096.0)]
-        by_vector = {4: lambda: hold(a("WJ"), a("FJ")),
-                     5: lambda: tt(a("NE"), a("WJ", col15), a("iW"), A.is_equal),
-                     6: lambda: tt(a("NTW"), a("NE"), a("W256"), A.mult)}
+        def past(c):
+            return (256 + c[0], 256 + c[1])
 
-        def summed(n, m, rest, c):
-            tt(a("YW", n, c), ind(rest, a("LV", m, (c[0] // 16, c[1] // 16))), a("YW", m, c) if m else a("Y0", 1, c), A.add)
-        for n in range(1, LAST + 1):
-            ac(a("PW", n, ()), ind(a("PW", n - 1, ()) if n > 1 else a("PX", lo), a("LV", max(n - 2, 0), ())))
-            if n > 1:
-                by_scalar[n - 2]()
-            rest = a("YW", n - 2, ()) if n > 2 else y0
-            if n == 1:
-                summed(n, 0, rest, lo)
-            hold(a("WS", n, ()), a("PW", n, ()))
-            if n > 1:
-                summed(n, n - 1, rest, halves[0])
-            ts(a("LV", n, ()), a("WS", n, col15), pd(12), A.mult, -1.0, A.add)
-            if n == LAST:
-                tt(a("SLf"), a("WS", n, col15), a("NTW"), A.max)
-            if n > 1:
-                summed(n, n - 1, rest, halves[1])
-            if n in by_vector:
-                by_vector[n]()
-        ts(a("SL"), a("SLf"), pd(12), A.mult, -1.0, A.add)
-        ac(a("PW", LAST + 1, ()), ind(a("PW", LAST, ()), a("LV", LAST - 1, ())))
-        by_scalar[LAST - 1]()
-        cp(a("YW", 0, ()), a("YW", LAST, ()))
-        ac(a("PE", lo), ind(a("PW", LAST + 1, ()), a("LV", LAST, ())))
-        summed(LAST + 1, LAST, a("YW", 0, ()), lo)
-        ac(a("PW", 0, ()), ind(a("PE", (0, 512)), a("SL")))
-        ac(a("PW", STEPS, ()), ind(a("PE", lo), a("LV", LAST, ())))
-        lin(a("sg"), a("ps1", lo), -1.0, lc(2), AF.Sign)
-        hold(a("WS", 0, ()), a("PW", 0, ()))
-        summed(STEPS, LAST, a("YW", LAST + 1, ()), lo)
-        YT, TT = ["%s%d" % (x, t) for x in ("YT", "TT")]
-        yf, root = a("YW", STEPS, ()), a("WS", STEPS, col15)
-        lin(a("t2"), a("sg"), lc(3), lc(3))
-        places()
-        lin(a("Yc"), yf, -1.0, 4097.0)
-        lin(a("ps4", (1, 512, 2)), a("PC"), 4097.0, 4096.0)
-        ts(a("LU"), a("WS", 0, col15), pd(12), A.mult, -1.0, A.add)
-        hold(a("WS", STEPS, ()), a("PW", STEPS, ()))
-        cp(ind(a(YT, (8, 1032)), a("LU")), yf)
-        ts(a("RL"), root, pd(12), A.mult, -1.0, A.add)
-        scan(a("G"), a("R16"), a(YT, (7, 263)), A.add, A.add)
+        def lst(n, c):
+            return a("LV", n, (c[0] // 16, c[1] // 16))
+
+        def ends(n, c):
+            return a("WS", n, (c[0] + 15, c[1], 16))
+
+        def summed(n, c):
+            rest = a("ZW", (n - 2) % 4, ()) if n > 2 else a("Y0", (0, 512))
+            out = a("YV", past(c)) if c[1] <= BLOCK else a("ZT", past(c)) if n == STEPS and c[0] == 0 else a("ZW", n % 4, c)
+            tt(out, ind(rest, lst(n - 1, c)), a("ZW", (n - 1) % 4, c) if n > 1 else a("Y0", (512 + c[0], 512 + c[1])), A.add)
+        mm(a("ps0", (0, 16)), [(a("Zj", (31 - 16 * e - q, 159 - 16 * e - q)), a("RT", (256 * e + q, 256 * e + 256, 16)))
+                               for e in range(2) for q in range(16)])
+        followed = [lambda: cp(a("LJ"), a("ps0", (0, 16))),
+                    lambda: ac(a("FJ", halves[0]), ind(a("PX"), a("LJ", (0, 8)))),
+                    lambda: ac(a("FJ", halves[1]), ind(a("PX"), a("LJ", (8, 16)))),
+                    lambda: hold(a("WJ"), a("FJ"), A.add),
+                    lambda: ts(a("NI", 0, ()), a("WJ", col15), pd(12), A.mult),
+                    lambda: ts(a("NI", 1, ()), a("NI", 0, ()), 255, AND),
+                    lambda: tt(a("NI", 2, ()), a("NI", 1, ()), a("PC", (0, 16)), A.is_equal),
+                    lambda: tt(a("NTW"), a("NI", 2, ()), a("W256"), A.mult),
+                    lambda: ts(a("SLf", (16, 20)), a("NTW", (12, 16)), pd(21), A.subtract)]
+        for n in range(1, STEPS + 1):
+            pw, out = a("PW", (n - 1) % 3, ()) if n > 1 else a("PX"), a("PW", n % 3, lo) if n < STEPS else a("PT", past(lo))
+            ac(out, ind(pw, lst(max(n - 2, 0), lo)))
+            if n == STEPS:
+                lin(a("RW", past((0, BLOCK))), ind(pw, lst(n - 2, (0, BLOCK))), 1.0, 257.0)
+            hold(a("WS", n % 2, ()), out, A.add)
+            ts(lst(n, lo), ends(n % 2, lo), pd(12), A.mult, 256.0, A.add)
+            for x in halves if n < STEPS else ((0, BLOCK), halves[0], halves[1]):
+                summed(n, x)
+            weave(followed[OPT["flags"][n - 1]:OPT["flags"][n]])
+        up = halves[1]
+        ac(a("PW", 0, up), ind(a("PT"), lst(STEPS, up)))
+        hold(a("WS", 0, up), a("PW", 0, up), A.add, up)
+        ts(lst(STEPS + 1, up), ends(0, up), pd(12), A.mult, 256.0, A.add)
+        ac(a("ZT", (384, 480)), a("ZW", STEPS % 4, (128, 224)))
+        tt(a("ZW", 0, up), ind(a("ZT", (0, 480)), lst(STEPS, up)), a("ZW", STEPS % 4, up), A.add)
+        blocks = [(32, 64), (64, 96), (96, 128), (128, 192), (192, 256)]
+        end, TT = blocks[-1], "TT%d" % t
+        tt(a("SLf", (20, 24)), ends(0, end), a("SLf", (16, 20)), A.max)
+        ts(a("LU", 1, (12, 16)), a("SLf", (20, 24)), pd(12), A.mult, 256.0, A.add)
+
+        def tails(n, c):
+            tt(ind(a("YT", 2 * t + n, (8, 520)), a("LU", 2 * n, (c[0] // 16, c[1] // 16))), a("YV", past(c)), a("C16", c), A.add)
+        for c in blocks:
+            n = STEPS + c[0] // 128
+            if c == end:
+                ac(a("RW", (528, 592)), ind(a("RW", (0, 528)), a("LU", 1, (12, 16))))
+            ac(a("RW", past(c) if c != end else (592, 656)), ind(a("RW", (0, 256 + c[0])), lst(n, c)))
+            tt(a("YV", past(c)), ind(a("YV", (0, 256 + c[0])), lst(n, c)), a("ZW", 0, c) if c[0] // 128 else a("ZT", past(c)), A.add)
+            for x in OPT["tails"]:
+                if x[1] + OPT["behind"] == c[1] or x[1] + OPT["behind"] > c[1] == 256:
+                    w = (x[0] // 16, x[1] // 16)
+                    hold(a("WS", 2, x), a("RW", past(x)), A.max, x)
+                    tt(a("SLf", w), ends(2, x), a("NTW", w), A.max)
+                    ts(a("LU", 0, w), a("SLf", w), pd(12), A.mult, -1.0, A.add)
+                    tails(0, x)
+        hold(a("WS", 1, end), a("RW", (528, 592)), A.max, end)
+        ts(a("LU", 2, (12, 16)), ends(1, end), pd(12), A.mult, -1.0, A.add)
+        tails(1, end)
+        hold(a("WS", 2, end), a("RW", (592, 656)), A.max, end)
+        lin(a("Yc"), a("YV", (256, 512)), -1.0, 4081.0)
+        ts(a("RL"), ends(2, lo), pd(12), A.mult, -1.0, A.add)
+        scan(a("G"), a("YT", 2 * t, (7, 263)), a("YT", 2 * t + 1, (7, 263)), A.add, A.add)
         tt(a("sti"), ind(a("G", lo), a("RL")), a("Yc"), A.subtract)
         lin(a("Q"), a("sti"), -4097.0, -4097.0)
-        lin(a("ps6", (0, 1)), pf(0), 0.0, 0.0)
-        kids = [lambda k=k: ts(a("CC", quarter(k)), a("ps2", (k, 256, 4)), -1.0, A.add) for k in range(4)]
-        weave(kids[:2])
         hold(a("WF"), a("sti"), A.min)
-        kids[2]()
-        ts(a("LU"), a("WF", col15), pd(13), A.mult, -0.5625, A.add)
-        kids[3]()
-        tt(ind(a(TT, (0, 512)), a("LU")), a("Q"), a("CJ"), A.add)
+        ts(a("LU", 0, ()), a("WF", col15), pd(13), A.mult, -0.5625, A.add)
+        tt(ind(a(TT, (0, 512)), a("LU", 0, ())), a("Q"), a("CJ"), A.add)
 
         def twice(c, x=None):
             return (2 * c[0], 2 * c[1]) if x is None else (2 * c[0] + x, 2 * c[1], 2)
-        for c in halves[::-1]:
-            tt(a("ps5", twice(c)), a(TT, twice(c)), a("ps4", twice(c)), A.is_le)
-        tt(a("OT", twice(halves[1])), a(TT, twice(halves[1])), a("ps5", twice(halves[1])), A.mult)
-        scan(a("ps6", (1, 257)), a(TT, (0, 512, 2)), a(TT, (1, 512, 2)), A.max, A.max)
-        tt(a("OT", twice(halves[0])), a(TT, twice(halves[0])), a("ps5", twice(halves[0])), A.mult)
-        for f in (lambda c: tt(a("ps7", c), a("ps6", c), a("OT", twice(c, 0)), A.max),
-                  lambda c: tt(a("ps3", c), a("ps7", c), a("OT", twice(c, 1)), A.max),
-                  lambda c: tt(a("ci", c), a("ps3", c), a("PC", c), A.subtract),
-                  lambda c: ts(a("ca", c), a("ci", c), 4095, AND),
-                  lambda c: cp(a("LL", c), a("ca", c))):
-            for n in (2, 3, 0, 1):
-                f(quarter(n))
-        if t + 1 < ROUNDS:
-            hold(a("WL"), a("ps0", lo))
-        for f, c in ((ac, (OPT["split"][t], 256)), (cp, (0, OPT["split"][t]))):
+        for x in range(2):
+            lin(a("ps4", (x, 512, 2)), a("PC"), 4097.0, 4096.0)
+        lin(a("ps6", (0, 1)), pf(0), 0.0, 0.0)
+        weave(*[[None] * (OPT["skew"] * n) + [
+            lambda c=c: tt(a("OT", 0, twice(c)), a(TT, twice(c)), a("ps4", twice(c)), A.subtract),
+            lambda n=n: None if n else scan(a("ps6", (1, 257)), a(TT, (0, 512, 2)), a(TT, (1, 512, 2)), A.max, A.max),
+            lambda c=c: ts(a("OT", 1, twice(c)), a("OT", 0, twice(c)), 2 ** 24 - 1, AND),
+            lambda c=c: tt(a("ps3", c), a("ps6", c), a("PB", c), A.subtract),
+            lambda c=c: tt(a("ps5", c), a("ps3", c), a("OT", 1, twice(c, 0)), A.max),
+            lambda c=c: tt(a("ci", c), a("ps5", c), a("OT", 1, twice(c, 1)), A.max),
+            lambda c=c: ts(a("ca", c), a("ci", c), 4095, AND),
+            lambda c=c: cp(a("LL", c), a("ca", c))] for n, c in enumerate(OPT["cols"])])
+        x = OPT["split"][t]
+        for f, c in [(ac, c) for c in OPT["cols"] if c[0] >= 128] + [(ac, (x, 128))] * (x < 128) + [(cp, (0, x))]:
             f(a("XLD", (16 * c[0], 16 * c[1])), ind(win, a("LL", c)))
-        if t + 1 < ROUNDS:
-            ts(a("LE"), a("WL", col15), pd(12), A.mult, -1.0, A.add)
+        mm(a("ps7", lo), [(a("WH"), last(lo))])
+        lin(a("y1"), a("ps7", lo), 1.0 / 128, 1.0 / 256 - 0.5)
+        lin(a("W0"), a("ps7", lo), pd(3), 0.0, COPY)
+        lin(a("y2"), a("y1"), 1.0, ROUNDER)
+        lin(a("y1"), a("y2"), 1.0, -ROUNDER)
+        lin(a("HP"), a("y1"), pd(5), 0.0, COPY)
+        terms = (("W0", 0), ("HP", 0), ("y3", 1), ("t2", 0))
+        run("s", lambda: s.activation(T.sg[:], y0[0], ABS, bias=-8.0, accum_out=lc(0)[0]), (None, a("sg")[1] + lc(0)[1]), (y0,), 280)
+        lin(lc(1), lc(0), 1.0, 2048.0)
+        lin(lc(2), lc(0), -1.0, 2048.5)
+        lin(lc(3), lc(0), 0.5, 1024.0)
+        lin(a("y1"), a("IK8"), lc(1), 1.0 / 512 - 0.5)
+        lin(a("y2"), a("y1"), 1.0, ROUNDER)
+        lin(a("y3"), a("y2"), 1.0, pd(4))
+        for b in ("ps1", "ps2"):
+            mm(a(b, lo), [(a("IDfn" if n else "IDf"), a(x)) for x, n in terms[:3]], stop=b == "ps1")
+        lin(a("sg"), a("ps1", lo), -1.0, lc(2), AF.Sign)
+        lin(a("t2"), a("sg"), lc(3), lc(3))
+        mm(a("ps2", lo), [(a("IDf"), a("t2"))], start=False)
+        for k in range(4):
+            ts(a("CC", quarter(k)), a("ps2", (k, 256, 4)), -1.0, A.add)
         mine, laid = 1024 * rank, a("XLD", (0, 4096))
         if t + 1 < ROUNDS:
+            for k in range(4):
+                mm(a("ps0", quarter(k)), [(a("SEn" if n else "SE"), a(x, (k, 256, 4))) for x, n in terms])
+            hold(a("WL"), a("ps0", lo))
+            ts(a("LE"), a("WL", col15), pd(12), A.mult, -1.0, A.add)
             cp(a("LO", (64, 192)), ind(laid, a("LE", (4, 12))))
             ac(a("LO", quarter(3)), ind(laid, a("LE", (12, 16))))
             ac(a("LC", quarter(rank)), ind(laid, a("LE", (0, 4))))
             send((1, 2, 3), "e", lambda k: a("LO", quarter(k)), lambda r: a("LC", quarter(r)))
+            land("e", lambda k: (1, 2, 3), lambda r: a("LC", quarter(r)), OPT["ahead"])
         for k in sorted((1, 2, 3), key=lambda k: way(core, to(k))) + [0]:
             for f, b in ((cp, 0), (ac, 512)):
                 out = a("OB", 3 * t + k - 1, (b, b + 512)) if k else a(nx, (mine + b, mine + b + 512))
                 f(out, ind(laid, a("CC", (64 * k + b // 16, 64 * k + b // 16 + 32))))
             if k:
                 send((k,), "m%d" % t, lambda k: a("OB", 3 * t + k - 1, ()), lambda r: a(nx, (1024 * r, 1024 * r + 1024)))
+        land("m%d" % t, lambda k: (k,), lambda r: a(nx, (1024 * r, 1024 * r + 1024)), OPT["bulk"])
     first, second, near = sorted(((rank - k) % 4 for k in (1, 2, 3)), key=lambda r: way(T.cores[r], core))
     for n, r in enumerate((rank, first, near, second)):
-        dma("ys"[n % 2], a("y", (1024 * r, 1024 * r + 1024)), a("X2", (1024 * r, 1024 * r + 1024)), "dy%d" % n)
+        dma("ys"[n % 2], a("y", (1024 * r, 1024 * r + 1024)), a("X2", (1024 * r, 1024 * r + 1024)), "dy%d" % n, OPT["store"])
+    issue_all()
     for sm in sorted(total, key=lambda x: (x[:2] == "dy", x)):
         if know["g"].get(sm, 0) < total[sm]:
             g.wait_ge(T.sem[sm], total[sm])

import numpy as np
from concourse.bass import DstId, RemoteDMATransfer
from concourse.mybir import AluOpType as A, AxisListType, ActivationFunctionType as AF

ROUNDS = 2
SCRATCH = {}
DTN = {"b": "bfloat16", "f": "float32", "i": "int32", "u": "uint16"}
for _w in """X0 4096 b,X1 4096 b,X2 4096 b,XLD 4096 b,XR 4096 b,R2 512 b,DF 8192 b,AD 8192 b,wti 1 i,kmi 4 i,thi 2 i,wtf 1 f,kmf 4 f,
T4 4 f,MQ 16 f,Zx 144 b,ipart 1 i,IC 160 f,GM 128 f,IK8 256 f,PC 256 f,CJ 256 f,PI 8 i,PF 8 f,PD 24 f,WH 128 b,Zj 160 b,
ID 128 b,IDn 128 b,IDf 128 f,IDfn 128 f,SE 128 f,SEn 128 f,Zx0 144 b,Zx1 144 b,jn 8 i,CB 8x4 i,CTb 8x32 b,CTT 8x32 b,CL 8x128 b,
PM 128 f,ONE 128 b,DT 4x128 b,TI 4 i,WK 3x16 b,G8 8 f,CTR 128 f,iT 2x16 f,BO 16 f,W256 16 f,WD 256 b,RP 256 b,LC 256 b,LO 256 b,WL 256 f,LE 16 u,
U1 256 i,U 256 i,UU 256 i,UB 256 i,CA 2x256 i,CI 2x256 i,CU 2x256 u,CF 2x256 f,HP 256 f,W0 256 f,pen 4x128 b,SC 2x256 f,
RSi 256 b,RS 128 f,best 16 i,Jt 16 i,LJ 16 u,PX 512 b,FJ 256 b,WJ 256 b,FI 16x8 i,FB 4x4x32 b,RT 512 b,SH 8x256 f,SCN 16x128 i,
PZ 2x16 i,FP 2x256 b,FQ 2x256 b,Y0 768 b,C16 256 f,PB 256 f,NTW 16 f,SLf 24 f,NI 3x16 i,RL 16 u,Lc 4 f,y1 256 f,y2 256 f,
sg 256 f,t2 256 f,CC 256 u,G 256 f,Yc 256 f,sti 256 f,WF 256 f,y3 256 f,Q 256 f,LU 3x16 u,ci 256 i,ca 256 i,LL 256 u,PW 3x512 b,ZW 4x512 f,
RW 656 b,PT 512 b,ZT 480 f,YV 512 f,WS 3x256 b,LV 10x16 u,YT 4x528 f,TT0 512 f,TT1 512 f,OT 2x512 i,OB 6x1024 b""".replace("\n", "").split(","):
    _n, _s, _d = _w.split()
    SCRATCH[_n] = ("sbuf", [128] + [int(z) for z in _s.split("x")], DTN[_d])
for _b in range(8):
    SCRATCH["ps%d" % _b] = ("psum", [128, 512], "float32")
SEMAPHORES = (["cv", "cs", "ct", "cg", "dwt", "dkm", "dth", "e_l1", "e_1", "e_2", "e_3"] + ["d%s%d" % (x, q) for x in "xy" for q in range(4)]
              + ["m%d_%s%d" % (t, x, k) for t in range(ROUNDS) for k in (1, 2, 3) for x in ("", "l")])
P24 = 16777216.0
ROUNDER = 12582912.0
HOLD = 65536.0
BLOCK, STEPS = 32, 7
WAKE, GATHER, SCATTER = 270, 1.4, 3.8
COPY, ABS = AF.Copy, AF.Abs
SHR, AND = A.arith_shift_right, A.bitwise_and
NUM = {n: np.arange(int(np.prod(s[1][1:]))).reshape(s[1][1:]) for n, s in SCRATCH.items()}
OPT = dict(split=(110, 110), help=(32, 32), passes=(None, 100, None), load=(3000, 3700, 4400, 5100), ahead=(3800, 3800, 3800),
           bulk=(3000, 4800, 3500), store=4000, pieces=((0, 32), (32, 64)), first=(0, 1), lag=2, mid=(7, 7), late=2, behind=0, flags=(0, 2, 3, 4, 5, 6, 7, 9), parts=0, order=(0, 1, 2, 3),
           tails=((0, 96), (96, 192)), skew=2, cols=((192, 256), (128, 192), (64, 128), (0, 64)))


def rank_program(g, core, T, topo):
    rank = T.rank_of(core)
    if rank is None:
        return
    v, s, te = g.vector, g.scalar, g.tensor

    def a(n, *ix):
        ix = tuple((slice(*z) if len(z) else slice(None)) if isinstance(z, tuple) else z for z in ix)
        ap = T[n][(slice(None),) + ix]
        if n not in NUM:
            return ap, []
        return ap, [(n, NUM[n][ix].reshape(-1))]

    def ind(w, o):
        return w[0].indirect(o[0]), w[1] + o[1], 16 * o[1][0][1].size
    eng = {"v": v, "s": s, "t": te, "g": g, "y": g.sync}
    cnt, total, know, snap, ev = {}, {}, {e: {} for e in eng}, {}, []
    wr = {n: np.full(NUM[n].size, -1) for n in NUM}
    rd = {n: {} for n in NUM}
    bank = {n: {} for n in NUM if n[:2] == "ps"}

    def need(e, reads, writes, adds=False):
        ids, own = set(), "c" + e
        for w, lst in ((0, reads), (1, writes)):
            for n, c in lst:
                ids.update(i for i in np.unique(wr[n][c]).tolist() if not (w and adds and ev[i][0] == own))
                if w:
                    for r in rd[n].values():
                        ids.update(np.unique(r[c]).tolist())
                if n in bank:
                    ids.update(i for sm, i in bank[n].items() if sm != own)
        nd, kn = {}, know[e]
        for i in ids:
            if i >= 0:
                nd[ev[i][0]] = max(nd.get(ev[i][0], 0), ev[i][1])
        for sm, val in sorted(nd.items(), key=lambda z: z[0] == own):
            if kn.get(sm, 0) < val:
                eng[e].wait_ge(T.sem[sm], val)
                for s2, v2 in list(snap[(sm, val)].items()) + [(sm, val)]:
                    kn[s2] = max(kn.get(s2, 0), v2)

    def done(e, sm, val, reads, writes):
        ev.append((sm, val))
        snap[(sm, val)] = dict(know[e]) if e else {}
        total[sm] = val
        for n, c in reads:
            rd[n].setdefault(sm, np.full(NUM[n].size, -1))[c] = len(ev) - 1
        for n, c in writes:
            wr[n][c] = len(ev) - 1
            for r in rd[n].values():
                r[c] = -1
        for n, c in reads + writes:
            if n in bank:
                bank[n][sm] = len(ev) - 1

    calls = []

    def run(e, call, out, ins, cycles, adds=False):
        reads = [z for x in ins if isinstance(x, tuple) for z in x[1]]

        def issue():
            need(e, reads, out[1], adds)
            sm = "c" + e
            cnt[sm] = cnt.get(sm, 0) + 1
            call().then_inc(T.sem[sm], 1)
            done(e, sm, cnt[sm], reads, out[1])
        calls.append((e, issue, reads, out[1], cycles, cycles, [], adds))

    def dma(e, out, in_, sm, cycles):
        def issue():
            need(e, in_[1], out[1])
            eng[e].dma_start(out[0], in_[0]).then_inc(T.sem[sm], 16)
            done(e, sm, 16, in_[1], out[1])
        calls.append((e, issue, in_[1], out[1], 60, cycles, [], False))

    def issue_all():
        w = {n: np.full(NUM[n].size, -1) for n in NUM}
        r = {n: [] for n in NUM}
        pe, pre = {}, []
        for i, (e, _, reads, writes, _, _, before, adds) in enumerate(calls):
            p = {j: calls[j][4] - calls[j][5] for j in before}
            for n, c in writes:
                keep = []
                for j, c2 in r[n]:
                    m = np.isin(c2, c)
                    if m.any():
                        p[j] = WAKE
                    if not m.all():
                        keep.append((j, c2[~m]))
                r[n] = keep
                if e == "t":
                    p.setdefault(pe.get(n, -1), 0)
                    pe[n] = i
                p.update({j: 0 if adds and calls[j][0] == e else WAKE for j in np.unique(w[n][c]).tolist()})
            for n, c in reads:
                p.update({j: WAKE for j in np.unique(w[n][c]).tolist()})
                r[n].append((i, c))
            for n, c in writes:
                w[n][c] = i
            p.pop(-1, None)
            p.pop(i, None)
            pre.append(p)
        post = [{} for c in calls]
        for i, p in enumerate(pre):
            for j, d in p.items():
                post[j][i] = d

        def place(order, deps, back):
            end, busy = {}, {}
            for i in order:
                e, hold, span = calls[i][0], calls[i][4], calls[i][5]
                uses = [(e, span - hold if back else 0, hold, None)] + [(n, -WAKE, span + 2 * WAKE, e) for n in
                                                                        {n for n, c in calls[i][2] + calls[i][3] if n in bank}]
                at, moved = max([0.0] + [end[j] + d for j, d in deps[i].items()]), True
                while moved:
                    moved = False
                    for n, off, length, own in uses:
                        for x, y, who in busy.get(n, ()):
                            if y > at + off + 0.01 and x < at + off + length and (own is None or who != own):
                                at, moved = y - off, True
                end[i] = at + span
                for n, off, length, own in uses:
                    busy.setdefault(n, []).append((at + off, at + off + length, e) if own is None else (at, at + span, e))
            return end

        def eager(order, wait):
            rank_, left, ready = {i: n for n, i in enumerate(order)}, [len(p) for p in pre], [0.0] * len(calls)
            end, free, held, some = {}, {}, {}, [i for i in order if not pre[i]]
            banks = [{n for n, x in c[2] + c[3] if n in bank} for c in calls]
            while some:
                at = {i: max([free.get(calls[i][0], 0.0), ready[i]] + [held[n][1] + WAKE for n in banks[i] if n in held and held[n][0] != calls[i][0]])
                      for i in some}
                i = min(some, key=lambda i: at[i])
                i = min((j for j in some if calls[j][0] == calls[i][0] and at[j] <= at[i] + wait), key=lambda j: rank_[j])
                some.remove(i)
                free[calls[i][0]], end[i] = at[i] + calls[i][4], at[i] + calls[i][5]
                for n in banks[i]:
                    held[n] = (calls[i][0], end[i])
                for j, d in post[i].items():
                    ready[j], left[j] = max(ready[j], end[i] + d), left[j] - 1
                    if left[j] == 0:
                        some.append(j)
            return end
        order, best = list(range(len(calls))), None
        for n, wait in enumerate(OPT["passes"]):
            end = place(order, pre, False) if wait is None else eager(order, wait)
            if best is None or max(end.values()) < max(best.values()):
                best = end
            back = place(sorted(order, key=lambda i: (-end[i], -i)), post, True)
            order = sorted(order, key=lambda i: (-back[i], i))
        OPT["est"] = max(best.values())
        for i in sorted(order, key=lambda i: (best[i] - calls[i][5], i)):
            calls[i][1]()

    def z(x):
        return x[0] if isinstance(x, tuple) else x

    def size(out, x, rate, fixed=60):
        if len(out) > 2:
            return fixed + SCATTER * out[2]
        if len(x) > 2:
            return fixed + GATHER * x[2]
        return max(64, rate * x[1][0][1].size)

    def fast(*xs):
        return 0.5 if all(SCRATCH[x[1][0][0]][2] in ("bfloat16", "uint16") for x in xs) else 1

    def ts(out, x, s1, o0, s2=None, o1=None):
        if o1 is None:
            run("v", lambda: v.tensor_scalar(out[0], x[0], z(s1), None, o0), out, (x, s1), size(out, x, fast(out, x)))
        else:
            run("v", lambda: v.tensor_scalar(out[0], x[0], z(s1), z(s2), o0, o1), out, (x, s1, s2), size(out, x, fast(out, x)))

    def tt(out, x, y, o):
        run("v", lambda: v.tensor_tensor(out[0], x[0], y[0], o), out, (x, y),
            size(out, x, 1 if x[1][0][0] in bank or y[1][0][0] in bank else 2))

    def cp(out, x):
        run("v", lambda: v.tensor_copy(out[0], x[0]), out, (x,), size(out, x, fast(out, x)))

    def ac(out, x, f=COPY):
        run("s", lambda: s.activation(out[0], x[0], f), out, (x,), size(out, x, 1, 78))

    def lin(out, x, scale, bias, f=AF.Identity):
        run("s", lambda: s.activation(out[0], x[0], f, bias=z(bias), scale=z(scale)), out, (x, bias, scale), size(out, x, 1, 78))

    def tr(out, x):
        run("v", lambda: v.transpose(out[0], x[0]), out, (x,), size(out, x, fast(x)))

    def ms(out, c):
        run("v", lambda: v.memset(out[0], c), out, (), size(out, out, fast(out)))

    def red(out, x, o):
        run("v", lambda: v.tensor_reduce(out[0], x[0], AxisListType.X, o), out, (x,), size(out, x, 1))

    def scan(out, x, y, o0, o1, init=0.0):
        run("v", lambda: v.tensor_tensor_scan(out[0], x[0], y[0], z(init), o0, o1), out, (x, y, init), size(out, x, fast(out, x, y)))

    def iota(out, pat, base=0, cm=0):
        run("g", lambda: g.iota(out[0], pat, base, cm, allow_small_or_imprecise_dtypes=True), out, (), 156 + 2 * out[1][0][1].size)

    def mm(out, prs, start=True, stop=True, each=False):
        def call():
            r = None
            for n, p in enumerate(prs):
                r = te.matmul((p[2] if len(p) > 2 else out)[0], p[0][0], p[1][0], each or start and n == 0,
                              each or stop and n == len(prs) - 1)
            return r
        run("t", call, out, [x for p in prs for x in p[:2]],
            sum(max(min(64, p[0][1][0][1].size), p[1][1][0][1].size) * (0.5 if fast(p[1]) < 1 else 2) for p in prs), not start)

    def hold(out, x, o=A.max, c=(0, 256)):
        scan(out, a("WD", c), x, A.mult, o)

    def pf(n):
        return a("PF", (n, n + 1))

    def pd(n):
        return a("PD", (n, n + 1))

    def lc(n):
        return a("Lc", (n, n + 1))

    def weave(*lists):
        for n in range(max(len(x) for x in lists)):
            for x in lists:
                if n < len(x) and x[n]:
                    x[n]()

    dma("y", a("wti"), a("wt"), "dwt", 2300)
    dma("s", a("kmi"), a("km"), "dkm", 2300)
    dma("s", a("thi"), a("th"), "dth", 2500)
    for n, q in enumerate(OPT["order"]):
        dma("y", a("X0", (1024 * q, 1024 * q + 1024)), a("gen0", (1024 * q, 1024 * q + 1024)), "dx%d" % q, OPT["load"][n])
        calls[-1][6].append(len(calls) - 2 - 2 * (n == 0))
    ip, q15 = a("ipart"), a("MQ", (15, 16))
    iota(ip, [[0, 1]], 0, 1)
    iota(a("GM"), [[16, 8], [0, 16]])
    iota(a("IC"), [[1, 160]])
    for n, m in enumerate((15, 112, 31, 111)):
        ts(a("PI", (n, n + 1)), ip, m, AND)
    ts(a("PI", (4, 5)), ip, 4, SHR, 1, AND)
    ts(a("PI", (5, 6)), ip, 5, SHR)
    cp(pf(6), ip)
    cp(a("PF", (0, 6)), a("PI", (0, 6)))
    ts(a("IDf"), a("IC", (0, 128)), pf(6), A.is_equal)
    cp(a("wtf"), a("wti"))
    cp(a("kmf"), a("kmi"))
    ts(a("WH"), a("GM"), pf(1), A.is_equal, a("wtf"), A.mult)
    ac(a("ID"), a("IDf"))
    lin(a("IDn"), a("IDf"), -1.0, 0.0)

    def for_probes():
        lin(pd(6), pf(4), 4.0, pf(5))
        lin(pd(0), pd(6), 16.0, pf(0))
        for x, m in enumerate((4064, 31)):
            ts(a("TI", (2 * x, 2 * x + 2)), a("thi"), m, AND)
            ts(a("T4", (2 * x, 2 * x + 2)), a("TI", (2 * x, 2 * x + 2)), -4 * P24, A.mult, 2 * P24 * x, A.add)
        ts(a("PM"), a("IC", (0, 128)), pd(0), A.is_equal)
        ts(a("G8"), a("IC", (0, 8)), pd(6), A.is_equal)
        iota(a("ONE"), [[0, 128]], 1)
        for n in range(4):
            lin(a("DT", n, ()), a("PM"), a("T4", (n, n + 1)), 0.0, COPY)
        for n, x in enumerate((1.0, 2.0, -1.0)):
            lin(a("WK", n, (0, 8)), a("G8"), 4096.0 * x, 0.0)
            lin(a("WK", n, (8, 16)), a("G8"), 4 * P24 * x, 0.0)
        iota(a("RSi"), [[0, 16], [1, 16]])
        lin(a("RS"), a("RSi", (0, 128)), -2 * P24, 2 * P24, AF.Relu)

    def for_links():
        iota(a("iT"), [[1, 2], [128, 2], [0, 8]], 0, 1)
        iota(a("FB"), [[0, 512]])
        iota(a("FB", (), (), 20), [[128, 2], [0, 8]], 0, 1)
        iota(a("FB", (), (), 21), [[0, 16]], 1)
        iota(a("jn"), [[32, 8]])
        iota(a("CTb", (), 21), [[-16 * BLOCK, 8]], 4096)
        ms(a("CTb", (), (22, 32)), 0.0)
        for f, c in ((16, 4096.0), (17, 1048576.0), (18, 1.0), (19, P24), (20, 16.0)):
            ms(a("CTb", (), f), c)
        ts(a("jn"), a("jn"), pf(2), A.add)
        for f in range(4):
            ts(a("CB", (), f), a("jn"), 2 * f, SHR, 3, AND)
        for x in range(4):
            ts(a("CTb", (), (4 * x, 4 * x + 4)), a("CB"), float(x), A.not_equal, P24, A.mult)
        tr(a("CTT"), a("CTb"))
        ts(a("PD", (8, 12)), a("IC", (0, 4)), pf(5), A.is_equal)
        for n in range(4):
            lin(a("CL", (), (32 * n, 32 * n + 32)), a("CTT"), pd(8 + n), 0.0, COPY)
        lin(pd(16), pf(2), 16.0, float(4081 * 4096 + 15))
        lin(a("CTR"), a("IC", (0, 128)), 0.0, pd(16))
        iota(a("FP"), [[0, 512]])
        iota(a("BO"), [[BLOCK, 8], [0, 2]], -256)
        lin(a("RP"), a("RSi"), 1.0, 0.0, AF.Sign)
        lin(pd(1), pf(3), 1.0, 16.0)
        lin(pd(2), pf(4), -1.0, 1.0)
        ts(a("Zx"), a("IC", (0, 144)), pd(1), A.is_equal)
        lin(a("Zx0"), a("Zx"), pd(2), 0.0, COPY)
        lin(a("Zx1"), a("Zx"), pf(4), 0.0, COPY)
        lin(pd(7), pf(6), 1.0, 9.0)
        ts(pd(17), pf(2), 22.0, A.is_equal)
        ts(a("Zj"), a("IC"), pd(7), A.is_equal, pd(17), A.mult)

    def for_chains():
        lin(pd(15), pf(0), 1.0, 1.0)
        ts(a("MQ"), a("IC", (0, 16)), pf(0), A.is_equal)
        ts(a("FJ"), a("RSi"), pf(0), A.not_equal)
        ts(a("WJ"), a("RSi"), pd(15), A.is_equal, HOLD, A.mult)
        tt(a("WD"), a("FJ"), a("WJ"), A.max)
        lin(pd(12), q15, 1.0 - 1.0 / HOLD, 1.0 / HOLD)
        lin(pd(14), q15, 1.0 - HOLD, HOLD)
        iota(a("PX", (256, 512)), [[1, 256]])
        iota(a("Y0", (256, 512)), [[0, 256]])
        iota(a("PW", (), (256, 512)), [[0, 3], [1, 256]])
        iota(a("ZW", (), (256, 512)), [[0, 1024]])
        iota(a("PC"), [[16, 256]])
        iota(a("IK8"), [[1, 256]])
        iota(a("RW", (0, 256)), [[1, 256]], 1)
        iota(a("YV", (0, 256)), [[0, 256]])
        iota(a("CJ"), [[16, 256]], 15)
        lin(a("IK8"), a("IK8"), 1.0 / 256, 0.0)
        lin(a("PC"), a("PC"), 1.0, pf(0))
        lin(pd(20), pd(14), 257.0, 0.0)
        lin(pd(4), pf(0), 1.0, -4096.0 - ROUNDER)
        lin(a("IDfn"), a("IDf"), -1.0, 0.0)
        ts(a("SE"), a("GM"), pf(1), A.is_equal, q15, A.mult)
        lin(a("SEn"), a("SE"), -1.0, 0.0)
        lin(pd(13), pd(12), -0.125, 0.0)
        lin(a("W256"), a("PC", (0, 16)), pd(14), pd(20))
        lin(pd(21), pd(14), 256.0, 0.0)
        lin(a("PB"), a("PC"), 4097.0, 4096.0 - P24)
        iota(a("RW", (448, 528)), [[2, 80]], 258)
        iota(a("PT", (0, 256)), [[1, 256]], -256)
        iota(a("ZT", (0, 256)), [[0, 256]])
        iota(a("C16"), [[0, 256]], 16)
        for t in range(ROUNDS):
            iota(a("YT", (2 * t, 2 * t + 2), (0, 272)), [[0, 544]])
            iota(a("TT%d" % t), [[0, 512]])
    lo, col15, halves = (0, 256), (15, 256, 16), ((0, 128), (128, 256))

    def quarter(n):
        return (64 * n, 64 * n + 64)

    def to(k):
        return T.cores[(rank + k) % 4]

    def engines(src, k):
        dst = T.cores[(T.rank_of(src) + k) % 4]
        es = topo.engines(src, dst)
        if topo.chip(src) == topo.chip(dst):
            es = [x for x in es if x not in topo.engines(src, T.cores[(T.rank_of(src) + 1) % 4])]
        return es

    def way(src, dst):
        return 2 if topo.chip(src) == topo.chip(dst) else int(topo.die(src) == topo.die(dst))

    def share(c, ks, k):
        alike = {m: [x for x in ks if engines(c, x) == engines(c, m)] for m in ks}
        n = min(len(engines(c, m)) // len(alike[m]) for m in ks)
        return engines(c, k)[n * alike[k].index(k):][:n]

    def send(ks, name, src, dst):
        reads = [x for k in ks for x in src(k)[1]]
        ws = [(topo.addr(to(k)), sum(1 << x for x in share(core, ks, k)), T.sem["%s_%d" % (name, k)], src(k)[0]) for k in ks]
        left, there = "%s_l%d" % (name, ks[0]), dst(rank)[0]

        def issue():
            need("g", reads, [])
            if len(ks) == 1:
                ad, mask, sem, x = ws[0]
                g.remote_dma(there, x, sem, T.sem[left], ad[1], ad[0], mask)
            else:
                g.remote_dma_fused([RemoteDMATransfer(dst_ids=[DstId(rid=ad[0], pnc=ad[1])], dma_engine_mask=mask, remote_sem=sem,
                                                      src=x, dst=there) for ad, mask, sem, x in ws], local_sem=T.sem[left])
            total[left] = sum(len(share(core, ks, k)) for k in ks)
        calls.append(("g", issue, reads, [], 300, 300, sent[-1:], False))
        sent.append(len(calls) - 1)

    def land(name, ks, dst, cycles):
        for k in (1, 2, 3):
            fr = (rank - k) % 4
            n = len(share(T.cores[fr], ks(k), k))
            calls.append(("w%s%d" % (name, k), lambda k=k, n=n, w=dst(fr)[1]: done("", "%s_%d" % (name, k), n, [], w), [], dst(fr)[1], 0,
                          cycles[way(T.cores[fr], core)], sent[-1:], False))
    sent = []

    for t in range(ROUNDS):
        xn, nx = "X%d" % t, "X%d" % (t + 1)
        win = a(xn, (0, 4096))
        own = rank if t else 0
        vb = own // 2 if OPT["first"][t] else 1
        sb = 1 - vb
        s0, v0, aid = 128 * sb, 128 * vb, 128 - OPT["help"][t]

        def last(i):
            return a("LC", i) if t else a(xn, (16 * i[0] + 15, 16 * i[1], 16))

        def hashes(i):
            j = (256 + i[0], 256 + i[1])
            b = "ps%d" % (7 if t or OPT["order"].index(i[0] // 64) % 2 else 3)
            return ([lambda: mm(a(b, i), [(a("WH"), last(i))]) if t == 0 or i[0] == 64 * own else None,
                     lambda: cp(a("U1", i), a(b, i)),
                     lambda: ts(a("U", i), a("U1", i), 4095, AND),
                     lambda: tt(a("UU", i), a("U", i), a("U", i), A.mult),
                     lambda: ts(a("UB", i), a("UU", i), 5, SHR),
                     lambda: ts(a("ps6", i), a("U", i), a("kmf", (2 * t, 2 * t + 1)), A.mult),
                     lambda: ts(a("ps6", j), a("U", i), a("kmf", (2 * t + 1, 2 * t + 2)), A.mult)]
                    + [lambda h=h, f=f: f(h) for h in range(2) for f in (
                        lambda h: tt(a("CA", h, i), a("ps6", j if h else i), a("UB", i), A.add),
                        lambda h: ts(a("CI", h, i), a("CA", h, i), 4095, AND),
                        lambda h: cp(a("CU", h, i), a("CI", h, i)))])

        def repeats(i, b):
            n = 16 * (i[1] - i[0])
            mm(a(b, (0, n)), [(a("ID"), last(i), a(b, (x, n, 16))) for x in range(16)], each=True)
            ac(a("XR", (16 * i[0], 16 * i[1])), a(b, (0, n)))
        helped = [(s0 + x, s0 + min(x + 32, 128)) for x in range(aid, 128, 32)]
        v1, v2 = (64 * own, 64 * (own ^ 1)) if own // 2 == vb else (v0, v0 + 64)
        xr = [(v1, v1 + 32), (v1 + 32, v1 + 64)] + helped + [(v2, v2 + 32), (v2 + 32, v2 + 64)]
        if t:
            far = [quarter(x) for x in (2 * sb, 2 * sb + 1, own ^ 1)]
            weave(hashes(quarter(own)))
            mm((None, [x for i in far for x in a("ps7", i)[1]]), [(a("WH"), last(i), a("ps7", i)) for i in far], each=True)
            weave(*[hashes(i) for i in far])
        else:
            weave(*[[None] * (OPT["late"] * n) + hashes(quarter(q)) for n, q in enumerate(OPT["order"])])
        for n in (2 * sb, 2 * sb + 1):
            for x in range(2):
                ac(a("R2", (128 * n + x, 128 * n + 128, 2)), last(quarter(n)))
        for n, i in enumerate(xr):
            repeats(i, "ps%d" % ((4 + n) % 6))
        if t == 0:
            for_probes()

        def span(h, i):
            return (4096 * h + 16 * i[0], 4096 * h + 16 * i[1])

        def keys(b, h, c=(0, 256)):
            return a("ps%d" % (2 * b + h), c)

        def opened(b, h):
            mm(keys(b, h, (128, 256)), [(a("ONE"), a("DT", 2 * x + h, ())) for x in range(2)], stop=False)
            o, x = a("CF", h, halves[b]), a("CI", h, halves[b])
            run("g", lambda: g.affine_select(o[0], x[0], [[0, 128]], A.is_ge, 0.0, 0, 0), o, (x,), 205 + 256)
            mm(keys(b, h, (0, 128)), [(a("CF", h, halves[b]), a("PM"))], False, False)

        def sums(b, h, x, w, stop, i=None):
            i = i or halves[b]
            d, ps = span(h, i), T["ps%d" % (2 * b + h)]
            mm(keys(b, h), [(a(x, (d[0] + p, d[1], 16)), a("WK", w, ()), (ps[i[0] % 128:(i[1] - 1) % 128 + 1, p:256:16],))
                            for p in range(16)], False, stop)

        def less(h, i):
            tt(a("DF", span(h, i)), ind(win, a("CU", h, i)), a("XR", (16 * i[0], 16 * i[1])), A.subtract)

        def plain(h, i, b):
            d, n = span(h, i), 16 * (i[1] - i[0])
            return [lambda: ac(a("DF", d), ind(win, a("CU", h, i))),
                    lambda: mm(a(b, (0, n)), [(a("IDn"), a("R2", (2 * i[0], 2 * i[1])), a(b, (x, n, 8))) for x in range(8)], stop=False),
                    lambda: mm(a(b, (0, n)), [(a("ID"), a("DF", d))], False),
                    lambda: ac(a("AD", d), a(b, (0, n)), ABS)]

        def ended(b, h):
            parts = [i for x, i in by_v if x] if b == vb and h and OPT["parts"] else [None]
            for i in parts[:-1]:
                sums(b, h, "AD", 1, False, i)
            if b == vb:
                sums(b, h, "DF", 2, False)
            sums(b, h, "AD", int(b == vb), True, parts[-1])
            bests(b, h)

        def bests(b, h):
            ac(a("pen", 2 * b + h, ()), keys(b, h, (128, 256)), AF.Relu)
            tt(a("CF", h, halves[b]), keys(b, h, (0, 128)), a("pen", 2 * b + h, ()), A.max)
            scan(a("SC", h, halves[b]), a("RS"), a("CF", h, halves[b]), A.max, A.min)

        by_s = [(h, (s0 + x, s0 + min(x + 32, w))) for h, w in ((0, aid), (1, 128)) for x in range(0, w, 32)]
        by_v = ([(0, (v1, v1 + 64))] + [(0, i) for i in helped] + [(0, (v2, v2 + 64)), (1, (v1, v1 + 64))]
                + [(1, (v2 + x, v2 + y)) for x, y in OPT["pieces"]])
        by_s = [plain(h, i, "ps%d" % (4 + n % 4)) for n, (h, i) in enumerate(by_s)]
        lag = OPT["lag"]

        def after(h, i):
            if i in helped:
                ac(a("AD", span(h, i)), a("DF", span(h, i)), ABS)
            else:
                ts(a("AD", span(h, i)), a("DF", span(h, i)), 0.0, A.max)
        for n in range(len(by_s) + lag):
            if n < len(by_s):
                weave(by_s[n][:3])
            if n >= lag:
                by_s[n - lag][3]()
            if n < len(by_v):
                less(*by_v[n])
            if 0 < n <= len(by_v):
                after(*by_v[n - 1])
            if n < 2:
                opened(sb, n)
                opened(vb, n)
            if n == OPT["mid"][0]:
                ended(sb, 0)
            if n == OPT["mid"][1]:
                ended(vb, 0)
        ended(sb, 1)
        ended(vb, 1)
        if t == 0:
            for_links()
        be = a("best")
        tt(be, a("SC", 0, col15), a("SC", 1, col15), A.min)
        for f in range(4):
            ts(a("FI", (), f), be, 4 + 2 * f, SHR, 3, AND)
        ts(a("Jt"), be, 4, SHR, 255, AND)
        ts(a("FI", (), 4), be, 12, SHR, 255, AND)
        ts(a("FI", (), 5), be, 20, SHR, 31, AND)
        ts(a("FI", (), 6), be, 1, SHR, 7, AND)
        for x in range(4):
            ts(a("FB", (), (), (4 * x, 4 * x + 4)), a("FI", (), (0, 4)), float(x), A.is_equal)
        tt(a("FB", (), (), 19), a("Jt"), a("iT", 0, ()), A.is_le)
        tt(a("FB", (), (), 22), a("Jt"), a("iT", 1, ()), A.max)
        cp(a("FB", (), (), (16, 19)), a("FI", (), (4, 7)))
        for e in range(2):
            mm(a("ps%d" % (4 + e), lo), [(a("FB", 2 * b + e, (), ()), a("ID"), a("ps%d" % (4 + e), halves[b])) for b in range(2)], each=True)
            (cp, ac)[e](a("RT", (256 * e, 256 * e + 256)), a("ps%d" % (4 + e), lo))
        def pieces(bs):
            for b, e in [(0, 0), (1, 0), (0, 1), (1, 1)] + [(b, e) for b in bs for e in range(2)]:
                w = 32 * b + 32
                yield (b, e, "ps%d" % e, 32 * b, w) if b < 2 else (b, e, "ps%d" % b, w * e, w)
        for b, e, ps, o, w in pieces((2, 7, 3, 6, 5, 4)):
            mm(a(ps, (o, o + w)), [(a("CL", b, ()), a("RT", (256 * e, 256 * e + w)))])
            if b > 3 and e:
                ac(a("SH", b, (0, w)), a(ps, (1, 2 * w, 2)))
        for b, e, ps, o, w in pieces((2, 3, 7, 6, 5, 4)):
            if b > 3:
                scan(a("SCN", 2 * b + e, (128 - w // 2, 128)), a(ps, (o, o + w, 2)),
                     a("SH", b, (w // 2 * e, w // 2 * (e + 1))), A.min, A.min, pd(16))
            else:
                scan(a("SCN", 2 * b + e, (128 - w, 128)), a(ps, (o, o + w)), a("CTR", (0, w)), A.min, A.min, pd(16))
        ts(a("PZ", 0, ()), a("SCN", (), 127), 4, SHR, 255, AND)
        ts(a("PZ", 1, ()), a("SCN", (), 127), 15, AND)
        tt(a("FP", 0, (0, 256, 16)), a("PZ", 0, ()), a("BO"), A.add)
        ts(a("FP", 1, (0, 256, 16)), a("PZ", 1, ()), -1.0, A.mult, 15.0, A.add)
        for x in range(2):
            mm(a("ps3", (x, 16, 2)), [(a("Zx%d" % x, (16 - 16 * e, 144 - 16 * e)), a("FP", 0, (16 * e, 256, 32))) for e in range(2)])
        for n in range(2):
            scan(a("FQ", n, ()), a("RP"), a("FP", n, ()), A.mult, A.add)
        tr(a("PX", lo), a("FQ", 0, ()))
        ts(a("LV", 0, ()), a("ps3", (0, 16)), 256.0, A.add)
        for n in (0, 512):
            tr(a("Y0", (n, n + 256)), a("FQ", 1, ()))
        if t == 0:
            for_chains()
            lin(pd(3), pf(0), -1.0, 0.0)
            lin(pd(5), pf(0), 128.0, 0.0)

        y0 = a("Y0", lo)

        def past(c):
            return (256 + c[0], 256 + c[1])

        def lst(n, c):
            return a("LV", n, (c[0] // 16, c[1] // 16))

        def ends(n, c):
            return a("WS", n, (c[0] + 15, c[1], 16))

        def summed(n, c):
            rest = a("ZW", (n - 2) % 4, ()) if n > 2 else a("Y0", (0, 512))
            out = a("YV", past(c)) if c[1] <= BLOCK else a("ZT", past(c)) if n == STEPS and c[0] == 0 else a("ZW", n % 4, c)
            tt(out, ind(rest, lst(n - 1, c)), a("ZW", (n - 1) % 4, c) if n > 1 else a("Y0", (512 + c[0], 512 + c[1])), A.add)
        mm(a("ps0", (0, 16)), [(a("Zj", (31 - 16 * e - q, 159 - 16 * e - q)), a("RT", (256 * e + q, 256 * e + 256, 16)))
                               for e in range(2) for q in range(16)])
        followed = [lambda: cp(a("LJ"), a("ps0", (0, 16))),
                    lambda: ac(a("FJ", halves[0]), ind(a("PX"), a("LJ", (0, 8)))),
                    lambda: ac(a("FJ", halves[1]), ind(a("PX"), a("LJ", (8, 16)))),
                    lambda: hold(a("WJ"), a("FJ"), A.add),
                    lambda: ts(a("NI", 0, ()), a("WJ", col15), pd(12), A.mult),
                    lambda: ts(a("NI", 1, ()), a("NI", 0, ()), 255, AND),
                    lambda: tt(a("NI", 2, ()), a("NI", 1, ()), a("PC", (0, 16)), A.is_equal),
                    lambda: tt(a("NTW"), a("NI", 2, ()), a("W256"), A.mult),
                    lambda: ts(a("SLf", (16, 20)), a("NTW", (12, 16)), pd(21), A.subtract)]
        for n in range(1, STEPS + 1):
            pw, out = a("PW", (n - 1) % 3, ()) if n > 1 else a("PX"), a("PW", n % 3, lo) if n < STEPS else a("PT", past(lo))
            ac(out, ind(pw, lst(max(n - 2, 0), lo)))
            if n == STEPS:
                lin(a("RW", past((0, BLOCK))), ind(pw, lst(n - 2, (0, BLOCK))), 1.0, 257.0)
            hold(a("WS", n % 2, ()), out, A.add)
            ts(lst(n, lo), ends(n % 2, lo), pd(12), A.mult, 256.0, A.add)
            for x in halves if n < STEPS else ((0, BLOCK), halves[0], halves[1]):
                summed(n, x)
            weave(followed[OPT["flags"][n - 1]:OPT["flags"][n]])
        up = halves[1]
        ac(a("PW", 0, up), ind(a("PT"), lst(STEPS, up)))
        hold(a("WS", 0, up), a("PW", 0, up), A.add, up)
        ts(lst(STEPS + 1, up), ends(0, up), pd(12), A.mult, 256.0, A.add)
        ac(a("ZT", (384, 480)), a("ZW", STEPS % 4, (128, 224)))
        tt(a("ZW", 0, up), ind(a("ZT", (0, 480)), lst(STEPS, up)), a("ZW", STEPS % 4, up), A.add)
        blocks = [(32, 64), (64, 96), (96, 128), (128, 192), (192, 256)]
        end, TT = blocks[-1], "TT%d" % t
        tt(a("SLf", (20, 24)), ends(0, end), a("SLf", (16, 20)), A.max)
        ts(a("LU", 1, (12, 16)), a("SLf", (20, 24)), pd(12), A.mult, 256.0, A.add)

        def tails(n, c):
            tt(ind(a("YT", 2 * t + n, (8, 520)), a("LU", 2 * n, (c[0] // 16, c[1] // 16))), a("YV", past(c)), a("C16", c), A.add)
        for c in blocks:
            n = STEPS + c[0] // 128
            if c == end:
                ac(a("RW", (528, 592)), ind(a("RW", (0, 528)), a("LU", 1, (12, 16))))
            ac(a("RW", past(c) if c != end else (592, 656)), ind(a("RW", (0, 256 + c[0])), lst(n, c)))
            tt(a("YV", past(c)), ind(a("YV", (0, 256 + c[0])), lst(n, c)), a("ZW", 0, c) if c[0] // 128 else a("ZT", past(c)), A.add)
            for x in OPT["tails"]:
                if x[1] + OPT["behind"] == c[1] or x[1] + OPT["behind"] > c[1] == 256:
                    w = (x[0] // 16, x[1] // 16)
                    hold(a("WS", 2, x), a("RW", past(x)), A.max, x)
                    tt(a("SLf", w), ends(2, x), a("NTW", w), A.max)
                    ts(a("LU", 0, w), a("SLf", w), pd(12), A.mult, -1.0, A.add)
                    tails(0, x)
        hold(a("WS", 1, end), a("RW", (528, 592)), A.max, end)
        ts(a("LU", 2, (12, 16)), ends(1, end), pd(12), A.mult, -1.0, A.add)
        tails(1, end)
        hold(a("WS", 2, end), a("RW", (592, 656)), A.max, end)
        lin(a("Yc"), a("YV", (256, 512)), -1.0, 4081.0)
        ts(a("RL"), ends(2, lo), pd(12), A.mult, -1.0, A.add)
        scan(a("G"), a("YT", 2 * t, (7, 263)), a("YT", 2 * t + 1, (7, 263)), A.add, A.add)
        tt(a("sti"), ind(a("G", lo), a("RL")), a("Yc"), A.subtract)
        lin(a("Q"), a("sti"), -4097.0, -4097.0)
        hold(a("WF"), a("sti"), A.min)
        ts(a("LU", 0, ()), a("WF", col15), pd(13), A.mult, -0.5625, A.add)
        tt(ind(a(TT, (0, 512)), a("LU", 0, ())), a("Q"), a("CJ"), A.add)

        def twice(c, x=None):
            return (2 * c[0], 2 * c[1]) if x is None else (2 * c[0] + x, 2 * c[1], 2)
        for x in range(2):
            lin(a("ps4", (x, 512, 2)), a("PC"), 4097.0, 4096.0)
        lin(a("ps6", (0, 1)), pf(0), 0.0, 0.0)
        weave(*[[None] * (OPT["skew"] * n) + [
            lambda c=c: tt(a("OT", 0, twice(c)), a(TT, twice(c)), a("ps4", twice(c)), A.subtract),
            lambda n=n: None if n else scan(a("ps6", (1, 257)), a(TT, (0, 512, 2)), a(TT, (1, 512, 2)), A.max, A.max),
            lambda c=c: ts(a("OT", 1, twice(c)), a("OT", 0, twice(c)), 2 ** 24 - 1, AND),
            lambda c=c: tt(a("ps3", c), a("ps6", c), a("PB", c), A.subtract),
            lambda c=c: tt(a("ps5", c), a("ps3", c), a("OT", 1, twice(c, 0)), A.max),
            lambda c=c: tt(a("ci", c), a("ps5", c), a("OT", 1, twice(c, 1)), A.max),
            lambda c=c: ts(a("ca", c), a("ci", c), 4095, AND),
            lambda c=c: cp(a("LL", c), a("ca", c))] for n, c in enumerate(OPT["cols"])])
        x = OPT["split"][t]
        for f, c in [(ac, c) for c in OPT["cols"] if c[0] >= 128] + [(ac, (x, 128))] * (x < 128) + [(cp, (0, x))]:
            f(a("XLD", (16 * c[0], 16 * c[1])), ind(win, a("LL", c)))
        mm(a("ps7", lo), [(a("WH"), last(lo))])
        lin(a("y1"), a("ps7", lo), 1.0 / 128, 1.0 / 256 - 0.5)
        lin(a("W0"), a("ps7", lo), pd(3), 0.0, COPY)
        lin(a("y2"), a("y1"), 1.0, ROUNDER)
        lin(a("y1"), a("y2"), 1.0, -ROUNDER)
        lin(a("HP"), a("y1"), pd(5), 0.0, COPY)
        terms = (("W0", 0), ("HP", 0), ("y3", 1), ("t2", 0))
        run("s", lambda: s.activation(T.sg[:], y0[0], ABS, bias=-8.0, accum_out=lc(0)[0]), (None, a("sg")[1] + lc(0)[1]), (y0,), 280)
        lin(lc(1), lc(0), 1.0, 2048.0)
        lin(lc(2), lc(0), -1.0, 2048.5)
        lin(lc(3), lc(0), 0.5, 1024.0)
        lin(a("y1"), a("IK8"), lc(1), 1.0 / 512 - 0.5)
        lin(a("y2"), a("y1"), 1.0, ROUNDER)
        lin(a("y3"), a("y2"), 1.0, pd(4))
        for b in ("ps1", "ps2"):
            mm(a(b, lo), [(a("IDfn" if n else "IDf"), a(x)) for x, n in terms[:3]], stop=b == "ps1")
        lin(a("sg"), a("ps1", lo), -1.0, lc(2), AF.Sign)
        lin(a("t2"), a("sg"), lc(3), lc(3))
        mm(a("ps2", lo), [(a("IDf"), a("t2"))], start=False)
        for k in range(4):
            ts(a("CC", quarter(k)), a("ps2", (k, 256, 4)), -1.0, A.add)
        mine, laid = 1024 * rank, a("XLD", (0, 4096))
        if t + 1 < ROUNDS:
            for k in range(4):
                mm(a("ps0", quarter(k)), [(a("SEn" if n else "SE"), a(x, (k, 256, 4))) for x, n in terms])
            hold(a("WL"), a("ps0", lo))
            ts(a("LE"), a("WL", col15), pd(12), A.mult, -1.0, A.add)
            cp(a("LO", (64, 192)), ind(laid, a("LE", (4, 12))))
            ac(a("LO", quarter(3)), ind(laid, a("LE", (12, 16))))
            ac(a("LC", quarter(rank)), ind(laid, a("LE", (0, 4))))
            send((1, 2, 3), "e", lambda k: a("LO", quarter(k)), lambda r: a("LC", quarter(r)))
            land("e", lambda k: (1, 2, 3), lambda r: a("LC", quarter(r)), OPT["ahead"])
        for k in sorted((1, 2, 3), key=lambda k: way(core, to(k))) + [0]:
            for f, b in ((cp, 0), (ac, 512)):
                out = a("OB", 3 * t + k - 1, (b, b + 512)) if k else a(nx, (mine + b, mine + b + 512))
                f(out, ind(laid, a("CC", (64 * k + b // 16, 64 * k + b // 16 + 32))))
            if k:
                send((k,), "m%d" % t, lambda k: a("OB", 3 * t + k - 1, ()), lambda r: a(nx, (1024 * r, 1024 * r + 1024)))
        land("m%d" % t, lambda k: (k,), lambda r: a(nx, (1024 * r, 1024 * r + 1024)), OPT["bulk"])
    first, second, near = sorted(((rank - k) % 4 for k in (1, 2, 3)), key=lambda r: way(T.cores[r], core))
    for n, r in enumerate((rank, first, near, second)):
        dma("ys"[n % 2], a("y", (1024 * r, 1024 * r + 1024)), a("X2", (1024 * r, 1024 * r + 1024)), "dy%d" % n, OPT["store"])
    issue_all()
    for sm in sorted(total, key=lambda x: (x[:2] == "dy", x)):
        if know["g"].get(sm, 0) < total[sm]:
            g.wait_ge(T.sem[sm], total[sm])
